import numpy as np, ml_dtypes
CORES = [35,38,43,46]
N = 4
BF = ml_dtypes.bfloat16
def gentries(a):
    return np.ascontiguousarray(a.reshape(8, 16, -1).transpose(0, 2, 1)).reshape(8, -1)
def gtable(e):
    e = np.asarray(e); return np.ascontiguousarray(e.reshape(8, -1, 16).transpose(0, 2, 1)).reshape(128, -1).astype(np.int32)
TP, C, W, S, Q, P, B = 16, 192, 4096, 5, 2, 3, 1024
CB = C // P
def sign(rng, *shape):
    return 1.0 - 2.0 * rng.integers(0, 2, shape)
def draw_lists(rng):
    nt = np.ascontiguousarray(np.argsort(rng.random((N, 8, S, W)), axis=-1)[..., :C])
    return rng.integers(0, W, (N, 8, TP, C)), rng.integers(0, W, (N, 8, Q, C)), nt
def draw_floats(rng):
    w = rng.standard_normal((N, 8, 16, TP, C), dtype=np.float32) * 0.25 * np.exp2(rng.integers(-1, 2, (N, 8, 1, TP, C)).astype(np.float32))
    r = rng.standard_normal((N, 8, 16, W), dtype=np.float32) * np.exp2(rng.integers(-1, 2, (N, 8, 16, 1)).astype(np.float32))
    d = rng.standard_normal((N, 8, 16, S, C), dtype=np.float32) * np.exp2(rng.integers(-1, 2, (N, 8, 16, 1, 1)).astype(np.float32))
    return w, r, d
def wide(rng, v, lo, hi):
    k = v.shape[:2] + (1,) + v.shape[3:]
    return v * np.exp2(rng.integers(lo, hi + 1, k).astype(np.float32)) * (rng.random(k) > 0.0625)
def pack(w, r, d, dl, qu, nt):
    b = lambda v: np.ascontiguousarray(np.clip(np.where(np.abs(v) < 2.0 ** -20, 0, v), -8, 8).reshape(N, 128, -1)).astype(np.float32).astype(BF)
    i = lambda v: np.stack([gtable(a.reshape(8, -1)) for a in v])
    return {"w0": b(w), "r0": b(r), "d0": b(d), "dl": i(dl), "qu": i(qu), "nt": i(nt)}
def kinds(rng):
    return ((np.arange(8) + np.arange(N)[:, None] + rng.integers(0, 4)) & 3).reshape(N, 8, 1, 1)
def plant(v, c, wt, x, des, tap, off):
    w, r, d, dl, qu, nt = v; col = W // 2 + TP * c + np.arange(TP)
    dl[:, :, :, c] = (nt[:, :, 0, c][:, :, None] - col) & (W - 1)
    qu[:, :, 0, c] = (dl[:, :, tap, c] + off) & (W - 1)
    w[..., c] = wt; r[..., col] = x; d[:, :, :, 0, c] = des
def setup_inputs(rng):
    w, r, d = draw_floats(rng); dl, qu, nt = draw_lists(rng)
    return pack(w, r, d, dl, qu, nt)
def setup_inputs_spread(rng):
    w, r, d = draw_floats(rng); dl, qu, nt = draw_lists(rng)
    return pack(wide(rng, w, -2, 2), wide(rng, r, -2, 2), wide(rng, d, -2, 2), dl, qu, nt)
def setup_inputs_ends(rng):
    w, r, d = draw_floats(rng); dr, qr, nt = draw_lists(rng)
    free = rng.random((N, 8, 1, C)) < 0.25; free[..., 0] = False; free[..., C - 1] = False
    dl = np.where(free, dr, rng.integers(0, 2, (N, 8, TP, C)) * (W - 1)); qu = np.where(free, qr, rng.integers(0, 2, (N, 8, Q, C)) * (W - 1))
    pool = np.concatenate([np.arange(C // 2), W - C // 2 + np.arange(C // 2)]); rest = pool[(pool != 1) & (pool != W - 1)]
    nt = pool[np.argsort(rng.random((N, 8, S, C)), axis=-1)]
    nt[:, :, 0, 1:C - 1] = rest[np.argsort(rng.random((N, 8, C - 2)), axis=-1)]; nt[:, :, 0, 0] = 1; nt[:, :, 0, C - 1] = W - 1
    w = np.where(rng.random((N, 8, 1, 1, C)) < 0.3, 8.0 * sign(rng, N, 8, 16, TP, C), w); w[..., C - 1] = 8.0; w[..., 0] = -8.0
    r = np.where(rng.random((N, 8, 1, W)) < 0.3, 8.0 * sign(rng, N, 8, 16, W), r)
    for j in (0, 1, 2, W - 1): r[..., j] = 8.0
    d = np.where(rng.random((N, 8, 1, S, C)) < 0.4, 8.0 * sign(rng, N, 8, 16, S, C), d); d[:, :, :, 0, C - 1] = -8.0; d[:, :, :, 0, 0] = 8.0
    v = (w, r, d, dl, qu, nt)
    u = 7.0 + rng.random((N, 8, 16, TP // 2))
    plant(v, 1, np.concatenate([u, -u], axis=3), 8.0, np.where(rng.random((N, 8, 16)) < 0.25, 0.0, 2.0 * rng.random((N, 8, 16)) - 1.0), 0, 0)
    x = 2.0 ** -6 + 2.0 ** -7 * rng.random((N, 8, 16, TP)); x[..., 4] = 2.0 ** -7; x[..., 2] = 2.0 ** -5; u = sign(rng, N, 8, 16, TP)
    plant(v, 2, 8.0 * u, x * u, 8.0, 2, 0)
    return pack(*v)
def setup_inputs_crowd(rng):
    w, r, d = draw_floats(rng); dl, qu, nt = draw_lists(rng); r = np.clip(r, -2, 2); kind = kinds(rng)
    row = np.arange(16).reshape(1, 1, 16, 1); tap = np.arange(TP).reshape(TP, 1)
    four = np.argsort(rng.random((N, 8, TP, C)), axis=2)[:, :, :4, None]
    turn = (row + rng.integers(0, 16, (N, 8, 1, C))) & 15
    other = np.where(kind == 1, turn == 0, (kind == 2) & (turn < 8))
    lo = np.where(other, four[:, :, 1], four[:, :, 0]); hi = np.where(other, four[:, :, 3], four[:, :, 2])
    w = sign(rng, N, 8, 16, TP, C) * (0.5 + 0.5 * rng.random((N, 8, 16, TP, C)))
    w = np.where(tap == lo[:, :, :, None], 0.0, w); w = np.where(tap == hi[:, :, :, None], 2.0 * sign(rng, N, 8, 16, TP, C), w)
    w = np.where(kind[..., None] == 3, sign(rng, N, 8, 16, 1, C) * (0.5 + 0.5 * rng.random((N, 8, 16, 1, C))), w)
    dl = np.where(kind == 3, dl[:, :, :1], dl)
    v = (w, r, d, dl, qu, nt)
    odd = np.arange(16) == rng.integers(0, 16, (N, 8, 1))
    u = sign(rng, N, 8, 16, TP) * (0.5 + 0.5 * rng.random((N, 8, 16, TP)))
    u[..., 1] = np.where(odd, 0.5, 0.125); u[..., 4] = 0.125; u[..., 2] = np.where(odd, 1.0, 2.0); u[..., 6] = 2.0
    plant(v, 0, u, 0.5 + rng.random((N, 8, 16, 1)), 2.0 * rng.random((N, 8, 16)) - 1.0, 6, -B)
    u = sign(rng, N, 8, 16, TP) * (1.5 + 0.5 * rng.random((N, 8, 16, TP))); x = 2.0 ** -4 * sign(rng, N, 8, 16, TP)
    u[..., 1] = 1.0; u[..., 4] = 1.0; u[..., 2] = 3.0; u[..., 6] = 3.0
    x[..., 1] = 1.5 * 2.0 ** -20; x[..., 4] = 2.0 ** -20; x[..., 2] = 2.0 ** -20; x[..., 6] = 1.5 * 2.0 ** -20
    plant(v, 1, u, x, 8.0, 2, B)
    return pack(*v)
def setup_inputs_corners(rng):
    w, r, d = draw_floats(rng); dl, qu, nt = draw_lists(rng); kind = kinds(rng); half = rng.random((N, 8, 1, C)) < 0.5
    w = np.where(kind[..., None] == 0, 0.0, w); dl = np.where((kind == 0) & half, dl[:, :, :1], dl)
    one = rng.integers(0, W, (N, 8, 1, C)); far = np.where(half, one, (one + W // 2) & (W - 1))
    dl = np.where(kind == 1, one, dl); qu = np.where(kind == 1, far, qu)
    few = rng.choice(np.array([0, 1, W // 2, W - 1]), (N, 8, Q, C)); qu = np.where(kind >= 2, few, qu)
    first = nt[:, :, :1]; nt = np.where(kind == 2, (first + np.arange(S)[:, None]) & (W - 1), np.where(kind == 3, first, nt))
    near = 1 + rng.integers(0, S, (N, 8, TP, C)); own = np.where(rng.random((N, 8, TP, C)) < 0.5, 0, rng.choice(np.array([0, 1, W // 2, W - 1]), (N, 8, TP, C)))
    dl = np.where(kind == 2, near, np.where(kind == 3, own, dl))
    v = (w, r, d, dl, qu, nt)
    u = np.zeros((N, 8, 16, TP)); u[..., 0] = 2.0 ** -16; x = 2.0 + 6.0 * rng.random((N, 8, 16, TP)); x[..., 0] = 2.0 ** -17; x[..., 4] = 1.0
    plant(v, 0, u, x, 0.0, 0, 0)
    u = sign(rng, N, 8, 16, TP) * (3.0 + rng.random((N, 8, 16, TP))); x = 2.0 ** -5 * sign(rng, N, 8, 16, TP)
    u[..., 1] = 1.9921875; u[..., 4] = 1.9921875; u[..., 2] = 6.0; x[..., 1] = 3.0 * 2.0 ** -18; x[..., 4] = 2.0 ** -17
    plant(v, 1, u, x, 8.0, 2, 0)
    return pack(*v)
def setup_inputs_edge(rng):
    w, r, d = draw_floats(rng); dl, qu, nt = draw_lists(rng); r = np.clip(r, -2, 2); w = np.clip(w, -0.5, 0.5)
    tap = np.arange(TP).reshape(TP, 1); k = rng.integers(0, TP, (N, 8, 1, C)); base = rng.integers(0, W, (N, 8, 1, C))
    w = np.where(tap == k[:, :, None], 1.5 * sign(rng, N, 8, 16, 1, C), w)
    away = np.array([B - 1, B, B + 1, 1 - B, -B, -B - 1, 0, W // 2])
    dl = np.where(tap == k, base, (base + rng.choice(away, (N, 8, TP, C))) & (W - 1)); qu = (base + rng.choice(away, (N, 8, Q, C))) & (W - 1)
    v = (w, r, d, dl, qu, nt)
    side = sign(rng, N, 8, 16); way = side * sign(rng, N, 8, 16)
    u = np.zeros((N, 8, 16, TP)); x = 1.0 + rng.random((N, 8, 16, TP))
    u[..., 0] = 7.5 * side; u[..., 1] = 1.5 * 2.0 ** -10 * way; u[..., 2] = -7.5 * side; u[..., 3] = -(2.0 ** -10) * way
    x[..., 0] = 8.0; x[..., 1] = 2.0 ** -10; x[..., 2] = 8.0; x[..., 3] = 2.0 ** -10
    plant(v, 0, u, x, 2.0 * side, 0, 0)
    return pack(*v)
def check_inputs(d):
    bad = []
    for k in ("dl", "qu", "nt"):
        if np.min(d[k]) < 0 or np.max(d[k]) > W - 1: bad.append("range of " + k)
    for k in ("w0", "r0", "d0"):
        m = np.abs(np.asarray(d[k]).astype(np.float32))
        if not np.all((m <= 8) & ((m == 0) | (m >= 2.0 ** -20))): bad.append("size of " + k)
    n = np.sort(np.stack([gentries(a) for a in d["nt"]]).reshape(N, 8, S, C), axis=-1)
    if np.any(n[..., 1:] == n[..., :-1]): bad.append("times of a step differ")
    return bad
def reference(w0, r0, d0, dl, qu, nt):
    w = w0.astype(np.float32).reshape(N, 8, 16, TP, C); r = r0.astype(np.float32).reshape(N, 8, 16, W); d = d0.astype(np.float32).reshape(N, 8, 16, S, C)
    a = np.stack([gentries(v) for v in dl]).astype(np.int64).reshape(N, 8, TP, C)
    q = np.stack([gentries(v) for v in qu]).astype(np.int64).reshape(N, 8, Q, C)
    n = np.stack([gentries(v) for v in nt]).astype(np.int64).reshape(N, 8, S, C)
    tap = np.arange(TP).reshape(TP, 1)
    for s in range(S):
        t = n[:, :, s]
        ix = (t[:, :, None] - a) & (W - 1)
        x = np.take_along_axis(r, ix.reshape(N, 8, 1, TP * C), 3).reshape(N, 8, 16, TP, C)
        p = w * x; y = p[:, :, :, 0]
        for k in range(1, TP): y = y + p[:, :, :, k]
        e = np.minimum(np.maximum(d[:, :, :, s] - y, np.float32(-2)), np.float32(2))
        w = w + np.float32(0.015625) * (e[:, :, :, None] * x)
        m = np.abs(w)
        least = np.add.reduce((m == np.min(m, axis=3, keepdims=True)).astype(np.int64), axis=2)
        most = np.add.reduce((m == np.max(m, axis=3, keepdims=True)).astype(np.int64), axis=2)
        weak = np.argmax(least, axis=2)[:, :, None]; strong = np.argmax(most, axis=2)[:, :, None]
        head = q[:, :, s % Q][:, :, None].copy()
        gap = (head - np.take_along_axis(a, strong, 2)) & (W - 1)
        ok = np.minimum(gap, W - gap) <= B
        q[:, :, s % Q] = np.where(ok, np.take_along_axis(a, weak, 2), head)[:, :, 0]
        hit = ok & (tap == weak)
        a = np.where(hit, head, a); w = np.where(hit[:, :, None], np.float32(0.25), w)
        come = np.concatenate([np.roll(np.roll(e[..., b * CB:(b + 1) * CB], 1 + b, axis=0), 1 + s, axis=1) for b in range(P)], axis=3)
        np.put_along_axis(r, t[:, :, None], come, 3)
    q = np.roll(q, -(S % Q), axis=2)
    return {"yw": np.ascontiguousarray(w.reshape(N, 128, TP * C)), "yr": np.ascontiguousarray(come.reshape(N, 128, C)),
            "yd": np.stack([gtable(v.reshape(8, -1)) for v in a]).astype(np.float32), "yq": np.stack([gtable(v.reshape(8, -1)) for v in q]).astype(np.float32)}

@@ -1,0 +1,587 @@
+from concourse.mybir import AluOpType as A, ActivationFunctionType as F
+
+TP, C, WN, S, NB, CB = 16, 192, 4096, 5, 3, 64
+BW = TP * CB
+BIG = float(2 ** 40)
+DP, DT, DE = 1, 1, 1
+NS = 10 if DP == 1 else 12
+PEB = ()
+f32, bf, i32, u16 = "float32", "bfloat16", "int32", "uint16"
+
+
+def sb(n, t):
+    return ("sbuf", [128, n], t)
+
+
+SCRATCH = {
+    "wp": ("psum", [128, 3072], f32), "px": ("psum", [128, 512], f32), "py": ("psum", [128, 512], f32),
+    "wb": sb(3072, bf), "rb": sb(WN, bf), "db": sb(960, bf), "dli": sb(192, i32), "nq": sb(88, i32),
+    "rr": sb(WN, f32), "ws": sb(6144, f32), "wk": sb(17 * C, f32), "xs": sb(3072, f32), "ts": sb(3072, f32),
+    "pe": sb(NS * C, f32), "po": sb(NS * C, f32), "so": sb(NS * C, f32), "dup": sb(4 * CB, f32),
+    "mx": sb(BW, f32), "mn": sb(BW, f32), "m01": sb(BW, bf), "mbg": sb(BW, bf),
+    "eqs": sb(3072, bf), "eqw": sb(3072, bf),
+    "es": sb(S * C, f32), "land": sb(S * C, f32), "rot": sb(C, f32),
+    "ip": sb(4, i32), "it": sb(8, i32), "col": sb(16, f32), "fj": sb(144, f32), "gb": sb(128, f32), "fn": sb(24, f32),
+    "m16": sb(16, f32), "dm": sb(C, f32),
+    "s0": sb(144, bf), "s1": sb(144, bf), "w0s": sb(144, bf), "w1s": sb(144, bf),
+    "idf": sb(128, f32), "nid": sb(128, f32), "n64": sb(128, f32), "bof": sb(128, f32), "nbo": sb(128, f32),
+    "bob": sb(128, bf), "boc": sb(128, bf), "idb": sb(128, bf), "cn": sb(4, bf),
+    "pqt": sb(CB, f32),
+    "l1": sb(24, u16), "l2": sb(12, u16), "l3": sb(24, u16), "l4": sb(12, u16), "cj": sb(12, f32), "kj": sb(12, i32),
+    "tj": sb(12, f32), "ntu": sb(60, u16), "ex": sb(1344, f32), "tin": sb(384, f32), "tout": sb(384, f32),
+    "aa": sb(2 * C, f32), "qq": sb(2 * C, f32), "ab1": sb(C, f32), "ab2": sb(C, f32), "sgn": sb(C, bf),
+    "us": sb(CB, bf), "us2": sb(CB, bf), "uw": sb(CB, bf), "sz": sb(CB, f32), "thr": sb(CB, f32), "hit": sb(CB, bf),
+    "vi": sb(C, i32), "vm": sb(C, i32), "idx": sb(C, u16), "sl": sb(12, u16),
+    "k0s": sb(144, bf), "k1s": sb(144, bf), "ck": sb(12, bf),
+    "ydo": sb(C, f32), "qm": sb(2 * C, f32), "qs": sb(2 * C, f32), "yqo": sb(24, f32),
+}
+SEMAPHORES = (["cv", "ca", "cp", "cg", "snt"] + ["arr%d" % s for s in range(S)] + ["dm%d" % i for i in range(24)])
+
+
+def rank_program(g, core, T, topo):
+    rank = T.rank_of(core)
+    if rank is None:
+        return
+    N = len(T.cores)
+    V, ACT, PE, SY = g.vector, g.scalar, g.tensor, g.sync
+    Q = {"v": V, "a": ACT, "p": PE, "g": g, "s": SY}
+    cnt = {"v": 0, "a": 0, "p": 0, "g": 0}
+    seen = {e: {} for e in Q}
+    wrote, read, bank = {}, {}, {}
+    ndma = [0]
+
+    def wait(e, tok):
+        if seen[e].get(tok[0], 0) < tok[1]:
+            Q[e].wait_ge(T.sem[tok[0]], tok[1])
+            seen[e][tok[0]] = tok[1]
+
+    def op(e, call, R=(), W=(), B=(), dma=False):
+        need = {}
+
+        def add(tok, raw):
+            if tok[2] == e and not tok[3] and not dma and (e == "p" or not raw):
+                return
+            need[tok[0]] = max(need.get(tok[0], 0), tok[1])
+        for k in R:
+            if k in wrote:
+                add(wrote[k], True)
+        for k in W:
+            if k in wrote:
+                add(wrote[k], True)
+            for t in read.get(k, {}).values():
+                add(t, False)
+        for b in B:
+            if b in bank:
+                add(bank[b], False)
+        for s_, n_ in need.items():
+            wait(e, (s_, n_))
+        ins = call()
+        if dma:
+            name = "dm%d" % ndma[0]
+            ndma[0] += 1
+            ins.then_inc(T.sem[name], 16)
+            tok = (name, 16, e, True)
+        else:
+            cnt[e] += 1
+            ins.then_inc(T.sem["c" + e], 1)
+            tok = ("c" + e, cnt[e], e, False)
+        for k in R:
+            read.setdefault(k, {})[tok[0]] = tok
+        for k in W:
+            wrote[k] = tok
+            read[k] = {}
+        for b in B:
+            bank[b] = tok
+        return tok
+
+    def tt(o, a, b, f, R, W, B=()):
+        return lambda: op("v", lambda: V.tensor_tensor(o, a, b, f), R, W, B)
+
+    def ts(o, a, s1, f1, R, W, B=(), s2=None, f2=None):
+        if f2 is None:
+            return lambda: op("v", lambda: V.tensor_scalar(o, a, s1, None, f1), R, W, B)
+        return lambda: op("v", lambda: V.tensor_scalar(o, a, s1, s2, f1, f2), R, W, B)
+
+    def cp(o, a, R, W, B=()):
+        return lambda: op("v", lambda: V.tensor_copy(o, a), R, W, B)
+
+    def ms(o, c, W):
+        op("v", lambda: V.memset(o, c), (), W)
+
+    def act(o, a, f, R, W, B=(), bias=0.0, scale=1.0):
+        op("a", lambda: ACT.activation(o, a, f, bias=bias, scale=scale), R, W, B)
+
+    def mm(o, l, r, st, sp, R, W, B):
+        op("p", lambda: PE.matmul(o, l, r, st, sp), R, W, B)
+
+    def col(i):
+        return T.col[:, i:i + 1]
+
+    def wbank(b):
+        return (2 * b, 2 * b + 1)
+
+    def blk(t, b, k=None):
+        return t[:, b * BW:(b + 1) * BW] if k is None else t[:, b * BW + k:(b + 1) * BW:TP]
+
+    def taps(t, b, k, n):
+        return t[:, b * BW + k:(b + 1) * BW:n]
+
+    def spread(calls):
+        return [f for c_ in calls for f in [c_] + [lambda: None] * (TP // len(calls) - 1)]
+
+    def cs(t, b, off=0):
+        return t[:, off + b * CB:off + (b + 1) * CB]
+
+    X, Y = 6, 7
+    yD, yN, yZ, yH = T.py[:, 0:192], T.py[:, 192:384], T.py[:, 384:448], T.py[:, 448:512]
+    xV, xZ = T.px[:, 384:448], T.px[:, 448:512]
+
+    op("s", lambda: SY.dma_start(T.rb[:], T.r0[:]), (), ["rb"], dma=True)
+    op("a", lambda: ACT.dma_start(T.nq[:, 0:60], T.nt[:]), (), ["nt"], dma=True)
+    op("a", lambda: ACT.dma_start(T.dli[:], T.dl[:]), (), ["dli"], dma=True)
+    op("a", lambda: ACT.dma_start(T.nq[:, 60:84], T.qu[:]), (), ["qu"], dma=True)
+    op("s", lambda: SY.dma_start(T.wb[:, 0:1536], T.w0[:, 0:1536]), (), ["wb0"], dma=True)
+    op("a", lambda: ACT.dma_start(T.db[:, 0:C], T.d0[:, 0:C]), (), ["db0"], dma=True)
+    op("s", lambda: SY.dma_start(T.wb[:, 1536:3072], T.w0[:, 1536:3072]), (), ["wb1"], dma=True)
+    op("s", lambda: SY.dma_start(T.db[:, C:960], T.d0[:, C:960]), (), ["db1"], dma=True)
+
+    def io(o, pat, cm, W, small=True):
+        if small:
+            op("g", lambda: g.iota(o, pat, 0, cm, allow_small_or_imprecise_dtypes=True), (), W)
+        else:
+            op("g", lambda: g.iota(o, pat, 0, cm), (), W)
+    io(T.ip[:, 0:1], [[0, 1]], 1, ["ip"], False)
+    io(T.fj[:], [[1, 144]], 0, ["fj"])
+    io(T.gb[:], [[16, 8], [0, 16]], 0, ["gb"])
+    io(T.fn[:], [[1, 12], [0, 2]], 0, ["fn"])
+    io(T.dm[:], [[0, 12], [1, 16]], 0, ["dmr"])
+    op("g", lambda: g.dma_start(T.rr[:], T.r0[:]), ["wb1"], ["rr"], dma=True)
+
+    P_, PM, PG, G15, G16, P31, M12, M16, H16, BS, BWK, WSL, WK = range(13)
+    ts(T.it[:, 0:1], T.ip[:, 0:1], 15, A.bitwise_and, ["ip"], ["it0"])()
+    ts(T.it[:, 1:2], T.ip[:, 0:1], 31, A.bitwise_and, ["ip"], ["it1"])()
+    ts(T.it[:, 2:3], T.ip[:, 0:1], 112, A.bitwise_and, ["ip"], ["it2"])()
+    cp(col(P_), T.ip[:, 0:1], ["ip"], ["cP"])()
+    cp(col(PM), T.it[:, 0:1], ["it0"], ["cPM"])()
+    cp(col(PG), T.it[:, 2:3], ["it2"], ["cPG"])()
+    cp(col(P31), T.it[:, 1:2], ["it1"], ["cP31"])()
+    ts(col(M12), T.it[:, 0:1], 12.0, A.mult, ["it0"], ["cM12"])()
+    ts(T.m16[:], T.fj[:, 0:16], col(PM), A.is_equal, ["fj", "cPM"], ["m16"])()
+    ts(T.bof[:], T.gb[:], col(PG), A.is_equal, ["gb", "cPG"], ["bof"])()
+    ts(T.l1[:], T.fn[:], col(M12), A.add, ["fn", "cM12"], ["l1"])()
+    ts(T.l2[:], T.fj[:, 0:12], 32.0, A.mult, ["fj", "cP31"], ["l2"], s2=col(P31), f2=A.add)()
+    ms(T.pe[:, 0:NS * C:NS], BIG, ["pc0"])
+    ms(T.po[:, 0:NS * C:NS], -BIG, ["pc1"])
+    for t_, j in ((T.pe, 5), (T.pe, 6), (T.po, 5), (T.po, 6)) if DP == 2 else ():
+        ms(t_[:, j:NS * C:NS], 0.0, [])
+    ms(T.po[:, NS - 1:NS * C:NS], 0.0, ["pc2"])
+    ms(T.m01[:], 1.0, ["m01"])
+    for r in range(16):
+        ts(T.ex[:, r:1344:16], T.nq[:, 0:84], T.m16[:, r:r + 1], A.mult, ["nt", "qu", "m16"], ["ex%d" % r])()
+    EX = ["ex%d" % r for r in range(16)]
+    mm(yN, T.bof[:], T.ex[:, 0:192], True, True, EX + ["bof"], ["yN"], [Y])
+    mm(T.px[:, 0:384], T.bof[:], T.ex[:, 960:1344], True, True, EX + ["bof"], ["xq"], [X])
+    cp(T.tin[:], T.dli[:, 0:192].indirect(T.l1[:, 0:24]), ["dli", "l1"], ["tin"])()
+    ts(T.idf[:], T.fj[:, 0:128], col(P_), A.is_equal, ["fj", "cP"], ["idf"])()
+    op("v", lambda: V.transpose(T.tout[:], T.tin[:]), ["tin"], ["tout"])
+    ts(col(G15), col(PG), 15.0, A.add, ["cPG"], ["cG15"])()
+    cp(T.aa[:, 0:192], T.tout[:, 0:384].indirect(T.l2[:, 0:12]), ["tout", "l2"], ["a0_0", "a0_1", "a0_2"])()
+    ts(col(G16), col(PG), 16.0, A.add, ["cPG"], ["cG16"])()
+    tt(T.vi[:], yN, T.aa[:, 0:192], A.subtract, ["yN", "a0_0", "a0_1", "a0_2"], ["vi0", "vi1", "vi2"], [Y])()
+    ts(T.nid[:], T.idf[:], -1.0, A.mult, ["idf"], ["nid"])()
+    ts(T.vm[:], T.vi[:], WN - 1, A.bitwise_and, ["vi0", "vi1", "vi2"], ["vm0", "vm1", "vm2"])()
+    ts(T.n64[:], T.idf[:], 1.0 / 64, A.mult, ["idf"], ["n64"])()
+    cp(T.idx[:], T.vm[:], ["vm0", "vm1", "vm2"], ["idx0", "idx1", "idx2"])()
+    act(T.qq[:], T.px[:, 0:384], F.Copy, ["xq"], ["q0", "q1"], [X])
+    ms(T.mbg[:], 0.0, ["mbg"])
+    ms(T.m01[:, 0:BW:16], 0.0, ["m01"])
+    ms(T.mbg[:, 0:BW:16], 1e20, ["mbg"])
+    ms(T.pqt[:], 0.25, ["pqt"])
+    ts(col(BS), col(PM), -0.71, A.mult, ["cPM"], ["cBS"], s2=-94.0, f2=A.add)()
+    ts(col(BWK), col(PM), -0.55, A.mult, ["cPM"], ["cBW"], s2=-78.8, f2=A.add)()
+    ts(col(WSL), col(PM), -256.0, A.add, ["cPM"], ["cWS"])()
+    ts(col(M16), col(PM), 16.0, A.mult, ["cPM"], ["cM16"])()
+    ts(T.s0[:], T.fj[:], col(G15), A.is_equal, ["fj", "cG15"], ["s0"])()
+    ts(T.s1[:], T.fj[:], col(G16), A.is_equal, ["fj", "cG16"], ["s1"])()
+    ts(T.w0s[:], T.fj[:], col(G15), A.is_equal, ["fj", "cG15", "cWS"], ["w0s"], s2=col(WSL), f2=A.mult)()
+    ts(T.w1s[:], T.fj[:], col(G16), A.is_equal, ["fj", "cG16", "cWS"], ["w1s"], s2=col(WSL), f2=A.mult)()
+    ts(T.nbo[:], T.bof[:], -1.0, A.mult, ["bof"], ["nbo"])()
+    ts(T.idb[:], T.idf[:], -2.5, A.mult, ["idf"], ["idb"])()
+    cp(T.bob[:], T.bof[:], ["bof"], ["bob"])()
+    ts(T.cn[:], T.fj[:, 0:4], 512.0, A.mult, ["fj"], ["cn"], s2=256.0, f2=A.add)()
+    tt(T.boc[:], T.idb[:], T.bof[:], A.add, ["idb", "bof"], ["boc"])()
+    cp(T.ntu[:], T.nq[:, 0:60], ["nt"], ["ntu"])()
+    cp(T.idb[:], T.idf[:], ["idf", "boc"], ["idb"])()
+
+    def late_consts():
+        return [
+            ts(T.cj[:], T.fj[:, 0:12], 16.0, A.mult, ["fj", "cPM"], ["cj"], s2=col(PM), f2=A.add),
+            ts(T.l3[:], T.fn[:], 16.0, A.mult, ["fn", "cPM"], ["l3"], s2=col(PM), f2=A.add),
+            tt(col(H16), col(P31), col(PM), A.subtract, ["cP31", "cPM"], ["cH"]),
+            ts(T.tj[:], T.cj[:], -5.5, A.add, ["cj"], ["tj"], s2=1.0 / 12, f2=A.mult),
+            ts(T.dm[:], T.dm[:], col(PM), A.is_equal, ["dmr", "cPM"], ["dmr"]),
+            cp(T.kj[:], T.tj[:], ["tj"], ["kj"]),
+            ts(col(WK), col(PM), float(C), A.mult, ["cPM"], ["cWK"], s2=-16.0 * C, f2=A.add),
+            ts(T.ck[:], T.fj[:, 0:12], 16.0, A.mult, ["fj"], ["ck"], s2=16.0 * C, f2=A.add),
+            ts(T.k0s[:], T.s0[:], col(WK), A.mult, ["s0", "cWK"], ["k0s"]),
+            ts(T.k1s[:], T.s1[:], col(WK), A.mult, ["s1", "cWK"], ["k1s"]),
+            ts(T.tj[:], T.kj[:], -383.0 / 32, A.mult, ["kj"], ["tj"]),
+            tt(T.tj[:], T.tj[:], T.cj[:], A.add, ["tj", "cj"], ["tj"]),
+            ts(T.l4[:], T.tj[:], 32.0, A.mult, ["tj", "cH"], ["l4"], s2=col(H16), f2=A.add),
+        ]
+
+    def sel(k, even, odd):
+        return even[:, 16 - k:144 - k] if k % 2 == 0 else odd[:, 15 - k:143 - k]
+
+    def gather(s, b):
+        win, key = (T.rb, "rb") if s == 0 else (T.rr, "rr")
+        act(blk(T.xs, b), win[:, 0:WN].indirect(cs(T.idx, b)), F.Copy, [key, "idx%d" % b], ["x%d" % b])
+
+    def dslot(s):
+        act(T.pe[:, NS - 1:NS * C:NS], T.db[:, s * C:(s + 1) * C], F.Copy, ["db%d" % min(s, 1)], ["pd0", "pd1", "pd2"])
+
+    def copy_in(s, b, on_v=False):
+        if s == 0:
+            for k in (range(TP) if on_v is False else on_v):
+                src, key = cs(T.wb, b, k * C), ["wb%d" % (k // 8)]
+                if on_v:
+                    ts(blk(T.wp, b, k), src, -1.0, A.mult, key, ["wp%d" % b] if k % 8 in (0, 7) else [], wbank(b))()
+                else:
+                    act(blk(T.wp, b, k), src, F.Copy, key, ["wp%d" % b] if k in (0, TP - 1) else [], wbank(b), scale=-1.0)
+            return
+        for n in range(4):
+            o = 256 * (4 * b + n)
+            act(T.wp[:, o:o + 256], T.ws[:, 2 * o:2 * o + 256], F.Copy, ["ws%d" % b],
+                ["wp%d" % b] if n in (0, 3) else [], wbank(b), scale=-1.0)
+
+    def by_pe(s, b):
+        return s > 0 and b in PEB
+
+    def in_psum(s, b):
+        return s in (0, S - 1) or by_pe(s, b)
+
+    def copy_out(s, b):
+        if s == S - 1:
+            for k in range(TP):
+                act(cs(T.wk, b, k * C), blk(T.wp, b, k), F.Copy, ["wp%d" % b], ["wk%d" % b] if k in (0, TP - 1) else [],
+                    wbank(b))
+        elif in_psum(s, b):
+            for n in range(4):
+                o = 256 * (4 * b + n)
+                act(T.ws[:, 2 * o:2 * o + 256], T.wp[:, o:o + 256], F.Copy, ["wp%d" % b],
+                    ["ws%d" % b] if n in (0, 3) else [], wbank(b))
+
+    def size(s, b):
+        if in_psum(s, b):
+            act(blk(T.wp, b), blk(T.wp, b), F.Abs, ["wp%d" % b, "ws%d" % b, "wk%d" % b], ["wp%d" % b], wbank(b))
+            return
+        for n in range(4):
+            o = 256 * (4 * b + n)
+            act(T.wp[:, o:o + 256], T.ws[:, 2 * o:2 * o + 256], F.Abs, ["ws%d" % b], ["wp%d" % b] if n in (0, 3) else [], wbank(b))
+
+    def prod(b):
+        c0, c1 = NS * b * CB, NS * (b + 1) * CB
+        n = TP // DP
+        return spread([tt((T.pe, T.po)[k % 2][:, c0 + 1 + k // 2:c1:NS // DP], taps(T.wp, b, k, n), taps(T.xs, b, k, n), A.mult,
+                          ["wp%d" % b, "x%d" % b], ["p%d" % b] if k in (0, n - 1) else [], wbank(b)) for k in range(n)])
+
+    def scan_y(b):
+        c0, c1 = NS * b * CB, NS * (b + 1) * CB
+        return lambda: op("v", lambda: V.tensor_tensor_scan(T.so[:, c0:c1], T.pe[:, c0:c1], T.po[:, c0:c1], 0.0,
+                                                           A.add, A.add),
+                          ["p%d" % b, "pd%d" % b, "pc0", "pc1", "pc2"], ["so%d" % b])
+
+    def resid(b):
+        return T.so[:, NS * b * CB + NS - 1:NS * (b + 1) * CB:NS]
+
+    def clip_x(b):
+        def run():
+            for i in range(DT):
+                ts(T.px[:, i:DT * CB:DT], resid(b), -2.0, A.max, ["so%d" % b], ["e", "xq"] if i == DT - 1 else [], [X],
+                   s2=2.0, f2=A.min)()
+        return run
+
+    def clip_send(s, b):
+        def run():
+            ts(cs(T.es, b, s * C), resid(b), -2.0, A.max, ["so%d" % b], ["es"], s2=2.0, f2=A.min)()
+            dst = T.cores[(rank + 1 + b) % N]
+            eng = topo.engines(core, dst)[-8:]
+            rid, pid, _ = topo.addr(dst)
+            tok = wrote["es"]
+            wait("g", tok)
+            g.remote_dma(cs(T.land, b, s * C), cs(T.es, b, s * C), T.sem["arr%d" % s], T.sem.snt, pid, rid,
+                         sum(1 << e for e in eng))
+            del wrote["es"]
+        return run
+
+    def tmul(s, b):
+        n = TP // DT
+        dst, key, bk = (T.ts, "t%d" % b, [X]) if by_pe(s, b) else (T.wp, "wp%d" % b, [X, 2 * b, 2 * b + 1])
+        return spread([tt(taps(dst, b, k, n), taps(T.xs, b, k, n), T.px[:, 0:DT * CB], A.mult, ["x%d" % b, "e"],
+                          [key] if k in (0, n - 1) else [], bk) for k in range(n)])
+
+    def preload(s, b):
+        if by_pe(s, b):
+            for n in range(4):
+                o = 256 * (4 * b + n)
+                mm(T.wp[:, o:o + 256], T.idf[:], T.ws[:, 2 * o:2 * o + 256], n % 2 == 0, False, ["ws%d" % b, "idf"],
+                   ["wp%d" % b], wbank(b))
+
+    def update(s, b):
+        if by_pe(s, b):
+            for j in wbank(b):
+                mm(T.wp[:, 512 * j:512 * (j + 1)], T.n64[:], T.ts[:, 512 * j:512 * (j + 1)], False, True,
+                   ["t%d" % b, "n64"], ["wp%d" % b], wbank(b))
+        else:
+            act(blk(T.wp, b), blk(T.wp, b), F.Copy, ["wp%d" % b], ["wp%d" % b], wbank(b), scale=1.0 / 64)
+
+    def summ(s, b):
+        if by_pe(s, b):
+            return [lambda: None] * 4
+        if s == 0:
+            calls = [tt(blk(T.wp, b, k), cs(T.wb, b, k * C), blk(T.wp, b, k), A.add, ["wp%d" % b] if k == 0 else [],
+                        ["wa%d" % b] if k == TP - 1 else [], wbank(b)) for k in range(TP)]
+            return [lambda j=j: [f() for f in calls[4 * j:4 * j + 4]] for j in range(4)]
+        out = []
+        for n in range(4):
+            o = 256 * (4 * b + n)
+            p_, w_ = T.wp[:, o:o + 256], T.ws[:, 2 * o:2 * o + 256]
+            out.append(tt(p_ if s == S - 1 else w_, w_, p_, A.add, ["wp%d" % b, "ws%d" % b] if n == 0 else [],
+                          ["wa%d" % b] if n == 3 else [], wbank(b)))
+        return out
+
+    def scans(b):
+        out = []
+        for nm, msk, o, f0, f1 in (("mx", T.m01, T.mx, A.mult, A.max), ("mn", T.mbg, T.mn, A.max, A.min)):
+            for h in range(2):
+                def run(nm=nm, msk=msk, o=o, f0=f0, f1=f1, h=h):
+                    c0 = 512 * h
+                    op("v", lambda: V.tensor_tensor_scan(o[:, c0:c0 + 512], msk[:, c0:c0 + 512],
+                                                         T.wp[:, b * BW + c0:b * BW + c0 + 512], 0.0, f0, f1),
+                       ["wp%d" % b, "m01", "mbg"], [nm + str(h)], wbank(b))
+                out.append(run)
+        return out
+
+    def votes(b, strong):
+        nm, ext, eq, o, bk = ("mx", T.mx, T.eqs, xV, X) if strong else ("mn", T.mn, T.eqw, yZ, Y)
+        out = []
+        n, w = TP // DE, DE * CB
+        per = max(1, 4 // DE)
+        for k in range(n):
+            def run(k=k):
+                key = "eq%s%d_%d" % (nm, b, k)
+                src, skey = ext[:, TP - 1:BW:TP], [nm + "0", nm + "1"]
+                if DE > 1:
+                    for i in range(DE if k == 0 else 0):
+                        cp(T.dup[:, i:w:DE], src, skey, ["dup"] if i == DE - 1 else [])()
+                    src, skey = T.dup[:, 0:w], ["dup"]
+                tt(eq[:, b * BW + k * w:b * BW + (k + 1) * w], taps(T.wp, b, k, n), src, A.is_equal, ["wp%d" % b] + skey, [key],
+                   wbank(b))()
+                if k % per == per - 1:
+                    for j in range(k - per + 1, k + 1):
+                        for i in range(DE):
+                            mm(o, sel(j + n * i, T.s1, T.s0), eq[:, b * BW + j * w + i:b * BW + (j + 1) * w:DE],
+                               j == 0 and i == 0, j == n - 1 and i == DE - 1, [key, "s0", "s1"], ["xV" if strong else "yZ"], [bk])
+                if k == n - 1 and strong:
+                    act(T.us[:], xV, F.Exp, ["xV", "cBS"], ["us"], [X], bias=col(BS), scale=11.36)
+                if k == n - 1 and not strong:
+                    act(T.uw[:], yZ, F.Exp, ["yZ", "cBW"], ["uw"], [Y], bias=col(BWK), scale=8.8)
+                    mm(yZ, T.boc[:], T.uw[:], True, True, ["uw", "boc"], ["yZ"], [Y])
+            out.append(run)
+        return spread(out)
+
+    def strong_side(b):
+        def run():
+            tt(T.us2[:], T.us[:], cs(T.sgn, b), A.mult, ["us", "sgn"], ["us2"])()
+            mm(xZ, T.bob[:], T.us2[:], True, True, ["us2", "bob"], ["xZ"], [X])
+            act(T.sz[:], xZ, F.Sign, ["xZ"], ["sz"], [X])
+            act(T.thr[:], T.sz[:], F.Identity, ["sz"], ["thr"], bias=-5e28, scale=5e28)
+        return run
+
+    def chain(s, b):
+        old, new = "a%d_%d" % (s % 2, b), "a%d_%d" % ((s + 1) % 2, b)
+        ao, an = cs(T.aa, b, (s % 2) * C), cs(T.aa, b, ((s + 1) % 2) * C)
+        last = s == S - 1
+        yS = T.py[:, 384:388]
+        slb = T.sl[:, 4 * b:4 * b + 4]
+
+        def slots():
+            even, odd, base = (T.k1s, T.k0s, T.ck[:, 4 * b:4 * b + 4]) if last else (T.w1s, T.w0s, T.cn[:])
+            mm(yS, T.idb[:], base, True, False, ["idb", "cn", "ck"], ["yZ"], [Y])
+            for r in range(16):
+                mm(yS, sel(r, even, odd), T.hit[:, r:CB:16], False, r == 15, ["hit", "w0s", "w1s", "k0s", "k1s"], ["yZ"], [Y])
+        hit = tt(T.hit[:], yZ, T.thr[:], A.is_lt, ["yZ", "thr"], ["hit"], [Y])
+        hd = tt(yH, T.hit[:], cs(T.py, b), A.mult, ["hit", "yD"], ["yH"], [Y])
+        anew = tt(an, yH, ao, A.add, ["yH", old], [new], [Y])
+        if last:
+            def first():
+                hit()
+                slots()
+            return [first, ts(slb, yS, col(PM), A.add, ["yZ", "cPM"], ["sl%d" % b], [Y]), hd,
+                    cp(T.wk[:, 0:17 * C].indirect(slb), T.pqt[:], ["sl%d" % b, "pqt"], ["wk0", "wk1", "wk2"]), anew]
+
+        def vsub():
+            tt(cs(T.vi, b), cs(T.py, b, 192), an, A.subtract, ["yN", new], ["vi%d" % b], [Y])()
+            slots()
+        return [hit, hd, anew, vsub,
+                ts(cs(T.vm, b), cs(T.vi, b), WN - 1, A.bitwise_and, ["vi%d" % b], ["vm%d" % b]),
+                cp(cs(T.idx, b), cs(T.vm, b), ["vm%d" % b], ["idx%d" % b]),
+                ts(slb, yS, col(M16), A.add, ["yZ", "cM16"], ["sl%d" % b], [Y]),
+                cp(T.ws[:, 2048 * b:2048 * (b + 1)].indirect(slb), T.pqt[:], ["sl%d" % b, "pqt"], ["ws%d" % b])]
+
+    def akeys(i):
+        return ["a%d_%d" % (i, b) for b in range(NB)]
+
+    def queue_step(s):
+        j = s % 2
+        mm(yN, T.idf[:], T.qq[:, j * C:(j + 1) * C], True, False, ["q%d" % j, "idf"], ["yN"], [Y])
+        mm(yN, T.bof[:], T.aa[:, j * C:(j + 1) * C], False, False, akeys(j) + ["bof"], ["yN"], [Y])
+        mm(yN, T.nbo[:], T.aa[:, (1 - j) * C:(2 - j) * C], False, True, akeys(1 - j) + ["nbo"], ["yN"], [Y])
+
+    def books_pe(s):
+        j = s % 2
+        mm(yD, T.idf[:], T.qq[:, j * C:(j + 1) * C], True, False, ["q%d" % j, "idf"], ["yD"], [Y])
+        mm(yD, T.nid[:], T.aa[:, j * C:(j + 1) * C], False, True, akeys(j) + ["nid"], ["yD"], [Y])
+        if s > 0:
+            queue_step(s - 1)
+
+    def books_act(s):
+        act(T.ab1[:], yD, F.Abs, ["yD"], ["ab1"], [Y])
+        if s > 0:
+            j = (s - 1) % 2
+            act(T.qq[:, j * C:(j + 1) * C], yN, F.Copy, ["yN"], ["q%d" % j], [Y])
+        act(T.ab2[:], T.ab1[:], F.Abs, ["ab1"], ["ab2"], bias=-2048.0)
+        act(T.sgn[:], T.ab2[:], F.Sign, ["ab2"], ["sgn"], bias=-1023.5)
+
+    def times(s):
+        mm(yN, T.bof[:], T.ex[:, s * C:(s + 1) * C], True, True, EX + ["bof"], ["yN"], [Y])
+
+    def turn(s):
+        sh = 16 * (1 + s)
+        last = s == S - 1
+        dst = T.yr if last else T.rot
+        src = T.land[:, s * C:(s + 1) * C]
+        SY.wait_ge(T.sem["arr%d" % s], 8 * NB)
+        op("s", lambda: SY.dma_start(dst[sh:128, :], src[0:128 - sh, :]), (), ["rot0"], dma=True)
+        op("s", lambda: SY.dma_start(dst[0:sh, :], src[128 - sh:128, :]), (), ["rot1"], dma=True)
+
+    def put(s):
+        return cp(T.rr[:, 0:WN].indirect(T.ntu[:, 12 * s:12 * s + 12]), T.rot[:], ["rot0", "rot1", "ntu"], ["rr"])
+
+    def weave(main, extra, first, every):
+        extra = list(extra)
+        for i, f in enumerate(main):
+            f()
+            if extra and i >= first and (i - first) % every == 0:
+                extra.pop(0)()
+        for f in extra:
+            f()
+
+    def place(main, at):
+        for i, f in enumerate(main):
+            f()
+            for h in at.get(i, ()):
+                h()
+
+    gather(0, 0)
+    gather(0, 1)
+    dslot(0)
+    gather(0, 2)
+    pend = []
+    for s in range(S):
+        last = s == S - 1
+        pa, pb, pc, ta, tb, tc = prod(0), prod(1), prod(2), tmul(s, 0), tmul(s, 1), tmul(s, 2)
+        sa, sb_, sc_ = summ(s, 0), summ(s, 1), summ(s, 2)
+        if s == 0:
+            early = 8 if DP == 1 else 0
+            copy_in(0, 0, on_v=range(0, 8))
+            place(pa[0:early], {})
+            copy_in(0, 0, on_v=range(8, 16))
+            copy_in(0, 1)
+            copy_in(0, 2)
+            books_pe(0)
+            lc = late_consts()
+            place(pa[early:] + [lc[0], scan_y(0), lc[1], clip_x(0), clip_send(s, 0)] + ta,
+                  {22 - early + i: [f] for i, f in enumerate(lc[2:])})
+        else:
+            copy_in(s, 1)
+            hit, hd, an, vs_, msk, idx, sl, rs = pend
+            place(pa + [msk, pb[0], idx, lambda: gather(s, 2), scan_y(0), sl, lambda: preload(s, 0), lambda: books_pe(s),
+                        clip_x(0), rs, lambda: copy_in(s, 2), clip_send(s, 0)] + ta, {8: [hit], 10: [hd], 12: [an], 14: [vs_]})
+            pb = pb[1:]
+        if by_pe(s, 0):
+            books_act(s)
+            update(s, 0)
+        else:
+            update(s, 0)
+            books_act(s)
+        if by_pe(s, 0):
+            copy_out(s, 0)
+            size(s, 0)
+        place(pb + [lambda: preload(s, 1), scan_y(1), sa[0], clip_x(1), clip_send(s, 1)] + tb, {})
+        if not last:
+            times(s + 1)
+        update(s, 1)
+        place(sa[1:], {})
+        if not by_pe(s, 0):
+            copy_out(s, 0)
+            size(s, 0)
+        if by_pe(s, 1):
+            copy_out(s, 1)
+            size(s, 1)
+        place(pc + [lambda: preload(s, 2), sb_[0], scan_y(2), sb_[1], clip_x(2), clip_send(s, 2)], {})
+        turn(s)
+        place(tc, {})
+        update(s, 2)
+        place(sb_[2:], {})
+        if not by_pe(s, 1):
+            copy_out(s, 1)
+            size(s, 1)
+        pend = []
+        for b in range(NB):
+            sc, vs, vw = scans(b), votes(b, True), votes(b, False)
+            at = {}
+            if b == 0:
+                at = {1: sc_[0:1], 17: sc_[1:3], 19: sc_[3:4]}
+                if by_pe(s, 2):
+                    at[18] = [lambda: copy_out(s, 2)]
+            if b == 1:
+                if not by_pe(s, 2):
+                    copy_out(s, 2)
+                size(s, 2)
+            if pend and last:
+                at.update({0: pend[0:1], 1: pend[1:2], 3: pend[2:3], 5: pend[3:4], 7: pend[4:5]})
+            elif pend:
+                hit, hd, an, vs_, msk, idx, sl, rs = pend
+                if b == 2:
+                    copy_in(s + 1, 0)
+                at.update({0: [hit] + ([put(s)] if b == 1 else []), 1: [hd], 3: [an], 5: [vs_], 7: [msk],
+                           9: [idx, lambda: gather(s + 1, b - 1)], 13: [sl], 15: [rs]})
+                if b == 1:
+                    dslot(s + 1)
+            at[ST_AT] = at.get(ST_AT, []) + [strong_side(b)]
+            place(sc[0:2] + vs + sc[2:4] + vw, at)
+            pend = chain(s, b)
+
+    for f in pend:
+        f()
+    op("s", lambda: SY.dma_start(T.yw[:], T.wk[:, 0:3072]), ["wk0", "wk1", "wk2", "wkall"], (), dma=True)
+    fin = S % 2
+    queue_step(S - 1)
+    cp(T.tin[:], T.aa[:, fin * C:(fin + 1) * C].indirect(T.l3[:, 0:24]), akeys(fin) + ["l3"], ["tin"])()
+    tt(T.qm[:, 0:C], T.qq[:, fin * C:(fin + 1) * C], T.dm[:], A.mult, ["q%d" % fin, "dmr"], ["qm0"])()
+    op("v", lambda: V.transpose(T.tout[:], T.tin[:]), ["tin"], ["tout"])
+    tt(T.qm[:, C:2 * C], yN, T.dm[:], A.mult, ["yN", "dmr"], ["qm1"], [Y])()
+    cp(T.ydo[:], T.tout[:, 0:384].indirect(T.l4[:, 0:12]), ["tout", "l4"], ["ydo"])()
+    op("v", lambda: V.tensor_tensor_scan(T.qs[:], T.m01[:, 0:2 * C], T.qm[:], 0.0, A.mult, A.add), ["qm0", "qm1", "m01"], ["qs"])
+    op("a", lambda: ACT.dma_start(T.yd[:], T.ydo[:]), ["ydo"], (), dma=True)
+    cp(T.yqo[:], T.qs[:, 15:2 * C:16], ["qs"], ["yqo"])()
+    op("a", lambda: ACT.dma_start(T.yq[:], T.yqo[:]), ["yqo"], (), dma=True)
+    g.wait_ge(T.sem.snt, 8 * NB * S)
+    for e in ("v", "a", "p", "g"):
+        g.wait_ge(T.sem["c" + e], cnt[e])
+    for i in range(ndma[0]):
+        g.wait_ge(T.sem["dm%d" % i], 16)
+
+
+ST_AT = 27

@@ -69,7 +69,7 @@ def rank_program(g, core, T, topo):
             if k in wrote:
                 add(wrote[k], True)
             for t in read.get(k, {}).values():
-                add(t, False)
+                add(t, True)
         for b in B:
             if b in bank:
                 add(bank[b], False)
@@ -297,7 +297,7 @@ def rank_program(g, core, T, topo):
     def clip_x(b):
         def run():
             for i in range(DT):
-                ts(T.px[:, i:DT * CB:DT], resid(b), -2.0, A.max, ["so%d" % b], ["e", "xq"] if i == DT - 1 else [], [X],
+                ts(cs(T.px, b), resid(b), -2.0, A.max, ["so%d" % b], ["e%d" % b, "xq"] if i == DT - 1 else [], [X],
                    s2=2.0, f2=A.min)()
         return run
 
@@ -317,7 +317,7 @@ def rank_program(g, core, T, topo):
     def tmul(s, b):
         n = TP // DT
         dst, key, bk = (T.ts, "t%d" % b, [X]) if by_pe(s, b) else (T.wp, "wp%d" % b, [X, 2 * b, 2 * b + 1])
-        return spread([tt(taps(dst, b, k, n), taps(T.xs, b, k, n), T.px[:, 0:DT * CB], A.mult, ["x%d" % b, "e"],
+        return spread([tt(taps(dst, b, k, n), taps(T.xs, b, k, n), cs(T.px, b), A.mult, ["x%d" % b, "e%d" % b],
                           [key] if k in (0, n - 1) else [], bk) for k in range(n)])
 
     def preload(s, b):
@@ -366,7 +366,7 @@ def rank_program(g, core, T, topo):
         nm, ext, eq, o, bk = ("mx", T.mx, T.eqs, xV, X) if strong else ("mn", T.mn, T.eqw, yZ, Y)
         out = []
         n, w = TP // DE, DE * CB
-        per = max(1, 4 // DE)
+        per = n if strong else max(1, 4 // DE)
         for k in range(n):
             def run(k=k):
                 key = "eq%s%d_%d" % (nm, b, k)
@@ -394,39 +394,38 @@ def rank_program(g, core, T, topo):
         def run():
             tt(T.us2[:], T.us[:], cs(T.sgn, b), A.mult, ["us", "sgn"], ["us2"])()
             mm(xZ, T.bob[:], T.us2[:], True, True, ["us2", "bob"], ["xZ"], [X])
-            act(T.sz[:], xZ, F.Sign, ["xZ"], ["sz"], [X])
-            act(T.thr[:], T.sz[:], F.Identity, ["sz"], ["thr"], bias=-5e28, scale=5e28)
         return run
+
+    thr = ts(T.thr[:], xZ, 0.0, A.is_le, ["xZ"], ["thr"], [X], s2=-1e29, f2=A.mult)
 
     def chain(s, b):
         old, new = "a%d_%d" % (s % 2, b), "a%d_%d" % ((s + 1) % 2, b)
         ao, an = cs(T.aa, b, (s % 2) * C), cs(T.aa, b, ((s + 1) % 2) * C)
         last = s == S - 1
-        yS = T.py[:, 384:388]
+        yS = T.px[:, 320:324]
         slb = T.sl[:, 4 * b:4 * b + 4]
 
         def slots():
             even, odd, base = (T.k1s, T.k0s, T.ck[:, 4 * b:4 * b + 4]) if last else (T.w1s, T.w0s, T.cn[:])
-            mm(yS, T.idb[:], base, True, False, ["idb", "cn", "ck"], ["yZ"], [Y])
+            mm(yS, T.idb[:], base, True, False, ["idb", "cn", "ck"], ["xS"], [X])
             for r in range(16):
-                mm(yS, sel(r, even, odd), T.hit[:, r:CB:16], False, r == 15, ["hit", "w0s", "w1s", "k0s", "k1s"], ["yZ"], [Y])
+                mm(yS, sel(r, even, odd), T.hit[:, r:CB:16], False, r == 15, ["hit", "w0s", "w1s", "k0s", "k1s"], ["xS"], [X])
         hit = tt(T.hit[:], yZ, T.thr[:], A.is_lt, ["yZ", "thr"], ["hit"], [Y])
+
+        def first():
+            hit()
+            slots()
         hd = tt(yH, T.hit[:], cs(T.py, b), A.mult, ["hit", "yD"], ["yH"], [Y])
         anew = tt(an, yH, ao, A.add, ["yH", old], [new], [Y])
         if last:
-            def first():
-                hit()
-                slots()
-            return [first, ts(slb, yS, col(PM), A.add, ["yZ", "cPM"], ["sl%d" % b], [Y]), hd,
+            return [first, ts(slb, yS, col(PM), A.add, ["xS", "cPM"], ["sl%d" % b], [X]), hd,
                     cp(T.wk[:, 0:17 * C].indirect(slb), T.pqt[:], ["sl%d" % b, "pqt"], ["wk0", "wk1", "wk2"]), anew]
 
-        def vsub():
-            tt(cs(T.vi, b), cs(T.py, b, 192), an, A.subtract, ["yN", new], ["vi%d" % b], [Y])()
-            slots()
-        return [hit, hd, anew, vsub,
+        vsub = tt(cs(T.vi, b), cs(T.py, b, 192), an, A.subtract, ["yN", new], ["vi%d" % b], [Y])
+        return [first, hd, anew, vsub,
                 ts(cs(T.vm, b), cs(T.vi, b), WN - 1, A.bitwise_and, ["vi%d" % b], ["vm%d" % b]),
                 cp(cs(T.idx, b), cs(T.vm, b), ["vm%d" % b], ["idx%d" % b]),
-                ts(slb, yS, col(M16), A.add, ["yZ", "cM16"], ["sl%d" % b], [Y]),
+                ts(slb, yS, col(M16), A.add, ["xS", "cM16"], ["sl%d" % b], [X]),
                 cp(T.ws[:, 2048 * b:2048 * (b + 1)].indirect(slb), T.pqt[:], ["sl%d" % b, "pqt"], ["ws%d" % b])]
 
     def akeys(i):
@@ -483,6 +482,9 @@ def rank_program(g, core, T, topo):
             for h in at.get(i, ()):
                 h()
 
+    def run(calls):
+        place(calls, {})
+
     gather(0, 0)
     gather(0, 1)
     dslot(0)
@@ -501,67 +503,56 @@ def rank_program(g, core, T, topo):
             copy_in(0, 2)
             books_pe(0)
             lc = late_consts()
-            place(pa[early:] + [lc[0], scan_y(0), lc[1], clip_x(0), clip_send(s, 0)] + ta,
-                  {22 - early + i: [f] for i, f in enumerate(lc[2:])})
+            run(pa[early:] + lc[0:3] + [scan_y(0)] + lc[3:5] + [clip_x(0), clip_send(s, 0)])
+            place(pb, {i: [f] for i, f in enumerate(lc[5:])})
+            run(ta[0:4])
         else:
             copy_in(s, 1)
-            hit, hd, an, vs_, msk, idx, sl, rs = pend
-            place(pa + [msk, pb[0], idx, lambda: gather(s, 2), scan_y(0), sl, lambda: preload(s, 0), lambda: books_pe(s),
-                        clip_x(0), rs, lambda: copy_in(s, 2), clip_send(s, 0)] + ta, {8: [hit], 10: [hd], 12: [an], 14: [vs_]})
-            pb = pb[1:]
-        if by_pe(s, 0):
-            books_act(s)
-            update(s, 0)
-        else:
-            update(s, 0)
-            books_act(s)
-        if by_pe(s, 0):
-            copy_out(s, 0)
-            size(s, 0)
-        place(pb + [lambda: preload(s, 1), scan_y(1), sa[0], clip_x(1), clip_send(s, 1)] + tb, {})
+            first, hd, an, vs_, msk, idx, sl, rs = pend
+            run(pa[0:6] + [thr] + pa[6:] + [first, scan_y(0), hd] + pb[0:3] + [clip_x(0), an, clip_send(s, 0)] + pb[3:6]
+                + [vs_, sl] + pb[6:9] + [lambda: books_pe(s), msk, rs, pb[9], idx, lambda: gather(s, 2)] + pb[10:] + ta[0:4])
+        run([scan_y(1)] + ta[4:12] + [clip_x(1), clip_send(s, 1)] + ta[12:16])
+        if s > 0:
+            copy_in(s, 2)
+        update(s, 0)
+        run(tb)
+        update(s, 1)
+        books_act(s)
         if not last:
             times(s + 1)
-        update(s, 1)
-        place(sa[1:], {})
-        if not by_pe(s, 0):
-            copy_out(s, 0)
-            size(s, 0)
-        if by_pe(s, 1):
-            copy_out(s, 1)
-            size(s, 1)
-        place(pc + [lambda: preload(s, 2), sb_[0], scan_y(2), sb_[1], clip_x(2), clip_send(s, 2)], {})
+        run(pc + [sa[0], scan_y(2), sa[1], clip_x(2), clip_send(s, 2), sa[2], sa[3]])
         turn(s)
-        place(tc, {})
+        copy_out(s, 0)
+        size(s, 0)
+        run(tc)
         update(s, 2)
-        place(sb_[2:], {})
-        if not by_pe(s, 1):
-            copy_out(s, 1)
-            size(s, 1)
+        run(sb_)
+        copy_out(s, 1)
+        size(s, 1)
         pend = []
         for b in range(NB):
             sc, vs, vw = scans(b), votes(b, True), votes(b, False)
-            at = {}
             if b == 0:
-                at = {1: sc_[0:1], 17: sc_[1:3], 19: sc_[3:4]}
-                if by_pe(s, 2):
-                    at[18] = [lambda: copy_out(s, 2)]
-            if b == 1:
-                if not by_pe(s, 2):
-                    copy_out(s, 2)
-                size(s, 2)
-            if pend and last:
-                at.update({0: pend[0:1], 1: pend[1:2], 3: pend[2:3], 5: pend[3:4], 7: pend[4:5]})
-            elif pend:
-                hit, hd, an, vs_, msk, idx, sl, rs = pend
-                if b == 2:
-                    copy_in(s + 1, 0)
-                at.update({0: [hit] + ([put(s)] if b == 1 else []), 1: [hd], 3: [an], 5: [vs_], 7: [msk],
-                           9: [idx, lambda: gather(s + 1, b - 1)], 13: [sl], 15: [rs]})
+                run(sc[0:3] + vs + sc_[0:2] + sc[3:4] + sc_[2:4])
+            else:
                 if b == 1:
-                    dslot(s + 1)
-            at[ST_AT] = at.get(ST_AT, []) + [strong_side(b)]
-            place(sc[0:2] + vs + sc[2:4] + vw, at)
+                    copy_out(s, 2)
+                    size(s, 2)
+                if last:
+                    first, sl, hd, rs, an = pend
+                    run([sc[0], thr, sc[1], sc[2], first] + vs[0:4] + [hd] + vs[4:14] + [an, sl] + vs[14:16] + [sc[3], rs])
+                else:
+                    first, hd, an, vs_, msk, idx, sl, rs = pend
+                    if b == 1:
+                        dslot(s + 1)
+                    else:
+                        copy_in(s + 1, 0)
+                    run([sc[0], thr, sc[1], sc[2], first] + vs[0:4] + [hd] + vs[4:8] + [an] + vs[8:12] + [vs_, sl] + vs[12:16]
+                        + [msk, rs, sc[3], idx] + ([put(s)] if b == 1 else []))
+                    gather(s + 1, b - 1)
+            place(vw, {ST_AT: [strong_side(b)]})
             pend = chain(s, b)
+    thr()
 
     for f in pend:
         f()
@@ -584,4 +575,4 @@ def rank_program(g, core, T, topo):
         g.wait_ge(T.sem["dm%d" % i], 16)
 
 
-ST_AT = 27
+ST_AT = 7

@@ -3,10 +3,17 @@ from concourse.mybir import AluOpType as A, ActivationFunctionType as F
 TP, C, WN, S, NB, CB = 16, 192, 4096, 5, 3, 64
 BW = TP * CB
 BIG = float(2 ** 40)
-DP, DT, DE = 1, 1, 1
-NS = 10 if DP == 1 else 12
-PEB = ()
-f32, bf, i32, u16 = "float32", "bfloat16", "int32", "uint16"
+HUGE = float(2 ** 96)
+OFF = 2048.0
+NS = 10
+LW = CB + 4
+MODE = ["VVD", "VVD", "VVD", "VVD", "VVV"]
+GCH = 2
+CY, PC, WAKE, AF, GA, SC, DADD, DREM = 0.83, 0.6, 220, 70, 1.4, 3.0, 5500, 5000
+ROUNDS = 3
+SCH, YCH = 256, 2
+ORDER = []
+f32, bf, f16, i32, u16 = "float32", "bfloat16", "float16", "int32", "uint16"
 
 
 def sb(n, t):
@@ -16,26 +23,83 @@ def sb(n, t):
 SCRATCH = {
     "wp": ("psum", [128, 3072], f32), "px": ("psum", [128, 512], f32), "py": ("psum", [128, 512], f32),
     "wb": sb(3072, bf), "rb": sb(WN, bf), "db": sb(960, bf), "dli": sb(192, i32), "nq": sb(88, i32),
-    "rr": sb(WN, f32), "ws": sb(6144, f32), "wk": sb(17 * C, f32), "xs": sb(3072, f32), "ts": sb(3072, f32),
-    "pe": sb(NS * C, f32), "po": sb(NS * C, f32), "so": sb(NS * C, f32), "dup": sb(4 * CB, f32),
-    "mx": sb(BW, f32), "mn": sb(BW, f32), "m01": sb(BW, bf), "mbg": sb(BW, bf),
+    "rr": sb(WN, f32), "ws": sb(6144, f32), "wk": sb(17 * C, f32), "xs": sb(3072, f32), "tr": sb(3072, f32),
+    "pe": sb(NS * C, f32), "po": sb(NS * C, f32), "so": sb(NS * C, f32),
+    "mx": sb(3072, f32), "mn": sb(3072, f32), "m01": sb(512, bf), "mbg": sb(512, bf),
     "eqs": sb(3072, bf), "eqw": sb(3072, bf),
-    "es": sb(S * C, f32), "land": sb(S * C, f32), "rot": sb(C, f32),
+    "es": sb(C, f32), "eo": sb(S * C, f32), "land": sb(S * C, f32),
     "ip": sb(4, i32), "it": sb(8, i32), "col": sb(16, f32), "fj": sb(144, f32), "gb": sb(128, f32), "fn": sb(24, f32),
-    "m16": sb(16, f32), "dm": sb(C, f32),
-    "s0": sb(144, bf), "s1": sb(144, bf), "w0s": sb(144, bf), "w1s": sb(144, bf),
-    "idf": sb(128, f32), "nid": sb(128, f32), "n64": sb(128, f32), "bof": sb(128, f32), "nbo": sb(128, f32),
-    "bob": sb(128, bf), "boc": sb(128, bf), "idb": sb(128, bf), "cn": sb(4, bf),
-    "pqt": sb(CB, f32),
+    "m16": sb(16, f32), "dm": sb(C, f32), "s0": sb(144, bf), "s1": sb(144, bf), "w0s": sb(144, f16), "w1s": sb(144, f16),
+    "jj": sb(256, f32), "i64": sb(128, f32), "bof": sb(128, f32), "nbo": sb(128, f32),
+    "bob": sb(128, bf), "boc": sb(128, bf), "idb": sb(128, bf), "nib": sb(128, bf), "nhu": sb(128, bf), "n2k": sb(128, bf),
+    "boh": sb(128, f16), "nbh": sb(128, f16), "nih": sb(128, f16), "cn": sb(4, f16), "neg": sb(CB, bf), "pqt": sb(CB, f32),
     "l1": sb(24, u16), "l2": sb(12, u16), "l3": sb(24, u16), "l4": sb(12, u16), "cj": sb(12, f32), "kj": sb(12, i32),
-    "tj": sb(12, f32), "ntu": sb(60, u16), "ex": sb(1344, f32), "tin": sb(384, f32), "tout": sb(384, f32),
-    "aa": sb(2 * C, f32), "qq": sb(2 * C, f32), "ab1": sb(C, f32), "ab2": sb(C, f32), "sgn": sb(C, bf),
-    "us": sb(CB, bf), "us2": sb(CB, bf), "uw": sb(CB, bf), "sz": sb(CB, f32), "thr": sb(CB, f32), "hit": sb(CB, bf),
-    "vi": sb(C, i32), "vm": sb(C, i32), "idx": sb(C, u16), "sl": sb(12, u16),
-    "k0s": sb(144, bf), "k1s": sb(144, bf), "ck": sb(12, bf),
+    "tj": sb(12, f32), "ntu": sb(60, u16), "ex": sb(1344, f16), "tin": sb(384, f32), "tout": sb(384, f32),
+    "aa": sb(S * C, f16), "af": sb(C, f32), "ab1": sb(C, f32), "ab2": sb(C, f32), "sgn": sb(C, bf),
+    "us2": sb(CB, bf), "uw": sb(CB, bf), "sx": sb(CB, bf), "sm": sb(CB, bf), "hit": sb(CB, f16),
+    "vi": sb(C, i32), "vm": sb(C, i32), "idx": sb(NB * LW, u16),
+    "k0s": sb(144, f16), "k1s": sb(144, f16), "ck": sb(12, f16),
     "ydo": sb(C, f32), "qm": sb(2 * C, f32), "qs": sb(2 * C, f32), "yqo": sb(24, f32),
 }
-SEMAPHORES = (["cv", "ca", "cp", "cg", "snt"] + ["arr%d" % s for s in range(S)] + ["dm%d" % i for i in range(24)])
+SEMAPHORES = (["cv", "ca", "cp", "cg", "snt"] + ["arr%d" % s for s in range(S)] + ["dm%d" % i for i in range(60)])
+
+
+def issue_order(calls):
+    n = len(calls)
+    after = [[] for _ in calls]
+    for i, c in enumerate(calls):
+        for d in c["deps"]:
+            after[d].append(i)
+
+    def lag(i, j):
+        return calls[i]["ns"] + (0 if calls[i]["e"] == calls[j]["e"] == "p" else WAKE)
+
+    def clash(spans, a, b, sign):
+        lo, hi = 0, len(spans)
+        while lo < hi:
+            m = (lo + hi) // 2
+            if spans[m][0] < b - 1e-6:
+                lo = m + 1
+            else:
+                hi = m
+        hits = [s for s in spans[max(0, lo - 12):lo] if s[1] > a + 1e-6]
+        if not hits:
+            return 0
+        return hits[-1][1] - a if sign > 0 else hits[0][0] - b
+
+    def place(order, sign):
+        t, spans = {}, {}
+        for i in order:
+            c = calls[i]
+            if sign > 0:
+                x = max([t[d] + lag(d, i) for d in c["deps"]] + [0.0])
+            else:
+                x = min([t[j] - lag(i, j) for j in after[i]] + [-c["ns"]])
+            moved = c["kind"] != "l"
+            if not moved and sign > 0:
+                x = i * c["hold"]
+            while moved:
+                moved = clash(spans.get(c["e"], []), x, x + c["hold"], sign)
+                for k in c["B"]:
+                    for f in "vap":
+                        if not moved and f != c["e"]:
+                            moved = clash(spans.get((k, f), []), x - WAKE, x + c["ns"] + WAKE, sign)
+                x += moved
+            t[i] = x
+            for key, end in [(c["e"], x + c["hold"])] + [((k, c["e"]), x + c["ns"]) for k in c["B"]]:
+                spans.setdefault(key, []).append((x, end))
+                spans[key].sort()
+        return t
+    order, best = list(range(n)), None
+    for _ in range(ROUNDS):
+        t = place(order, 1)
+        order = sorted(range(n), key=lambda i: (t[i], i))
+        span = max(t[i] + calls[i]["ns"] for i in range(n))
+        if best is None or span < best[0]:
+            best = (span, order)
+        u = place(sorted(range(n), key=lambda i: (-t[i] - calls[i]["ns"], -i)), -1)
+        order = sorted(range(n), key=lambda i: (u[i], i))
+    return best[1]
 
 
 def rank_program(g, core, T, topo):
@@ -44,75 +108,53 @@ def rank_program(g, core, T, topo):
         return
     N = len(T.cores)
     V, ACT, PE, SY = g.vector, g.scalar, g.tensor, g.sync
-    Q = {"v": V, "a": ACT, "p": PE, "g": g, "s": SY}
-    cnt = {"v": 0, "a": 0, "p": 0, "g": 0}
-    seen = {e: {} for e in Q}
-    wrote, read, bank = {}, {}, {}
-    ndma = [0]
+    calls, wrote, read, before = [], {}, {}, {}
 
-    def wait(e, tok):
-        if seen[e].get(tok[0], 0) < tok[1]:
-            Q[e].wait_ge(T.sem[tok[0]], tok[1])
-            seen[e][tok[0]] = tok[1]
-
-    def op(e, call, R=(), W=(), B=(), dma=False):
-        need = {}
-
-        def add(tok, raw):
-            if tok[2] == e and not tok[3] and not dma and (e == "p" or not raw):
-                return
-            need[tok[0]] = max(need.get(tok[0], 0), tok[1])
+    def op(e, call, ns, R=(), W=(), B=(), kind="c", part=None, hold=None):
+        i, deps = len(calls), set()
         for k in R:
-            if k in wrote:
-                add(wrote[k], True)
+            deps.update(wrote.get(k, (None, []))[1])
         for k in W:
-            if k in wrote:
-                add(wrote[k], True)
-            for t in read.get(k, {}).values():
-                add(t, True)
-        for b in B:
-            if b in bank:
-                add(bank[b], False)
-        for s_, n_ in need.items():
-            wait(e, (s_, n_))
-        ins = call()
-        if dma:
-            name = "dm%d" % ndma[0]
-            ndma[0] += 1
-            ins.then_inc(T.sem[name], 16)
-            tok = (name, 16, e, True)
-        else:
-            cnt[e] += 1
-            ins.then_inc(T.sem["c" + e], 1)
-            tok = ("c" + e, cnt[e], e, False)
+            if part is None or wrote.get(k, (None,))[0] != part:
+                before[k] = wrote.get(k, (None, []))[1] + read.get(k, [])
+                wrote[k], read[k] = (part, []), []
+            deps.update(before[k])
+            wrote[k][1].append(i)
         for k in R:
-            read.setdefault(k, {})[tok[0]] = tok
-        for k in W:
-            wrote[k] = tok
-            read[k] = {}
-        for b in B:
-            bank[b] = tok
-        return tok
+            if k not in W:
+                read.setdefault(k, []).append(i)
+        calls.append(dict(e=e, call=call, ns=ns, hold=ns if hold is None else hold, deps=sorted(deps), B=B, kind=kind))
 
-    def tt(o, a, b, f, R, W, B=()):
-        return lambda: op("v", lambda: V.tensor_tensor(o, a, b, f), R, W, B)
+    def vns(n):
+        return max(64, n) * CY
 
-    def ts(o, a, s1, f1, R, W, B=(), s2=None, f2=None):
+    def tt(o, a, b, f, R, W, B=(), n=64, part=None):
+        op("v", lambda: V.tensor_tensor(o, a, b, f), vns(n), R, W, B, part=part)
+
+    def ts(o, a, s1, f1, R, W, B=(), s2=None, f2=None, n=64, part=None):
         if f2 is None:
-            return lambda: op("v", lambda: V.tensor_scalar(o, a, s1, None, f1), R, W, B)
-        return lambda: op("v", lambda: V.tensor_scalar(o, a, s1, s2, f1, f2), R, W, B)
+            op("v", lambda: V.tensor_scalar(o, a, s1, None, f1), vns(n), R, W, B, part=part)
+        else:
+            op("v", lambda: V.tensor_scalar(o, a, s1, s2, f1, f2), vns(n), R, W, B, part=part)
 
-    def cp(o, a, R, W, B=()):
-        return lambda: op("v", lambda: V.tensor_copy(o, a), R, W, B)
+    def cp(o, a, R, W, B=(), n=64):
+        op("v", lambda: V.tensor_copy(o, a), vns(n), R, W, B)
 
-    def ms(o, c, W):
-        op("v", lambda: V.memset(o, c), (), W)
+    def ms(o, c, W, n=64):
+        op("v", lambda: V.memset(o, c), vns(n), (), W)
 
-    def act(o, a, f, R, W, B=(), bias=0.0, scale=1.0):
-        op("a", lambda: ACT.activation(o, a, f, bias=bias, scale=scale), R, W, B)
+    def scan(o, a, b, f0, f1, R, W, B, n, part=None):
+        op("v", lambda: V.tensor_tensor_scan(o, a, b, 0.0, f0, f1), vns(n), R, W, B, part=part)
 
-    def mm(o, l, r, st, sp, R, W, B):
-        op("p", lambda: PE.matmul(o, l, r, st, sp), R, W, B)
+    def act(o, a, f, R, W, B=(), bias=0.0, scale=1.0, n=64, part=None):
+        op("a", lambda: ACT.activation(o, a, f, bias=bias, scale=scale), AF + n * CY, R, W, B, part=part)
+
+    def mm(o, l, r, st, sp, R, W, bk, n=64):
+        op("p", lambda: PE.matmul(o, l, r, st, sp), n * PC, R, list(W) + ["bank%d" % bk], [bk])
+
+    def dma(e, o, a, ns, R, W, **kw):
+        q = {"a": ACT, "s": SY, "g": g}[e]
+        op(e, lambda: q.dma_start(o, a, **kw), ns, R, W, kind="d" if R else "l", hold=800 if e == "g" else 30)
 
     def col(i):
         return T.col[:, i:i + 1]
@@ -120,459 +162,362 @@ def rank_program(g, core, T, topo):
     def wbank(b):
         return (2 * b, 2 * b + 1)
 
+    def wkey(j, h=None):
+        return ["wp%d_%d" % (j, i) for i in ((0, 1) if h is None else (h,))]
+
+    def wkeys(b, h=None):
+        return wkey(2 * b, h) + wkey(2 * b + 1, h)
+
+    def per(name, b):
+        return ["%s%d" % (name, j) for j in wbank(b)]
+
     def blk(t, b, k=None):
         return t[:, b * BW:(b + 1) * BW] if k is None else t[:, b * BW + k:(b + 1) * BW:TP]
 
-    def taps(t, b, k, n):
-        return t[:, b * BW + k:(b + 1) * BW:n]
+    def half(t, j):
+        return t[:, 512 * j:512 * (j + 1)]
 
-    def spread(calls):
-        return [f for c_ in calls for f in [c_] + [lambda: None] * (TP // len(calls) - 1)]
+    def store(j):
+        return half(T.ws, j + 2 * (j // 2))
 
     def cs(t, b, off=0):
         return t[:, off + b * CB:off + (b + 1) * CB]
 
-    X, Y = 6, 7
-    yD, yN, yZ, yH = T.py[:, 0:192], T.py[:, 192:384], T.py[:, 384:448], T.py[:, 448:512]
-    xV, xZ = T.px[:, 384:448], T.px[:, 448:512]
-
-    op("s", lambda: SY.dma_start(T.rb[:], T.r0[:]), (), ["rb"], dma=True)
-    op("a", lambda: ACT.dma_start(T.nq[:, 0:60], T.nt[:]), (), ["nt"], dma=True)
-    op("a", lambda: ACT.dma_start(T.dli[:], T.dl[:]), (), ["dli"], dma=True)
-    op("a", lambda: ACT.dma_start(T.nq[:, 60:84], T.qu[:]), (), ["qu"], dma=True)
-    op("s", lambda: SY.dma_start(T.wb[:, 0:1536], T.w0[:, 0:1536]), (), ["wb0"], dma=True)
-    op("a", lambda: ACT.dma_start(T.db[:, 0:C], T.d0[:, 0:C]), (), ["db0"], dma=True)
-    op("s", lambda: SY.dma_start(T.wb[:, 1536:3072], T.w0[:, 1536:3072]), (), ["wb1"], dma=True)
-    op("s", lambda: SY.dma_start(T.db[:, C:960], T.d0[:, C:960]), (), ["db1"], dma=True)
-
-    def io(o, pat, cm, W, small=True):
-        if small:
-            op("g", lambda: g.iota(o, pat, 0, cm, allow_small_or_imprecise_dtypes=True), (), W)
-        else:
-            op("g", lambda: g.iota(o, pat, 0, cm), (), W)
-    io(T.ip[:, 0:1], [[0, 1]], 1, ["ip"], False)
-    io(T.fj[:], [[1, 144]], 0, ["fj"])
-    io(T.gb[:], [[16, 8], [0, 16]], 0, ["gb"])
-    io(T.fn[:], [[1, 12], [0, 2]], 0, ["fn"])
-    io(T.dm[:], [[0, 12], [1, 16]], 0, ["dmr"])
-    op("g", lambda: g.dma_start(T.rr[:], T.r0[:]), ["wb1"], ["rr"], dma=True)
-
-    P_, PM, PG, G15, G16, P31, M12, M16, H16, BS, BWK, WSL, WK = range(13)
-    ts(T.it[:, 0:1], T.ip[:, 0:1], 15, A.bitwise_and, ["ip"], ["it0"])()
-    ts(T.it[:, 1:2], T.ip[:, 0:1], 31, A.bitwise_and, ["ip"], ["it1"])()
-    ts(T.it[:, 2:3], T.ip[:, 0:1], 112, A.bitwise_and, ["ip"], ["it2"])()
-    cp(col(P_), T.ip[:, 0:1], ["ip"], ["cP"])()
-    cp(col(PM), T.it[:, 0:1], ["it0"], ["cPM"])()
-    cp(col(PG), T.it[:, 2:3], ["it2"], ["cPG"])()
-    cp(col(P31), T.it[:, 1:2], ["it1"], ["cP31"])()
-    ts(col(M12), T.it[:, 0:1], 12.0, A.mult, ["it0"], ["cM12"])()
-    ts(T.m16[:], T.fj[:, 0:16], col(PM), A.is_equal, ["fj", "cPM"], ["m16"])()
-    ts(T.bof[:], T.gb[:], col(PG), A.is_equal, ["gb", "cPG"], ["bof"])()
-    ts(T.l1[:], T.fn[:], col(M12), A.add, ["fn", "cM12"], ["l1"])()
-    ts(T.l2[:], T.fj[:, 0:12], 32.0, A.mult, ["fj", "cP31"], ["l2"], s2=col(P31), f2=A.add)()
-    ms(T.pe[:, 0:NS * C:NS], BIG, ["pc0"])
-    ms(T.po[:, 0:NS * C:NS], -BIG, ["pc1"])
-    for t_, j in ((T.pe, 5), (T.pe, 6), (T.po, 5), (T.po, 6)) if DP == 2 else ():
-        ms(t_[:, j:NS * C:NS], 0.0, [])
-    ms(T.po[:, NS - 1:NS * C:NS], 0.0, ["pc2"])
-    ms(T.m01[:], 1.0, ["m01"])
-    for r in range(16):
-        ts(T.ex[:, r:1344:16], T.nq[:, 0:84], T.m16[:, r:r + 1], A.mult, ["nt", "qu", "m16"], ["ex%d" % r])()
-    EX = ["ex%d" % r for r in range(16)]
-    mm(yN, T.bof[:], T.ex[:, 0:192], True, True, EX + ["bof"], ["yN"], [Y])
-    mm(T.px[:, 0:384], T.bof[:], T.ex[:, 960:1344], True, True, EX + ["bof"], ["xq"], [X])
-    cp(T.tin[:], T.dli[:, 0:192].indirect(T.l1[:, 0:24]), ["dli", "l1"], ["tin"])()
-    ts(T.idf[:], T.fj[:, 0:128], col(P_), A.is_equal, ["fj", "cP"], ["idf"])()
-    op("v", lambda: V.transpose(T.tout[:], T.tin[:]), ["tin"], ["tout"])
-    ts(col(G15), col(PG), 15.0, A.add, ["cPG"], ["cG15"])()
-    cp(T.aa[:, 0:192], T.tout[:, 0:384].indirect(T.l2[:, 0:12]), ["tout", "l2"], ["a0_0", "a0_1", "a0_2"])()
-    ts(col(G16), col(PG), 16.0, A.add, ["cPG"], ["cG16"])()
-    tt(T.vi[:], yN, T.aa[:, 0:192], A.subtract, ["yN", "a0_0", "a0_1", "a0_2"], ["vi0", "vi1", "vi2"], [Y])()
-    ts(T.nid[:], T.idf[:], -1.0, A.mult, ["idf"], ["nid"])()
-    ts(T.vm[:], T.vi[:], WN - 1, A.bitwise_and, ["vi0", "vi1", "vi2"], ["vm0", "vm1", "vm2"])()
-    ts(T.n64[:], T.idf[:], 1.0 / 64, A.mult, ["idf"], ["n64"])()
-    cp(T.idx[:], T.vm[:], ["vm0", "vm1", "vm2"], ["idx0", "idx1", "idx2"])()
-    act(T.qq[:], T.px[:, 0:384], F.Copy, ["xq"], ["q0", "q1"], [X])
-    ms(T.mbg[:], 0.0, ["mbg"])
-    ms(T.m01[:, 0:BW:16], 0.0, ["m01"])
-    ms(T.mbg[:, 0:BW:16], 1e20, ["mbg"])
-    ms(T.pqt[:], 0.25, ["pqt"])
-    ts(col(BS), col(PM), -0.71, A.mult, ["cPM"], ["cBS"], s2=-94.0, f2=A.add)()
-    ts(col(BWK), col(PM), -0.55, A.mult, ["cPM"], ["cBW"], s2=-78.8, f2=A.add)()
-    ts(col(WSL), col(PM), -256.0, A.add, ["cPM"], ["cWS"])()
-    ts(col(M16), col(PM), 16.0, A.mult, ["cPM"], ["cM16"])()
-    ts(T.s0[:], T.fj[:], col(G15), A.is_equal, ["fj", "cG15"], ["s0"])()
-    ts(T.s1[:], T.fj[:], col(G16), A.is_equal, ["fj", "cG16"], ["s1"])()
-    ts(T.w0s[:], T.fj[:], col(G15), A.is_equal, ["fj", "cG15", "cWS"], ["w0s"], s2=col(WSL), f2=A.mult)()
-    ts(T.w1s[:], T.fj[:], col(G16), A.is_equal, ["fj", "cG16", "cWS"], ["w1s"], s2=col(WSL), f2=A.mult)()
-    ts(T.nbo[:], T.bof[:], -1.0, A.mult, ["bof"], ["nbo"])()
-    ts(T.idb[:], T.idf[:], -2.5, A.mult, ["idf"], ["idb"])()
-    cp(T.bob[:], T.bof[:], ["bof"], ["bob"])()
-    ts(T.cn[:], T.fj[:, 0:4], 512.0, A.mult, ["fj"], ["cn"], s2=256.0, f2=A.add)()
-    tt(T.boc[:], T.idb[:], T.bof[:], A.add, ["idb", "bof"], ["boc"])()
-    cp(T.ntu[:], T.nq[:, 0:60], ["nt"], ["ntu"])()
-    cp(T.idb[:], T.idf[:], ["idf", "boc"], ["idb"])()
-
-    def late_consts():
-        return [
-            ts(T.cj[:], T.fj[:, 0:12], 16.0, A.mult, ["fj", "cPM"], ["cj"], s2=col(PM), f2=A.add),
-            ts(T.l3[:], T.fn[:], 16.0, A.mult, ["fn", "cPM"], ["l3"], s2=col(PM), f2=A.add),
-            tt(col(H16), col(P31), col(PM), A.subtract, ["cP31", "cPM"], ["cH"]),
-            ts(T.tj[:], T.cj[:], -5.5, A.add, ["cj"], ["tj"], s2=1.0 / 12, f2=A.mult),
-            ts(T.dm[:], T.dm[:], col(PM), A.is_equal, ["dmr", "cPM"], ["dmr"]),
-            cp(T.kj[:], T.tj[:], ["tj"], ["kj"]),
-            ts(col(WK), col(PM), float(C), A.mult, ["cPM"], ["cWK"], s2=-16.0 * C, f2=A.add),
-            ts(T.ck[:], T.fj[:, 0:12], 16.0, A.mult, ["fj"], ["ck"], s2=16.0 * C, f2=A.add),
-            ts(T.k0s[:], T.s0[:], col(WK), A.mult, ["s0", "cWK"], ["k0s"]),
-            ts(T.k1s[:], T.s1[:], col(WK), A.mult, ["s1", "cWK"], ["k1s"]),
-            ts(T.tj[:], T.kj[:], -383.0 / 32, A.mult, ["kj"], ["tj"]),
-            tt(T.tj[:], T.tj[:], T.cj[:], A.add, ["tj", "cj"], ["tj"]),
-            ts(T.l4[:], T.tj[:], 32.0, A.mult, ["tj", "cH"], ["l4"], s2=col(H16), f2=A.add),
-        ]
-
     def sel(k, even, odd):
         return even[:, 16 - k:144 - k] if k % 2 == 0 else odd[:, 15 - k:143 - k]
 
-    def gather(s, b):
+    X, Y = 6, 7
+    xD, xV, xZ = T.px[:, 192:384], T.px[:, 384:448], T.px[:, 448:512]
+    yE, yS, yL, yV, yR, yT = (T.py[:, 0:64], T.py[:, 64:68], T.py[:, 0:68], T.py[:, 128:192], T.py[:, 192:256],
+                              T.py[:, 256:448])
+    idf = T.jj[:, 0:128]
+
+    dma("a", T.nq[:, 0:60], T.nt[:], 2200, (), ["nt"])
+    dma("s", T.dli[:], T.dl[:], 2400, (), ["dli"])
+    dma("a", T.nq[:, 60:84], T.qu[:], 2400, (), ["qu"])
+    dma("s", T.rb[:], T.r0[:], 5000, (), ["rb"])
+    dma("s", T.wb[:, 0:1536], T.w0[:, 0:1536], 6000, (), ["wb0"])
+    dma("s", T.wb[:, 1536:3072], T.w0[:, 1536:3072], 7000, (), ["wb1"])
+    dma("s", T.db[:, 0:C], T.d0[:, 0:C], 7200, (), ["db0"])
+    dma("s", T.db[:, C:960], T.d0[:, C:960], 7800, (), ["db1"])
+
+    def io(o, pat, cm, W, n, small=True):
+        if small:
+            op("g", lambda: g.iota(o, pat, 0, cm, allow_small_or_imprecise_dtypes=True), 130 + 2 * n * CY, (), W)
+        else:
+            op("g", lambda: g.iota(o, pat, 0, cm), 130 + 2 * n * CY, (), W)
+    io(T.ip[:, 0:1], [[0, 1]], 1, ["ip"], 1, False)
+    io(T.fn[:], [[1, 12], [0, 2]], 0, ["fn"], 24)
+    io(T.fj[:], [[1, 144]], 0, ["fj"], 144)
+    io(T.gb[:], [[16, 8], [0, 16]], 0, ["gb"], 128)
+    io(T.jj[:], [[0, 2], [1, 128]], -1, ["jj"], 256)
+    io(T.dm[:], [[0, 12], [1, 16]], 0, ["dmr"], 192)
+    dma("g", T.rr[:], T.r0[:], 8000, ["wb1"], ["rr"])
+
+    PM, PG, G15, G16, P31, M12, M16, H16, BS, BWK, WSL, WK = range(12)
+    ts(T.it[:, 0:1], T.ip[:, 0:1], 15, A.bitwise_and, ["ip"], ["it0"])
+    ts(T.it[:, 1:2], T.ip[:, 0:1], 31, A.bitwise_and, ["ip"], ["it1"])
+    ts(T.it[:, 2:3], T.ip[:, 0:1], 112, A.bitwise_and, ["ip"], ["it2"])
+    cp(col(PM), T.it[:, 0:1], ["it0"], ["cPM"])
+    cp(col(PG), T.it[:, 2:3], ["it2"], ["cPG"])
+    cp(col(P31), T.it[:, 1:2], ["it1"], ["cP31"])
+    ts(col(M12), T.it[:, 0:1], 12.0, A.mult, ["it0"], ["cM12"])
+    ts(T.m16[:], T.fj[:, 0:16], col(PM), A.is_equal, ["fj", "cPM"], ["m16"])
+    ts(T.boh[:], T.gb[:], col(PG), A.is_equal, ["gb", "cPG"], ["boh"], n=128)
+    ts(T.l1[:], T.fn[:], col(M12), A.add, ["fn", "cM12"], ["l1"])
+    ts(T.l2[:], T.fj[:, 0:12], 32.0, A.mult, ["fj", "cP31"], ["l2"], s2=col(P31), f2=A.add)
+    ts(T.nib[:], T.jj[:, 0:128], 0.0, A.is_equal, ["jj"], ["nib"], s2=-1.0, f2=A.mult, n=128)
+    A0 = ["a0_0", "a0_1", "a0_2"]
+    cp(T.tin[:], T.dli[:, 0:192].indirect(T.l1[:, 0:24]), ["dli", "l1"], ["tin"], n=60 + 384 * GA / CY)
+    op("v", lambda: V.transpose(T.tout[:], T.tin[:]), vns(384), ["tin"], ["tout"])
+    ts(T.aa[:, 0:192], T.tout[:, 0:384].indirect(T.l2[:, 0:12]), -OFF, A.add, ["tout", "l2"], A0, n=60 + 192 * GA / CY)
+    for r in range(16):
+        ts(T.ex[:, r:1344:16], T.nq[:, 0:84], -OFF, A.add, ["nt", "qu", "m16"], ["ex"], s2=T.m16[:, r:r + 1], f2=A.mult,
+           n=84, part="ex")
+    mm(yT, T.boh[:], T.ex[:, 0:192], True, True, ["ex", "boh"], ["yT"], Y, 192)
+    for b in range(NB):
+        tt(cs(T.vi, b), cs(T.py, b, 256), cs(T.aa, b), A.subtract, ["yT"] + A0, ["vi%d" % b], [Y])
+        ts(cs(T.vm, b), cs(T.vi, b), WN - 1, A.bitwise_and, ["vi%d" % b], ["vm%d" % b])
+        cp(T.idx[:, LW * b:LW * b + CB], cs(T.vm, b), ["vm%d" % b], ["idx%d" % b])
+    ms(T.pe[:, 0:NS * C:NS], BIG, ["pc0"], 192)
+    ms(T.po[:, 0:NS * C:NS], -BIG, ["pc1"], 192)
+    ms(T.po[:, NS - 1:NS * C:NS], 0.0, ["pc2"], 192)
+    ts(T.jj[:], T.jj[:], 0.0, A.is_equal, [], ["jj"], n=256)
+
+    def constants():
+        act(T.bof[:], T.gb[:], F.Copy, ["gb"], ["bof"], n=128)
+        ts(T.bof[:], T.bof[:], col(PG), A.is_equal, ["cPG"], ["bof"], n=128)
+        ts(col(G15), col(PG), 15.0, A.add, ["cPG"], ["cG15"])
+        ts(col(G16), col(PG), 16.0, A.add, ["cPG"], ["cG16"])
+        ts(col(WSL), col(PM), -float(BW), A.add, ["cPM"], ["cWS"])
+        ts(col(M16), col(PM), 16.0, A.mult, ["cPM"], ["cM16"], s2=float(BW), f2=A.add)
+        ts(col(BS), col(PM), -0.71, A.mult, ["cPM"], ["cBS"], s2=-94.0, f2=A.add)
+        ts(col(BWK), col(PM), -0.55, A.mult, ["cPM"], ["cBW"], s2=-78.8, f2=A.add)
+        ts(col(WK), col(PM), -16.0, A.add, ["cPM"], ["cWK"], s2=float(C), f2=A.mult)
+        ts(T.s0[:], T.fj[:], col(G15), A.is_equal, ["fj", "cG15"], ["s0"], n=144)
+        ts(T.s1[:], T.fj[:], col(G16), A.is_equal, ["fj", "cG16"], ["s1"], n=144)
+        for o, a, c_, k in ((T.w0s, T.s0, WSL, "cWS"), (T.w1s, T.s1, WSL, "cWS"), (T.k0s, T.s0, WK, "cWK"), (T.k1s, T.s1, WK, "cWK")):
+            ts(o[:], a[:], col(c_), A.mult, ["s0", "s1", k], ["wsel"], n=72, part="wsel")
+        ts(T.nih[:], T.nib[:], 1.0, A.mult, ["nib"], ["nih"])
+        ts(T.nbh[:], T.boh[:], -1.0, A.mult, ["boh"], ["nbh"])
+        ts(T.cn[:], T.fj[:, 0:4], -256.0, A.mult, ["fj", "cM16"], ["cn"], s2=col(M16), f2=A.subtract)
+        ts(T.ck[:], T.fj[:, 0:12], -16.0, A.mult, ["fj"], ["ck"], s2=-16.0 * C, f2=A.add)
+        cp(T.ntu[:], T.nq[:, 0:60], ["nt"], ["ntu"])
+        ms(T.pqt[:], 0.25, ["pqt"])
+        ms(T.neg[:], -1.0, ["neg"])
+        for o, a, k, f in ((T.i64, idf, "jj", 1.0 / 64), (T.nbo, T.bof[:], "bof", -1.0), (T.bob, T.bof[:], "bof", 1.0),
+                           (T.nhu, T.nib[:], "nib", HUGE), (T.n2k, T.nib[:], "nib", 2048.0), (T.idb, T.nib[:], "nib", 2.5)):
+            act(o[:], a, F.Copy, [k], ["mats"], scale=f, n=128, part="mats")
+        tt(T.boc[:], T.idb[:], T.bob[:], A.add, ["mats"], ["boc"], n=256)
+        for h in range(4):
+            act(T.m01[:, 128 * h:128 * (h + 1)], T.fj[:, 0:128], F.Identity, ["fj"], ["m01"], scale=0.0, bias=1.0, n=128, part="m")
+            act(T.mbg[:, 128 * h:128 * (h + 1)], T.fj[:, 0:128], F.Copy, ["fj"], ["mbg"], scale=0.0, n=128, part="m")
+        act(T.m01[:, 0:512:16], T.fj[:, 0:32], F.Copy, ["fj"], ["m01"], scale=0.0)
+        act(T.mbg[:, 0:512:16], T.fj[:, 0:32], F.Exp, ["fj"], ["mbg"], scale=0.0, bias=8.0, n=1600)
+
+    def last_constants():
+        ts(T.cj[:], T.fj[:, 0:12], 16.0, A.mult, ["fj", "cPM"], ["cj"], s2=col(PM), f2=A.add)
+        ts(T.l3[:], T.fn[:], 16.0, A.mult, ["fn", "cPM"], ["l3"], s2=col(PM), f2=A.add)
+        tt(col(H16), col(P31), col(PM), A.subtract, ["cP31", "cPM"], ["cH"])
+        ts(T.dm[:], T.dm[:], col(PM), A.is_equal, ["cPM"], ["dmr"], n=192)
+        ts(T.tj[:], T.cj[:], -5.5, A.add, ["cj"], ["tj"], s2=1.0 / 12, f2=A.mult)
+        cp(T.kj[:], T.tj[:], ["tj"], ["kj"])
+        ts(T.tj[:], T.kj[:], -383.0 / 32, A.mult, ["kj"], ["tj"])
+        tt(T.tj[:], T.tj[:], T.cj[:], A.add, ["cj"], ["tj"])
+        ts(T.l4[:], T.tj[:], 32.0, A.mult, ["tj", "cH"], ["l4"], s2=col(H16), f2=A.add)
+
+    def taps_in(b, l, h, stop):
+        for j in wbank(b):
+            for k in range(8 * h, 8 * h + 8):
+                mm(T.wp[:, 512 * j + k:512 * (j + 1):TP], l, T.wb[:, k * C + 32 * j:k * C + 32 * (j + 1)],
+                   k % 8 == 0, stop and k % 8 == 7, ["wb%d" % h, "nib"], wkey(j, h), j)
+
+    def fetch(s, b):
         win, key = (T.rb, "rb") if s == 0 else (T.rr, "rr")
-        act(blk(T.xs, b), win[:, 0:WN].indirect(cs(T.idx, b)), F.Copy, [key, "idx%d" % b], ["x%d" % b])
-
-    def dslot(s):
-        act(T.pe[:, NS - 1:NS * C:NS], T.db[:, s * C:(s + 1) * C], F.Copy, ["db%d" % min(s, 1)], ["pd0", "pd1", "pd2"])
-
-    def copy_in(s, b, on_v=False):
+        n = CB // GCH
+        for i in range(GCH):
+            act(T.xs[:, b * BW + TP * n * i:b * BW + TP * n * (i + 1)],
+                win[:, 0:WN].indirect(T.idx[:, LW * b + n * i:LW * b + n * (i + 1)]), F.Copy,
+                [key, "idx%d" % b], ["x%d" % b], n=TP * n * GA / CY, part="x%d" % s)
         if s == 0:
-            for k in (range(TP) if on_v is False else on_v):
-                src, key = cs(T.wb, b, k * C), ["wb%d" % (k // 8)]
-                if on_v:
-                    ts(blk(T.wp, b, k), src, -1.0, A.mult, key, ["wp%d" % b] if k % 8 in (0, 7) else [], wbank(b))()
-                else:
-                    act(blk(T.wp, b, k), src, F.Copy, key, ["wp%d" % b] if k in (0, TP - 1) else [], wbank(b), scale=-1.0)
-            return
-        for n in range(4):
-            o = 256 * (4 * b + n)
-            act(T.wp[:, o:o + 256], T.ws[:, 2 * o:2 * o + 256], F.Copy, ["ws%d" % b],
-                ["wp%d" % b] if n in (0, 3) else [], wbank(b), scale=-1.0)
+            taps_in(b, T.nib[:], 0, True)
+            taps_in(b, T.nib[:], 1, True)
+        else:
+            for j in wbank(b):
+                act(half(T.wp, j), store(j), F.Copy, ["ws%d" % j], wkey(j), [j], scale=-1.0, n=512)
+        if b == 0:
+            act(T.pe[:, NS - 1:NS * C:NS], T.db[:, s * C:(s + 1) * C], F.Copy, ["db%d" % min(s, 1)], ["pd"], n=192)
 
-    def by_pe(s, b):
-        return s > 0 and b in PEB
-
-    def in_psum(s, b):
-        return s in (0, S - 1) or by_pe(s, b)
-
-    def copy_out(s, b):
-        if s == S - 1:
-            for k in range(TP):
-                act(cs(T.wk, b, k * C), blk(T.wp, b, k), F.Copy, ["wp%d" % b], ["wk%d" % b] if k in (0, TP - 1) else [],
-                    wbank(b))
-        elif in_psum(s, b):
-            for n in range(4):
-                o = 256 * (4 * b + n)
-                act(T.ws[:, 2 * o:2 * o + 256], T.wp[:, o:o + 256], F.Copy, ["wp%d" % b],
-                    ["ws%d" % b] if n in (0, 3) else [], wbank(b))
-
-    def size(s, b):
-        if in_psum(s, b):
-            act(blk(T.wp, b), blk(T.wp, b), F.Abs, ["wp%d" % b, "ws%d" % b, "wk%d" % b], ["wp%d" % b], wbank(b))
-            return
-        for n in range(4):
-            o = 256 * (4 * b + n)
-            act(T.wp[:, o:o + 256], T.ws[:, 2 * o:2 * o + 256], F.Abs, ["ws%d" % b], ["wp%d" % b] if n in (0, 3) else [], wbank(b))
-
-    def prod(b):
+    def residual(s, b):
         c0, c1 = NS * b * CB, NS * (b + 1) * CB
-        n = TP // DP
-        return spread([tt((T.pe, T.po)[k % 2][:, c0 + 1 + k // 2:c1:NS // DP], taps(T.wp, b, k, n), taps(T.xs, b, k, n), A.mult,
-                          ["wp%d" % b, "x%d" % b], ["p%d" % b] if k in (0, n - 1) else [], wbank(b)) for k in range(n)])
+        for k in range(TP):
+            tt((T.pe, T.po)[k % 2][:, c0 + 1 + k // 2:c1:NS], blk(T.wp, b, k), blk(T.xs, b, k), A.mult,
+               wkeys(b, k // 8) + ["x%d" % b], ["p%d" % b], wbank(b), part=s)
+        n = NS * CB // YCH
+        for o in range(c0, c1, n):
+            scan(T.so[:, o:o + n], T.pe[:, o:o + n], T.po[:, o:o + n], A.add, A.add, ["p%d" % b, "pd", "pc0", "pc1", "pc2"],
+                 ["so%d" % b], (), n, part=s)
+        src = T.so[:, c0 + NS - 1:c1:NS]
+        ts(cs(T.px, b), src, -2.0, A.max, ["so%d" % b], ["e%d" % b], [X], s2=2.0, f2=A.min)
+        ts(cs(T.es, b), src, -2.0, A.max, ["so%d" % b], ["es%d" % b], s2=2.0, f2=A.min)
 
-    def scan_y(b):
-        c0, c1 = NS * b * CB, NS * (b + 1) * CB
-        return lambda: op("v", lambda: V.tensor_tensor_scan(T.so[:, c0:c1], T.pe[:, c0:c1], T.po[:, c0:c1], 0.0,
-                                                           A.add, A.add),
-                          ["p%d" % b, "pd%d" % b, "pc0", "pc1", "pc2"], ["so%d" % b])
-
-    def resid(b):
-        return T.so[:, NS * b * CB + NS - 1:NS * (b + 1) * CB:NS]
-
-    def clip_x(b):
-        def run():
-            for i in range(DT):
-                ts(cs(T.px, b), resid(b), -2.0, A.max, ["so%d" % b], ["e%d" % b, "xq"] if i == DT - 1 else [], [X],
-                   s2=2.0, f2=A.min)()
-        return run
-
-    def clip_send(s, b):
-        def run():
-            ts(cs(T.es, b, s * C), resid(b), -2.0, A.max, ["so%d" % b], ["es"], s2=2.0, f2=A.min)()
-            dst = T.cores[(rank + 1 + b) % N]
-            eng = topo.engines(core, dst)[-8:]
-            rid, pid, _ = topo.addr(dst)
-            tok = wrote["es"]
-            wait("g", tok)
-            g.remote_dma(cs(T.land, b, s * C), cs(T.es, b, s * C), T.sem["arr%d" % s], T.sem.snt, pid, rid,
-                         sum(1 << e for e in eng))
-            del wrote["es"]
-        return run
-
-    def tmul(s, b):
-        n = TP // DT
-        dst, key, bk = (T.ts, "t%d" % b, [X]) if by_pe(s, b) else (T.wp, "wp%d" % b, [X, 2 * b, 2 * b + 1])
-        return spread([tt(taps(dst, b, k, n), taps(T.xs, b, k, n), cs(T.px, b), A.mult, ["x%d" % b, "e%d" % b],
-                          [key] if k in (0, n - 1) else [], bk) for k in range(n)])
-
-    def preload(s, b):
-        if by_pe(s, b):
-            for n in range(4):
-                o = 256 * (4 * b + n)
-                mm(T.wp[:, o:o + 256], T.idf[:], T.ws[:, 2 * o:2 * o + 256], n % 2 == 0, False, ["ws%d" % b, "idf"],
-                   ["wp%d" % b], wbank(b))
+    def send(s, b):
+        sh = 16 * (1 + s)
+        mm(yR, T.jj[:, 128 - sh:256 - sh], cs(T.es, b), True, True, ["es%d" % b, "jj"], ["yR"], Y, 256)
+        act(cs(T.eo, b, s * C), yR, F.Copy, ["yR"], ["eo%d_%d" % (s, b)], [Y])
+        dst = T.cores[(rank + 1 + b) % N]
+        eng = topo.engines(core, dst)[-8:]
+        rid, pid, _ = topo.addr(dst)
+        op("g", lambda: g.remote_dma(cs(T.land, b, s * C), cs(T.eo, b, s * C), T.sem["arr%d" % s], T.sem.snt, pid, rid,
+                                     sum(1 << e for e in eng)),
+           DREM, ["eo%d_%d" % (s, b)], ["arr%d" % s], kind="r", part="arr", hold=600)
 
     def update(s, b):
-        if by_pe(s, b):
+        m, last = MODE[s][b], s == S - 1
+        if m == "D" and s == 0:
             for j in wbank(b):
-                mm(T.wp[:, 512 * j:512 * (j + 1)], T.n64[:], T.ts[:, 512 * j:512 * (j + 1)], False, True,
-                   ["t%d" % b, "n64"], ["wp%d" % b], wbank(b))
-        else:
-            act(blk(T.wp, b), blk(T.wp, b), F.Copy, ["wp%d" % b], ["wp%d" % b], wbank(b), scale=1.0 / 64)
-
-    def summ(s, b):
-        if by_pe(s, b):
-            return [lambda: None] * 4
-        if s == 0:
-            calls = [tt(blk(T.wp, b, k), cs(T.wb, b, k * C), blk(T.wp, b, k), A.add, ["wp%d" % b] if k == 0 else [],
-                        ["wa%d" % b] if k == TP - 1 else [], wbank(b)) for k in range(TP)]
-            return [lambda j=j: [f() for f in calls[4 * j:4 * j + 4]] for j in range(4)]
-        out = []
-        for n in range(4):
-            o = 256 * (4 * b + n)
-            p_, w_ = T.wp[:, o:o + 256], T.ws[:, 2 * o:2 * o + 256]
-            out.append(tt(p_ if s == S - 1 else w_, w_, p_, A.add, ["wp%d" % b, "ws%d" % b] if n == 0 else [],
-                          ["wa%d" % b] if n == 3 else [], wbank(b)))
-        return out
-
-    def scans(b):
-        out = []
-        for nm, msk, o, f0, f1 in (("mx", T.m01, T.mx, A.mult, A.max), ("mn", T.mbg, T.mn, A.max, A.min)):
-            for h in range(2):
-                def run(nm=nm, msk=msk, o=o, f0=f0, f1=f1, h=h):
-                    c0 = 512 * h
-                    op("v", lambda: V.tensor_tensor_scan(o[:, c0:c0 + 512], msk[:, c0:c0 + 512],
-                                                         T.wp[:, b * BW + c0:b * BW + c0 + 512], 0.0, f0, f1),
-                       ["wp%d" % b, "m01", "mbg"], [nm + str(h)], wbank(b))
-                out.append(run)
-        return out
-
-    def votes(b, strong):
-        nm, ext, eq, o, bk = ("mx", T.mx, T.eqs, xV, X) if strong else ("mn", T.mn, T.eqw, yZ, Y)
-        out = []
-        n, w = TP // DE, DE * CB
-        per = n if strong else max(1, 4 // DE)
-        for k in range(n):
-            def run(k=k):
-                key = "eq%s%d_%d" % (nm, b, k)
-                src, skey = ext[:, TP - 1:BW:TP], [nm + "0", nm + "1"]
-                if DE > 1:
-                    for i in range(DE if k == 0 else 0):
-                        cp(T.dup[:, i:w:DE], src, skey, ["dup"] if i == DE - 1 else [])()
-                    src, skey = T.dup[:, 0:w], ["dup"]
-                tt(eq[:, b * BW + k * w:b * BW + (k + 1) * w], taps(T.wp, b, k, n), src, A.is_equal, ["wp%d" % b] + skey, [key],
-                   wbank(b))()
-                if k % per == per - 1:
-                    for j in range(k - per + 1, k + 1):
-                        for i in range(DE):
-                            mm(o, sel(j + n * i, T.s1, T.s0), eq[:, b * BW + j * w + i:b * BW + (j + 1) * w:DE],
-                               j == 0 and i == 0, j == n - 1 and i == DE - 1, [key, "s0", "s1"], ["xV" if strong else "yZ"], [bk])
-                if k == n - 1 and strong:
-                    act(T.us[:], xV, F.Exp, ["xV", "cBS"], ["us"], [X], bias=col(BS), scale=11.36)
-                if k == n - 1 and not strong:
-                    act(T.uw[:], yZ, F.Exp, ["yZ", "cBW"], ["uw"], [Y], bias=col(BWK), scale=8.8)
-                    mm(yZ, T.boc[:], T.uw[:], True, True, ["uw", "boc"], ["yZ"], [Y])
-            out.append(run)
-        return spread(out)
-
-    def strong_side(b):
-        def run():
-            tt(T.us2[:], T.us[:], cs(T.sgn, b), A.mult, ["us", "sgn"], ["us2"])()
-            mm(xZ, T.bob[:], T.us2[:], True, True, ["us2", "bob"], ["xZ"], [X])
-        return run
-
-    thr = ts(T.thr[:], xZ, 0.0, A.is_le, ["xZ"], ["thr"], [X], s2=-1e29, f2=A.mult)
-
-    def chain(s, b):
-        old, new = "a%d_%d" % (s % 2, b), "a%d_%d" % ((s + 1) % 2, b)
-        ao, an = cs(T.aa, b, (s % 2) * C), cs(T.aa, b, ((s + 1) % 2) * C)
-        last = s == S - 1
-        yS = T.px[:, 320:324]
-        slb = T.sl[:, 4 * b:4 * b + 4]
-
-        def slots():
-            even, odd, base = (T.k1s, T.k0s, T.ck[:, 4 * b:4 * b + 4]) if last else (T.w1s, T.w0s, T.cn[:])
-            mm(yS, T.idb[:], base, True, False, ["idb", "cn", "ck"], ["xS"], [X])
-            for r in range(16):
-                mm(yS, sel(r, even, odd), T.hit[:, r:CB:16], False, r == 15, ["hit", "w0s", "w1s", "k0s", "k1s"], ["xS"], [X])
-        hit = tt(T.hit[:], yZ, T.thr[:], A.is_lt, ["yZ", "thr"], ["hit"], [Y])
-
-        def first():
-            hit()
-            slots()
-        hd = tt(yH, T.hit[:], cs(T.py, b), A.mult, ["hit", "yD"], ["yH"], [Y])
-        anew = tt(an, yH, ao, A.add, ["yH", old], [new], [Y])
+                act(store(j), half(T.wp, j), F.Copy, wkey(j), ["ws%d" % j], [j], scale=-1.0, n=512)
+        if m == "P":
+            for j in wbank(b):
+                mm(half(T.wp, j), idf, store(j), True, False, ["ws%d" % j, "jj"], wkey(j), j, 2048)
+        for k in range(TP):
+            tt(blk(T.tr, b, k), blk(T.xs, b, k), cs(T.px, b), A.mult, ["x%d" % b, "e%d" % b], per("t", b), [X], part=s)
+        if m == "P":
+            for j in wbank(b):
+                mm(half(T.wp, j), T.i64[:], half(T.tr, j), False, True, ["t%d" % j, "mats"], wkey(j), j, 2048)
+                act(store(j), half(T.wp, j), F.Copy, wkey(j), ["ws%d" % j], [j], n=512)
+                act(half(T.wp, j), half(T.wp, j), F.Abs, [], wkey(j), [j], n=512)
+            return
+        for j in wbank(b):
+            act(half(T.tr, j), half(T.tr, j), F.Copy, [], ["t%d" % j], scale=1.0 / 64, n=512)
         if last:
-            return [first, ts(slb, yS, col(PM), A.add, ["xS", "cPM"], ["sl%d" % b], [X]), hd,
-                    cp(T.wk[:, 0:17 * C].indirect(slb), T.pqt[:], ["sl%d" % b, "pqt"], ["wk0", "wk1", "wk2"]), anew]
+            for k in range(TP):
+                tt(cs(T.wk, b, k * C), blk(T.tr, b, k), blk(T.wp, b, k), A.subtract, per("t", b) + wkeys(b, k // 8),
+                   ["wk%d_%d" % (b, k // 8)], wbank(b), part="sum")
+            for k in range(TP):
+                act(blk(T.wp, b, k), cs(T.wk, b, k * C), F.Abs, ["wk%d_%d" % (b, k // 8)], wkeys(b, k // 8), wbank(b), part="abs")
+            return
+        if m == "D":
+            dma("g", T.ws[:, 2 * BW * b:2 * BW * b + BW], blk(T.tr, b), DADD, per("t", b), per("ws", b), accum_op=A.add)
+        for j in wbank(b):
+            if m == "V":
+                for h in range(2):
+                    o = slice(256 * h, 256 * (h + 1))
+                    tt(store(j)[:, o], half(T.tr, j)[:, o], half(T.wp, j)[:, o], A.subtract, ["t%d" % j] + wkey(j),
+                       ["ws%d" % j], [j], n=256, part=s)
+            act(half(T.wp, j), store(j), F.Abs, ["ws%d" % j], wkey(j), [j], n=512)
 
-        vsub = tt(cs(T.vi, b), cs(T.py, b, 192), an, A.subtract, ["yN", new], ["vi%d" % b], [Y])
-        return [first, hd, anew, vsub,
-                ts(cs(T.vm, b), cs(T.vi, b), WN - 1, A.bitwise_and, ["vi%d" % b], ["vm%d" % b]),
-                cp(cs(T.idx, b), cs(T.vm, b), ["vm%d" % b], ["idx%d" % b]),
-                ts(slb, yS, col(M16), A.add, ["xS", "cM16"], ["sl%d" % b], [X]),
-                cp(T.ws[:, 2048 * b:2048 * (b + 1)].indirect(slb), T.pqt[:], ["sl%d" % b, "pqt"], ["ws%d" % b])]
+    def extreme(s, j, strong):
+        nm, ext, msk, f = ("mx", T.mx, T.m01, (A.mult, A.max)) if strong else ("mn", T.mn, T.mbg, (A.max, A.min))
+        for o in range(512 * j, 512 * (j + 1), SCH):
+            scan(ext[:, o:o + SCH], msk[:, 0:SCH], T.wp[:, o:o + SCH], f[0], f[1], wkey(j) + ["m01", "mbg"],
+                 ["%s%d" % (nm, j)], [j], SCH, part=s)
+
+    def votes(s, b, strong):
+        nm, ext, eq, o, bk = ("mx", T.mx, T.eqs, xV, X) if strong else ("mn", T.mn, T.eqw, yV, Y)
+        for k in range(TP):
+            tt(eq[:, b * BW + k * CB:b * BW + (k + 1) * CB], blk(T.wp, b, k), blk(ext, b, TP - 1), A.is_equal,
+               wkeys(b, k // 8) + per(nm, b), ["eq%s%d_%d" % (nm, b, k // 4)], wbank(b), part=s)
+        for k in range(TP):
+            mm(o, sel(k, T.s1, T.s0), eq[:, b * BW + k * CB:b * BW + (k + 1) * CB], k == 0, k == TP - 1,
+               ["eq%s%d_%d" % (nm, b, k // 4), "s0", "s1"], ["xV" if strong else "yV"], bk)
+
+    def choose(s, b):
+        old, new = "a%d_%d" % (s, b), "a%d_%d" % (s + 1, b)
+        last = s == S - 1
+        ao, an = cs(T.aa, b, s * C), cs(T.af, b) if last else cs(T.aa, b, (s + 1) * C)
+        slb = T.idx[:, LW * b + CB:LW * (b + 1)]
+        for j, strong in ((2 * b, True), (2 * b + 1, True), (2 * b, False)):
+            extreme(s, j, strong)
+        votes(s, b, True)
+        act(xV, xV, F.Exp, ["cBS"], ["xV"], [X], bias=col(BS), scale=11.36)
+        tt(T.us2[:], xV, cs(T.sgn, b), A.mult, ["xV", "sgn"], ["us2"], [X])
+        mm(xV, T.bob[:], T.us2[:], True, True, ["us2", "mats"], ["xV"], X)
+        act(T.sx[:], xV, F.Sign, ["xV"], ["sx"], [X])
+        extreme(s, 2 * b + 1, False)
+        votes(s, b, False)
+        act(T.uw[:], yV, F.Exp, ["yV", "cBW"], ["uw"], [Y], bias=col(BWK), scale=8.8)
+        mm(xZ, T.nhu[:], T.neg[:], True, False, ["mats", "neg"], ["xZ"], X)
+        mm(xZ, T.nhu[:], T.sx[:], False, False, ["mats", "sx"], ["xZ"], X)
+        mm(xZ, T.boc[:], T.uw[:], False, True, ["uw", "boc"], ["xZ"], X)
+        ts(T.hit[:], xZ, 0.0, A.is_lt, ["xZ"], ["hit"], [X])
+        mm(yS, T.nih[:], T.ck[:, 4 * b:4 * b + 4] if last else T.cn[:], True, False, ["nih", "ck", "cn"], ["yS"], Y)
+        for r in range(16):
+            mm(yS, sel(r, T.k1s, T.k0s) if last else sel(r, T.w1s, T.w0s), T.hit[:, r:CB:16], False, r == 15,
+               ["hit", "wsel"], ["yS"], Y)
+        tt(xZ, T.hit[:], cs(T.px, b, 192), A.mult, ["hit", "xD"], ["xZ"], [X])
+        tt(an, xZ, ao, A.add, ["xZ", old], [new], [X])
+        if last:
+            ts(slb, yS, col(PM), A.add, ["yS", "cPM"], ["idx%d" % b], [Y])
+            wk = ["wk%d_%d" % (i, h) for i in range(NB) for h in range(2)]
+            cp(T.wk[:, 0:17 * C].indirect(slb), T.pqt[:], ["idx%d" % b, "pqt"], wk, n=60 + CB * SC / CY)
+            return
+        for wrap in (False, True):
+            mm(yE, T.boh[:], cs(T.ex, b, (s + 1) * C), True, False, ["ex", "boh"], ["yE"], Y)
+            mm(yE, T.nih[:], an, False, not wrap, [new, "nih"], ["yE"], Y)
+            if wrap:
+                mm(yE, T.n2k[:], T.neg[:], False, False, ["mats", "neg"], ["yE"], Y)
+                mm(yE, T.n2k[:], T.sm[:], False, True, ["sm", "mats"], ["yE"], Y)
+            else:
+                act(T.sm[:], yE, F.Sign, ["yE"], ["sm"], [Y], bias=0.5)
+        cp(T.idx[:, LW * b:LW * (b + 1)], yL, ["yE", "yS"], ["idx%d" % b], [Y], n=68)
+        cp(T.ws[:, 2 * BW * b:2 * BW * (b + 1)].indirect(slb), T.pqt[:], ["idx%d" % b, "pqt"], per("ws", b), n=60 + CB * SC / CY)
 
     def akeys(i):
         return ["a%d_%d" % (i, b) for b in range(NB)]
 
-    def queue_step(s):
-        j = s % 2
-        mm(yN, T.idf[:], T.qq[:, j * C:(j + 1) * C], True, False, ["q%d" % j, "idf"], ["yN"], [Y])
-        mm(yN, T.bof[:], T.aa[:, j * C:(j + 1) * C], False, False, akeys(j) + ["bof"], ["yN"], [Y])
-        mm(yN, T.nbo[:], T.aa[:, (1 - j) * C:(2 - j) * C], False, True, akeys(1 - j) + ["nbo"], ["yN"], [Y])
+    def delays(s):
+        return T.aa[:, s * C:(s + 1) * C] if s < S else T.af[:]
 
-    def books_pe(s):
-        j = s % 2
-        mm(yD, T.idf[:], T.qq[:, j * C:(j + 1) * C], True, False, ["q%d" % j, "idf"], ["yD"], [Y])
-        mm(yD, T.nid[:], T.aa[:, j * C:(j + 1) * C], False, True, akeys(j) + ["nid"], ["yD"], [Y])
-        if s > 0:
-            queue_step(s - 1)
+    def head(s, o, key, bk, more=()):
+        terms = [(T.boh[:], T.ex[:, (S + s % 2) * C:(S + s % 2 + 1) * C], ["ex"], 192)]
+        for t in range(s % 2, s, 2):
+            terms += [(T.boh[:], delays(t), akeys(t), 192),
+                      (T.nbh[:], delays(t + 1), akeys(t + 1), 192) if t + 1 < S else (T.nbo[:], delays(S), akeys(S), 768)]
+        terms += more
+        for i, (l, r, keys, n) in enumerate(terms):
+            mm(o, l, r, i == 0, i == len(terms) - 1, keys + ["boh", "nbh", "mats", "nih"], [key], bk, n)
 
-    def books_act(s):
-        act(T.ab1[:], yD, F.Abs, ["yD"], ["ab1"], [Y])
-        if s > 0:
-            j = (s - 1) % 2
-            act(T.qq[:, j * C:(j + 1) * C], yN, F.Copy, ["yN"], ["q%d" % j], [Y])
-        act(T.ab2[:], T.ab1[:], F.Abs, ["ab1"], ["ab2"], bias=-2048.0)
-        act(T.sgn[:], T.ab2[:], F.Sign, ["ab2"], ["sgn"], bias=-1023.5)
+    def reach(s):
+        head(s, xD, "xD", X, [(T.nih[:], delays(s), akeys(s), 192)])
+        act(T.ab1[:], xD, F.Abs, ["xD"], ["ab1"], [X], n=192)
+        act(T.ab2[:], T.ab1[:], F.Abs, ["ab1"], ["ab2"], bias=-2048.0, n=192)
+        act(T.sgn[:], T.ab2[:], F.Sign, ["ab2"], ["sgn"], bias=-1023.5, n=192)
 
-    def times(s):
-        mm(yN, T.bof[:], T.ex[:, s * C:(s + 1) * C], True, True, EX + ["bof"], ["yN"], [Y])
-
-    def turn(s):
-        sh = 16 * (1 + s)
-        last = s == S - 1
-        dst = T.yr if last else T.rot
-        src = T.land[:, s * C:(s + 1) * C]
-        SY.wait_ge(T.sem["arr%d" % s], 8 * NB)
-        op("s", lambda: SY.dma_start(dst[sh:128, :], src[0:128 - sh, :]), (), ["rot0"], dma=True)
-        op("s", lambda: SY.dma_start(dst[0:sh, :], src[128 - sh:128, :]), (), ["rot1"], dma=True)
+    def landed(s, q, call):
+        def run():
+            q.wait_ge(T.sem["arr%d" % s], 8 * NB)
+            return call()
+        return run
 
     def put(s):
-        return cp(T.rr[:, 0:WN].indirect(T.ntu[:, 12 * s:12 * s + 12]), T.rot[:], ["rot0", "rot1", "ntu"], ["rr"])
-
-    def weave(main, extra, first, every):
-        extra = list(extra)
-        for i, f in enumerate(main):
-            f()
-            if extra and i >= first and (i - first) % every == 0:
-                extra.pop(0)()
-        for f in extra:
-            f()
-
-    def place(main, at):
-        for i, f in enumerate(main):
-            f()
-            for h in at.get(i, ()):
-                h()
-
-    def run(calls):
-        place(calls, {})
-
-    gather(0, 0)
-    gather(0, 1)
-    dslot(0)
-    gather(0, 2)
-    pend = []
-    for s in range(S):
-        last = s == S - 1
-        pa, pb, pc, ta, tb, tc = prod(0), prod(1), prod(2), tmul(s, 0), tmul(s, 1), tmul(s, 2)
-        sa, sb_, sc_ = summ(s, 0), summ(s, 1), summ(s, 2)
-        if s == 0:
-            early = 8 if DP == 1 else 0
-            copy_in(0, 0, on_v=range(0, 8))
-            place(pa[0:early], {})
-            copy_in(0, 0, on_v=range(8, 16))
-            copy_in(0, 1)
-            copy_in(0, 2)
-            books_pe(0)
-            lc = late_consts()
-            run(pa[early:] + lc[0:3] + [scan_y(0)] + lc[3:5] + [clip_x(0), clip_send(s, 0)])
-            place(pb, {i: [f] for i, f in enumerate(lc[5:])})
-            run(ta[0:4])
+        src = T.land[:, s * C:(s + 1) * C]
+        if s == S - 1:
+            op("s", landed(s, SY, lambda: SY.dma_start(T.yr[:], src)), 2500, ["arr%d" % s], (), kind="d", hold=60)
         else:
-            copy_in(s, 1)
-            first, hd, an, vs_, msk, idx, sl, rs = pend
-            run(pa[0:6] + [thr] + pa[6:] + [first, scan_y(0), hd] + pb[0:3] + [clip_x(0), an, clip_send(s, 0)] + pb[3:6]
-                + [vs_, sl] + pb[6:9] + [lambda: books_pe(s), msk, rs, pb[9], idx, lambda: gather(s, 2)] + pb[10:] + ta[0:4])
-        run([scan_y(1)] + ta[4:12] + [clip_x(1), clip_send(s, 1)] + ta[12:16])
-        if s > 0:
-            copy_in(s, 2)
-        update(s, 0)
-        run(tb)
-        update(s, 1)
-        books_act(s)
-        if not last:
-            times(s + 1)
-        run(pc + [sa[0], scan_y(2), sa[1], clip_x(2), clip_send(s, 2), sa[2], sa[3]])
-        turn(s)
-        copy_out(s, 0)
-        size(s, 0)
-        run(tc)
-        update(s, 2)
-        run(sb_)
-        copy_out(s, 1)
-        size(s, 1)
-        pend = []
+            op("v", landed(s, V, lambda: V.tensor_copy(T.rr[:, 0:WN].indirect(T.ntu[:, 12 * s:12 * s + 12]), src)),
+               50 + C * SC, ["ntu", "arr%d" % s], ["rr"])
+
+    for b in range(NB):
+        fetch(0, b)
+    for s in range(S):
         for b in range(NB):
-            sc, vs, vw = scans(b), votes(b, True), votes(b, False)
+            residual(s, b)
+            if s == 0 and b == 0:
+                constants()
+            send(s, b)
+            update(s, b)
+        reach(s)
+        if s == S - 1:
+            head(S, yT, "yT", Y)
+            tt(T.qm[:, 0:C], yT, T.dm[:], A.mult, ["yT", "dmr"], ["qm0"], [Y], n=192)
+        for b in range(NB):
+            choose(s, b)
             if b == 0:
-                run(sc[0:3] + vs + sc_[0:2] + sc[3:4] + sc_[2:4])
-            else:
-                if b == 1:
-                    copy_out(s, 2)
-                    size(s, 2)
-                if last:
-                    first, sl, hd, rs, an = pend
-                    run([sc[0], thr, sc[1], sc[2], first] + vs[0:4] + [hd] + vs[4:14] + [an, sl] + vs[14:16] + [sc[3], rs])
-                else:
-                    first, hd, an, vs_, msk, idx, sl, rs = pend
-                    if b == 1:
-                        dslot(s + 1)
-                    else:
-                        copy_in(s + 1, 0)
-                    run([sc[0], thr, sc[1], sc[2], first] + vs[0:4] + [hd] + vs[4:8] + [an] + vs[8:12] + [vs_, sl] + vs[12:16]
-                        + [msk, rs, sc[3], idx] + ([put(s)] if b == 1 else []))
-                    gather(s + 1, b - 1)
-            place(vw, {ST_AT: [strong_side(b)]})
-            pend = chain(s, b)
-    thr()
+                put(s)
+            if s < S - 1:
+                fetch(s + 1, b)
+        if s == 0:
+            last_constants()
 
-    for f in pend:
-        f()
-    op("s", lambda: SY.dma_start(T.yw[:], T.wk[:, 0:3072]), ["wk0", "wk1", "wk2", "wkall"], (), dma=True)
-    fin = S % 2
-    queue_step(S - 1)
-    cp(T.tin[:], T.aa[:, fin * C:(fin + 1) * C].indirect(T.l3[:, 0:24]), akeys(fin) + ["l3"], ["tin"])()
-    tt(T.qm[:, 0:C], T.qq[:, fin * C:(fin + 1) * C], T.dm[:], A.mult, ["q%d" % fin, "dmr"], ["qm0"])()
-    op("v", lambda: V.transpose(T.tout[:], T.tin[:]), ["tin"], ["tout"])
-    tt(T.qm[:, C:2 * C], yN, T.dm[:], A.mult, ["yN", "dmr"], ["qm1"], [Y])()
-    cp(T.ydo[:], T.tout[:, 0:384].indirect(T.l4[:, 0:12]), ["tout", "l4"], ["ydo"])()
-    op("v", lambda: V.tensor_tensor_scan(T.qs[:], T.m01[:, 0:2 * C], T.qm[:], 0.0, A.mult, A.add), ["qm0", "qm1", "m01"], ["qs"])
-    op("a", lambda: ACT.dma_start(T.yd[:], T.ydo[:]), ["ydo"], (), dma=True)
-    cp(T.yqo[:], T.qs[:, 15:2 * C:16], ["qs"], ["yqo"])()
-    op("a", lambda: ACT.dma_start(T.yq[:], T.yqo[:]), ["yqo"], (), dma=True)
+    dma("s", T.yw[:], T.wk[:, 0:3072], 6000, ["wk%d_%d" % (i, h) for i in range(NB) for h in range(2)], ())
+    head(S + 1, yT, "yT", Y)
+    cp(T.tin[:], T.af[:, 0:C].indirect(T.l3[:, 0:24]), akeys(S) + ["l3"], ["tin"], n=60 + 384 * GA / CY)
+    op("v", lambda: V.transpose(T.tout[:], T.tin[:]), vns(384), ["tin"], ["tout"])
+    ts(T.ydo[:], T.tout[:, 0:384].indirect(T.l4[:, 0:12]), OFF, A.add, ["tout", "l4"], ["ydo"], n=60 + 192 * GA / CY)
+    dma("a", T.yd[:], T.ydo[:], 2500, ["ydo"], ())
+    tt(T.qm[:, C:2 * C], yT, T.dm[:], A.mult, ["yT", "dmr"], ["qm1"], [Y], n=192)
+    scan(T.qs[:], T.m01[:, 0:2 * C], T.qm[:], A.mult, A.add, ["qm0", "qm1", "m01"], ["qs"], (), 384)
+    ts(T.yqo[:], T.qs[:, 15:2 * C:16], OFF, A.add, ["qs"], ["yqo"])
+    dma("a", T.yq[:], T.yqo[:], 2500, ["yqo"], ())
+
+    Q = {"v": V, "a": ACT, "p": PE, "g": g, "s": SY}
+    cnt, seen, tok, bank, ndma = {e: 0 for e in "vapg"}, {e: {} for e in Q}, {}, {}, 0
+    if not ORDER:
+        ORDER.extend(issue_order(calls))
+    for i in ORDER:
+        c = calls[i]
+        e, need = c["e"], {}
+        for d in c["deps"] + [bank[b] for b in c["B"] if b in bank and calls[bank[b]]["e"] != e]:
+            if d in tok and not (e == "p" and calls[d]["e"] == "p"):
+                need[tok[d][0]] = max(need.get(tok[d][0], 0), tok[d][1])
+        for name, n in need.items():
+            if seen[e].get(name, 0) < n:
+                Q[e].wait_ge(T.sem[name], n)
+                seen[e][name] = n
+        ins = c["call"]()
+        if c["kind"] in "dl":
+            tok[i] = ("dm%d" % ndma, 16)
+            ndma += 1
+            ins.then_inc(T.sem[tok[i][0]], 16)
+        elif c["kind"] == "c":
+            cnt[e] += 1
+            tok[i] = ("c" + e, cnt[e])
+            ins.then_inc(T.sem["c" + e], 1)
+        for b in c["B"]:
+            bank[b] = i
     g.wait_ge(T.sem.snt, 8 * NB * S)
-    for e in ("v", "a", "p", "g"):
+    for e in "vapg":
         g.wait_ge(T.sem["c" + e], cnt[e])
-    for i in range(ndma[0]):
+    for i in range(ndma):
         g.wait_ge(T.sem["dm%d" % i], 16)
-
-
-ST_AT = 7

@@ -5,12 +5,13 @@ BW = TP * CB
 BIG = float(2 ** 40)
 HUGE = float(2 ** 96)
 OFF = 2048.0
-NS = 10
+HP, HT = 1, 1
+NS = 10 + 2 * HP
 LW = CB + 4
-MODE = ["VVD", "VVD", "VVD", "VVD", "VVV"]
+MODE = ["VVD", "DDD", "DDD", "DDD", "DDD"]
 GCH = 2
-CY, PC, WAKE, AF, GA, SC, DADD, DREM = 0.83, 0.6, 220, 70, 1.4, 3.0, 5500, 5000
-ROUNDS = 3
+CY, PC, WAKE, OWN, AF, GA, SC, DADD, DREM = 0.83, 0.6, 300, 170, 40, 1.4, 3.0, 4200, 4000
+ROUNDS = 120
 SCH, YCH = 256, 2
 ORDER = []
 f32, bf, f16, i32, u16 = "float32", "bfloat16", "float16", "int32", "uint16"
@@ -52,54 +53,70 @@ def issue_order(calls):
             after[d].append(i)
 
     def lag(i, j):
-        return calls[i]["ns"] + (0 if calls[i]["e"] == calls[j]["e"] == "p" else WAKE)
+        a, b = calls[i]["e"], calls[j]["e"]
+        return calls[i]["ns"] + (WAKE if a != b else 0 if a == "p" else OWN)
 
-    def clash(spans, a, b, sign):
+    need = [[(d, lag(d, i)) for d in calls[i]["deps"]] for i in range(n)]
+    feed = [[(j, lag(i, j)) for j in after[i]] for i in range(n)]
+
+    def below(spans, x):
         lo, hi = 0, len(spans)
         while lo < hi:
             m = (lo + hi) // 2
-            if spans[m][0] < b - 1e-6:
+            if spans[m][0] < x:
                 lo = m + 1
             else:
                 hi = m
-        hits = [s for s in spans[max(0, lo - 12):lo] if s[1] > a + 1e-6]
-        if not hits:
+        return lo
+
+    def clash(spans, a, b, sign):
+        k = below(spans, b - 1e-6)
+        if not k or spans[k - 1][1] <= a + 1e-6:
             return 0
-        return hits[-1][1] - a if sign > 0 else hits[0][0] - b
+        if sign > 0:
+            return spans[k - 1][1] - a
+        while k > 1 and spans[k - 2][1] > a + 1e-6:
+            k -= 1
+        return spans[k - 1][0] - b
 
     def place(order, sign):
-        t, spans = {}, {}
+        t, spans = [0.0] * n, {}
         for i in order:
             c = calls[i]
+            e, ns, hold = c["e"], c["ns"], c["hold"]
             if sign > 0:
-                x = max([t[d] + lag(d, i) for d in c["deps"]] + [0.0])
+                x = max([t[d] + w for d, w in need[i]] + [0.0])
             else:
-                x = min([t[j] - lag(i, j) for j in after[i]] + [-c["ns"]])
+                x = min([t[j] - w for j, w in feed[i]] + [-ns])
             moved = c["kind"] != "l"
             if not moved and sign > 0:
-                x = i * c["hold"]
+                x = i * hold
+            own = spans.setdefault(e, [])
+            banks = [spans[k, f] for k in c["B"] for f in "vap" if f != e and (k, f) in spans]
             while moved:
-                moved = clash(spans.get(c["e"], []), x, x + c["hold"], sign)
-                for k in c["B"]:
-                    for f in "vap":
-                        if not moved and f != c["e"]:
-                            moved = clash(spans.get((k, f), []), x - WAKE, x + c["ns"] + WAKE, sign)
+                moved = clash(own, x, x + hold, sign)
+                for other in banks:
+                    moved = moved or clash(other, x - WAKE, x + ns + WAKE, sign)
                 x += moved
             t[i] = x
-            for key, end in [(c["e"], x + c["hold"])] + [((k, c["e"]), x + c["ns"]) for k in c["B"]]:
-                spans.setdefault(key, []).append((x, end))
-                spans[key].sort()
+            for row, end in [(own, x + hold)] + [(spans.setdefault((k, e), []), x + ns) for k in c["B"]]:
+                row.insert(below(row, x), (x, end))
         return t
-    order, best = list(range(n)), None
-    for _ in range(ROUNDS):
-        t = place(order, 1)
-        order = sorted(range(n), key=lambda i: (t[i], i))
-        span = max(t[i] + calls[i]["ns"] for i in range(n))
-        if best is None or span < best[0]:
-            best = (span, order)
-        u = place(sorted(range(n), key=lambda i: (-t[i] - calls[i]["ns"], -i)), -1)
-        order = sorted(range(n), key=lambda i: (u[i], i))
-    return best[1]
+
+    def settle(rank):
+        t = place(sorted(range(n), key=lambda i: (rank[i], i)), 1)
+        t = place(sorted(range(n), key=lambda i: (-t[i] - calls[i]["ns"], -i)), -1)
+        t = place(sorted(range(n), key=lambda i: (t[i], i)), 1)
+        return max(t[i] + calls[i]["ns"] for i in range(n)), t
+    best, seed = settle(list(range(n))), 1
+    for r in range(ROUNDS):
+        rank = []
+        for i in range(n):
+            seed = (seed * 1103515245 + 12345) % 2 ** 31
+            x = best[1][i] + (seed / 2 ** 30 - 1) * WAKE * (1 + r % 2) / 2
+            rank.append(max([x] + [rank[d] + 1e-3 for d, _ in need[i]]))
+        best = min(best, settle(rank), key=lambda b: b[0])
+    return sorted(range(n), key=lambda i: (best[1][i], i))
 
 
 def rank_program(g, core, T, topo):
@@ -140,8 +157,8 @@ def rank_program(g, core, T, topo):
     def cp(o, a, R, W, B=(), n=64):
         op("v", lambda: V.tensor_copy(o, a), vns(n), R, W, B)
 
-    def ms(o, c, W, n=64):
-        op("v", lambda: V.memset(o, c), vns(n), (), W)
+    def ms(o, c, W, n=64, part=None):
+        op("v", lambda: V.memset(o, c), vns(n), (), W, part=part)
 
     def scan(o, a, b, f0, f1, R, W, B, n, part=None):
         op("v", lambda: V.tensor_tensor_scan(o, a, b, 0.0, f0, f1), vns(n), R, W, B, part=part)
@@ -177,6 +194,9 @@ def rank_program(g, core, T, topo):
     def half(t, j):
         return t[:, 512 * j:512 * (j + 1)]
 
+    def pair(t, j, k):
+        return t[:, 512 * j + k:512 * (j + 1):8]
+
     def store(j):
         return half(T.ws, j + 2 * (j // 2))
 
@@ -195,11 +215,11 @@ def rank_program(g, core, T, topo):
     dma("a", T.nq[:, 0:60], T.nt[:], 2200, (), ["nt"])
     dma("s", T.dli[:], T.dl[:], 2400, (), ["dli"])
     dma("a", T.nq[:, 60:84], T.qu[:], 2400, (), ["qu"])
-    dma("s", T.rb[:], T.r0[:], 5000, (), ["rb"])
-    dma("s", T.wb[:, 0:1536], T.w0[:, 0:1536], 6000, (), ["wb0"])
-    dma("s", T.wb[:, 1536:3072], T.w0[:, 1536:3072], 7000, (), ["wb1"])
-    dma("s", T.db[:, 0:C], T.d0[:, 0:C], 7200, (), ["db0"])
-    dma("s", T.db[:, C:960], T.d0[:, C:960], 7800, (), ["db1"])
+    dma("s", T.rb[:], T.r0[:], 6500, (), ["rb"])
+    dma("s", T.wb[:, 0:1536], T.w0[:, 0:1536], 8000, (), ["wb0"])
+    dma("s", T.wb[:, 1536:3072], T.w0[:, 1536:3072], 9400, (), ["wb1"])
+    dma("s", T.db[:, 0:C], T.d0[:, 0:C], 9700, (), ["db0"])
+    dma("s", T.db[:, C:960], T.d0[:, C:960], 10500, (), ["db1"])
 
     def io(o, pat, cm, W, n, small=True):
         if small:
@@ -212,7 +232,6 @@ def rank_program(g, core, T, topo):
     io(T.gb[:], [[16, 8], [0, 16]], 0, ["gb"], 128)
     io(T.jj[:], [[0, 2], [1, 128]], -1, ["jj"], 256)
     io(T.dm[:], [[0, 12], [1, 16]], 0, ["dmr"], 192)
-    dma("g", T.rr[:], T.r0[:], 8000, ["wb1"], ["rr"])
 
     PM, PG, G15, G16, P31, M12, M16, H16, BS, BWK, WSL, WK = range(12)
     ts(T.it[:, 0:1], T.ip[:, 0:1], 15, A.bitwise_and, ["ip"], ["it0"])
@@ -239,9 +258,9 @@ def rank_program(g, core, T, topo):
         tt(cs(T.vi, b), cs(T.py, b, 256), cs(T.aa, b), A.subtract, ["yT"] + A0, ["vi%d" % b], [Y])
         ts(cs(T.vm, b), cs(T.vi, b), WN - 1, A.bitwise_and, ["vi%d" % b], ["vm%d" % b])
         cp(T.idx[:, LW * b:LW * b + CB], cs(T.vm, b), ["vm%d" % b], ["idx%d" % b])
-    ms(T.pe[:, 0:NS * C:NS], BIG, ["pc0"], 192)
-    ms(T.po[:, 0:NS * C:NS], -BIG, ["pc1"], 192)
-    ms(T.po[:, NS - 1:NS * C:NS], 0.0, ["pc2"], 192)
+    for t_, j, v in ((T.pe, 0, BIG), (T.po, 0, -BIG), (T.po, NS - 1, 0.0)) + (
+            ((T.pe, 5, 0.0), (T.pe, 6, 0.0), (T.po, 5, 0.0), (T.po, 6, 0.0)) if HP else ()):
+        ms(t_[:, j:NS * C:NS], v, ["pc"], 192, "pc")
     ts(T.jj[:], T.jj[:], 0.0, A.is_equal, [], ["jj"], n=256)
 
     def constants():
@@ -294,11 +313,10 @@ def rank_program(g, core, T, topo):
 
     def fetch(s, b):
         win, key = (T.rb, "rb") if s == 0 else (T.rr, "rr")
-        n = CB // GCH
-        for i in range(GCH):
-            act(T.xs[:, b * BW + TP * n * i:b * BW + TP * n * (i + 1)],
-                win[:, 0:WN].indirect(T.idx[:, LW * b + n * i:LW * b + n * (i + 1)]), F.Copy,
-                [key, "idx%d" % b], ["x%d" % b], n=TP * n * GA / CY, part="x%d" % s)
+        for j in wbank(b):
+            o = LW * b + 32 * (j % 2)
+            act(half(T.xs, j), win[:, 0:WN].indirect(T.idx[:, o:o + 32]), F.Copy, [key, "idx%d" % b], ["x%d" % j],
+                n=512 * GA / CY)
         if s == 0:
             taps_in(b, T.nib[:], 0, True)
             taps_in(b, T.nib[:], 1, True)
@@ -310,15 +328,23 @@ def rank_program(g, core, T, topo):
 
     def residual(s, b):
         c0, c1 = NS * b * CB, NS * (b + 1) * CB
-        for k in range(TP):
-            tt((T.pe, T.po)[k % 2][:, c0 + 1 + k // 2:c1:NS], blk(T.wp, b, k), blk(T.xs, b, k), A.mult,
-               wkeys(b, k // 8) + ["x%d" % b], ["p%d" % b], wbank(b), part=s)
-        n = NS * CB // YCH
-        for o in range(c0, c1, n):
-            scan(T.so[:, o:o + n], T.pe[:, o:o + n], T.po[:, o:o + n], A.add, A.add, ["p%d" % b, "pd", "pc0", "pc1", "pc2"],
-                 ["so%d" % b], (), n, part=s)
+        n = NS * CB // 2
+        if HP and (s, b) != (0, 0):
+            for j in wbank(b):
+                for k in range(8):
+                    tt((T.pe, T.po)[k % 2][:, n * j + 1 + k // 2:n * (j + 1):NS // 2], pair(T.wp, j, k), pair(T.xs, j, k), A.mult,
+                       wkey(j) + ["x%d" % j], ["p%d" % j], [j], part=s)
+        else:
+            for k in range(TP):
+                tt((T.pe, T.po)[k % 2][:, c0 + 1 + k // 2 + (NS - 10) * (k // 8):c1:NS], blk(T.wp, b, k), blk(T.xs, b, k), A.mult,
+                   wkeys(b, k // 8) + per("x", b), per("p", b), wbank(b), part=s)
+        for j in wbank(b):
+            o = slice(n * j, n * (j + 1))
+            scan(T.so[:, o], T.pe[:, o], T.po[:, o], A.add, A.add, ["p%d" % j, "pd", "pc"], ["so%d" % b], (), n, part=s)
         src = T.so[:, c0 + NS - 1:c1:NS]
-        ts(cs(T.px, b), src, -2.0, A.max, ["so%d" % b], ["e%d" % b], [X], s2=2.0, f2=A.min)
+        for i in range(1 + HT):
+            ts(T.px[:, 128 * b + i:128 * (b + 1):2] if HT else cs(T.px, b), src, -2.0, A.max, ["so%d" % b], ["e%d" % b], [X],
+               s2=2.0, f2=A.min, part=s)
         ts(cs(T.es, b), src, -2.0, A.max, ["so%d" % b], ["es%d" % b], s2=2.0, f2=A.min)
 
     def send(s, b):
@@ -340,8 +366,11 @@ def rank_program(g, core, T, topo):
         if m == "P":
             for j in wbank(b):
                 mm(half(T.wp, j), idf, store(j), True, False, ["ws%d" % j, "jj"], wkey(j), j, 2048)
-        for k in range(TP):
-            tt(blk(T.tr, b, k), blk(T.xs, b, k), cs(T.px, b), A.mult, ["x%d" % b, "e%d" % b], per("t", b), [X], part=s)
+        for j in wbank(b) if HT else ():
+            for k in range(8):
+                tt(pair(T.tr, j, k), pair(T.xs, j, k), cs(T.px, j), A.mult, ["x%d" % j, "e%d" % b], ["t%d" % j], [X], part=s)
+        for k in range(0 if HT else TP):
+            tt(blk(T.tr, b, k), blk(T.xs, b, k), cs(T.px, b), A.mult, per("x", b) + ["e%d" % b], per("t", b), [X], part=s)
         if m == "P":
             for j in wbank(b):
                 mm(half(T.wp, j), T.i64[:], half(T.tr, j), False, True, ["t%d" % j, "mats"], wkey(j), j, 2048)
@@ -350,22 +379,18 @@ def rank_program(g, core, T, topo):
             return
         for j in wbank(b):
             act(half(T.tr, j), half(T.tr, j), F.Copy, [], ["t%d" % j], scale=1.0 / 64, n=512)
-        if last:
-            for k in range(TP):
-                tt(cs(T.wk, b, k * C), blk(T.tr, b, k), blk(T.wp, b, k), A.subtract, per("t", b) + wkeys(b, k // 8),
-                   ["wk%d_%d" % (b, k // 8)], wbank(b), part="sum")
-            for k in range(TP):
-                act(blk(T.wp, b, k), cs(T.wk, b, k * C), F.Abs, ["wk%d_%d" % (b, k // 8)], wkeys(b, k // 8), wbank(b), part="abs")
-            return
-        if m == "D":
-            dma("g", T.ws[:, 2 * BW * b:2 * BW * b + BW], blk(T.tr, b), DADD, per("t", b), per("ws", b), accum_op=A.add)
         for j in wbank(b):
-            if m == "V":
+            if m == "D":
+                dma("g", store(j), half(T.tr, j), DADD, ["t%d" % j], ["ws%d" % j], accum_op=A.add)
+            else:
                 for h in range(2):
                     o = slice(256 * h, 256 * (h + 1))
                     tt(store(j)[:, o], half(T.tr, j)[:, o], half(T.wp, j)[:, o], A.subtract, ["t%d" % j] + wkey(j),
                        ["ws%d" % j], [j], n=256, part=s)
             act(half(T.wp, j), store(j), F.Abs, ["ws%d" % j], wkey(j), [j], n=512)
+        for k in range(TP if last else 0):
+            act(cs(T.wk, b, k * C), T.ws[:, 2 * BW * b + k:2 * BW * b + BW:TP], F.Copy, per("ws", b),
+                ["wk%d_%d" % (b, k // 8)], part="out")
 
     def extreme(s, j, strong):
         nm, ext, msk, f = ("mx", T.mx, T.m01, (A.mult, A.max)) if strong else ("mn", T.mn, T.mbg, (A.max, A.min))
@@ -397,50 +422,59 @@ def rank_program(g, core, T, topo):
         extreme(s, 2 * b + 1, False)
         votes(s, b, False)
         act(T.uw[:], yV, F.Exp, ["yV", "cBW"], ["uw"], [Y], bias=col(BWK), scale=8.8)
-        mm(xZ, T.nhu[:], T.neg[:], True, False, ["mats", "neg"], ["xZ"], X)
-        mm(xZ, T.nhu[:], T.sx[:], False, False, ["mats", "sx"], ["xZ"], X)
-        mm(xZ, T.boc[:], T.uw[:], False, True, ["uw", "boc"], ["xZ"], X)
-        ts(T.hit[:], xZ, 0.0, A.is_lt, ["xZ"], ["hit"], [X])
-        mm(yS, T.nih[:], T.ck[:, 4 * b:4 * b + 4] if last else T.cn[:], True, False, ["nih", "ck", "cn"], ["yS"], Y)
+        j0, j1 = wbank(b)
+        k0, k1 = wkey(j0), wkey(j1)
+        c0, c1 = 512 * j0, 512 * j1
+        zz, dd = T.wp[:, c0:c0 + CB], T.wp[:, c0 + CB:c0 + 2 * CB]
+        ee, sl, both = T.wp[:, c1:c1 + CB], T.wp[:, c1 + CB:c1 + LW], T.wp[:, c1:c1 + LW]
+        head(s, dd, k0, j0, b, True)
+        mm(zz, T.nhu[:], T.neg[:], True, False, ["mats", "neg"], k0, j0)
+        mm(zz, T.nhu[:], T.sx[:], False, False, ["mats", "sx"], k0, j0)
+        mm(zz, T.boc[:], T.uw[:], False, True, ["uw", "boc"], k0, j0)
+        ts(T.hit[:], zz, 0.0, A.is_lt, k0, ["hit"], [j0])
+        mm(sl, T.nih[:], T.ck[:, 4 * b:4 * b + 4] if last else T.cn[:], True, False, ["nih", "ck", "cn"], k1, j1)
         for r in range(16):
-            mm(yS, sel(r, T.k1s, T.k0s) if last else sel(r, T.w1s, T.w0s), T.hit[:, r:CB:16], False, r == 15,
-               ["hit", "wsel"], ["yS"], Y)
-        tt(xZ, T.hit[:], cs(T.px, b, 192), A.mult, ["hit", "xD"], ["xZ"], [X])
-        tt(an, xZ, ao, A.add, ["xZ", old], [new], [X])
+            mm(sl, sel(r, T.k1s, T.k0s) if last else sel(r, T.w1s, T.w0s), T.hit[:, r:CB:16], False, r == 15,
+               ["hit", "wsel"], k1, j1)
+        tt(zz, T.hit[:], dd, A.mult, ["hit"], k0, [j0])
+        tt(an, zz, ao, A.add, k0 + [old], [new], [j0])
         if last:
-            ts(slb, yS, col(PM), A.add, ["yS", "cPM"], ["idx%d" % b], [Y])
+            ts(slb, sl, col(PM), A.add, k1 + ["cPM"], ["idx%d" % b], [j1])
             wk = ["wk%d_%d" % (i, h) for i in range(NB) for h in range(2)]
             cp(T.wk[:, 0:17 * C].indirect(slb), T.pqt[:], ["idx%d" % b, "pqt"], wk, n=60 + CB * SC / CY)
             return
         for wrap in (False, True):
-            mm(yE, T.boh[:], cs(T.ex, b, (s + 1) * C), True, False, ["ex", "boh"], ["yE"], Y)
-            mm(yE, T.nih[:], an, False, not wrap, [new, "nih"], ["yE"], Y)
+            mm(ee, T.boh[:], cs(T.ex, b, (s + 1) * C), True, False, ["ex", "boh"], k1, j1)
+            mm(ee, T.nih[:], an, False, not wrap, [new, "nih"], k1, j1)
             if wrap:
-                mm(yE, T.n2k[:], T.neg[:], False, False, ["mats", "neg"], ["yE"], Y)
-                mm(yE, T.n2k[:], T.sm[:], False, True, ["sm", "mats"], ["yE"], Y)
+                mm(ee, T.n2k[:], T.neg[:], False, False, ["mats", "neg"], k1, j1)
+                mm(ee, T.n2k[:], T.sm[:], False, True, ["sm", "mats"], k1, j1)
             else:
-                act(T.sm[:], yE, F.Sign, ["yE"], ["sm"], [Y], bias=0.5)
-        cp(T.idx[:, LW * b:LW * (b + 1)], yL, ["yE", "yS"], ["idx%d" % b], [Y], n=68)
+                act(T.sm[:], ee, F.Sign, k1, ["sm"], [j1], bias=0.5)
+        cp(T.idx[:, LW * b:LW * (b + 1)], both, k1, ["idx%d" % b], [j1], n=68)
         cp(T.ws[:, 2 * BW * b:2 * BW * (b + 1)].indirect(slb), T.pqt[:], ["idx%d" % b, "pqt"], per("ws", b), n=60 + CB * SC / CY)
 
-    def akeys(i):
-        return ["a%d_%d" % (i, b) for b in range(NB)]
+    def akeys(i, b=None):
+        return ["a%d_%d" % (i, j) for j in (range(NB) if b is None else (b,))]
 
-    def delays(s):
-        return T.aa[:, s * C:(s + 1) * C] if s < S else T.af[:]
+    def head(s, o, keys, bk, b=None, gap=False):
+        c0, n = (0, C) if b is None else (b * CB, CB)
 
-    def head(s, o, key, bk, more=()):
-        terms = [(T.boh[:], T.ex[:, (S + s % 2) * C:(S + s % 2 + 1) * C], ["ex"], 192)]
+        def delays(t):
+            return T.aa[:, t * C + c0:t * C + c0 + n] if t < S else T.af[:, c0:c0 + n]
+        q0 = (S + s % 2) * C + c0
+        terms = [(T.boh[:], T.ex[:, q0:q0 + n], ["ex"], n)]
         for t in range(s % 2, s, 2):
-            terms += [(T.boh[:], delays(t), akeys(t), 192),
-                      (T.nbh[:], delays(t + 1), akeys(t + 1), 192) if t + 1 < S else (T.nbo[:], delays(S), akeys(S), 768)]
-        terms += more
-        for i, (l, r, keys, n) in enumerate(terms):
-            mm(o, l, r, i == 0, i == len(terms) - 1, keys + ["boh", "nbh", "mats", "nih"], [key], bk, n)
+            terms += [(T.boh[:], delays(t), akeys(t, b), n),
+                      (T.nbh[:], delays(t + 1), akeys(t + 1, b), n) if t + 1 < S else (T.nbo[:], delays(S), akeys(S, b), 4 * n)]
+        if gap:
+            terms.append((T.nih[:], delays(s), akeys(s, b), n))
+        for i, (l, r, rk, m) in enumerate(terms):
+            mm(o, l, r, i == 0, i == len(terms) - 1, rk + ["boh", "nbh", "mats", "nih"], keys, bk, m)
 
     def reach(s):
-        head(s, xD, "xD", X, [(T.nih[:], delays(s), akeys(s), 192)])
-        act(T.ab1[:], xD, F.Abs, ["xD"], ["ab1"], [X], n=192)
+        head(s, yT, ["yT"], Y, gap=True)
+        act(T.ab1[:], yT, F.Abs, ["yT"], ["ab1"], [Y], n=192)
         act(T.ab2[:], T.ab1[:], F.Abs, ["ab1"], ["ab2"], bias=-2048.0, n=192)
         act(T.sgn[:], T.ab2[:], F.Sign, ["ab2"], ["sgn"], bias=-1023.5, n=192)
 
@@ -469,11 +503,13 @@ def rank_program(g, core, T, topo):
             update(s, b)
         reach(s)
         if s == S - 1:
-            head(S, yT, "yT", Y)
+            head(S, yT, ["yT"], Y)
             tt(T.qm[:, 0:C], yT, T.dm[:], A.mult, ["yT", "dmr"], ["qm0"], [Y], n=192)
         for b in range(NB):
             choose(s, b)
             if b == 0:
+                for j in range(8 if s == 0 else 0):
+                    act(half(T.rr, j), half(T.rb, j), F.Copy, ["rb"], ["rr"], n=512, part="wide")
                 put(s)
             if s < S - 1:
                 fetch(s + 1, b)
@@ -481,7 +517,7 @@ def rank_program(g, core, T, topo):
             last_constants()
 
     dma("s", T.yw[:], T.wk[:, 0:3072], 6000, ["wk%d_%d" % (i, h) for i in range(NB) for h in range(2)], ())
-    head(S + 1, yT, "yT", Y)
+    head(S + 1, yT, ["yT"], Y)
     cp(T.tin[:], T.af[:, 0:C].indirect(T.l3[:, 0:24]), akeys(S) + ["l3"], ["tin"], n=60 + 384 * GA / CY)
     op("v", lambda: V.transpose(T.tout[:], T.tin[:]), vns(384), ["tin"], ["tout"])
     ts(T.ydo[:], T.tout[:, 0:384].indirect(T.l4[:, 0:12]), OFF, A.add, ["tout", "l4"], ["ydo"], n=60 + 192 * GA / CY)

@@ -5,13 +5,14 @@ BW = TP * CB
 BIG = float(2 ** 40)
 HUGE = float(2 ** 96)
 OFF = 2048.0
-HP, HT = 1, 1
-NS = 10 + 2 * HP
+NS = (10, 12, 12)
+Y0 = (0, 10 * CB, 22 * CB, 34 * CB)
+K1 = 12
 LW = CB + 4
-MODE = ["VVD", "DDD", "DDD", "DDD", "DDD"]
+MODE = ["PVD", "DDD", "DDD", "DDD", "DDD"]
 GCH = 2
-CY, PC, WAKE, OWN, AF, GA, SC, DADD, DREM = 0.83, 0.6, 300, 170, 40, 1.4, 3.0, 4200, 4000
-ROUNDS = 120
+CY, PC, WAKE, OWN, AF, GA, SC, DADD, DREM = 0.83, 0.6, 310, 270, 40, 1.4, 3.0, 4200, 4000
+ROUNDS = 450
 SCH, YCH = 256, 2
 ORDER = []
 f32, bf, f16, i32, u16 = "float32", "bfloat16", "float16", "int32", "uint16"
@@ -25,7 +26,7 @@ SCRATCH = {
     "wp": ("psum", [128, 3072], f32), "px": ("psum", [128, 512], f32), "py": ("psum", [128, 512], f32),
     "wb": sb(3072, bf), "rb": sb(WN, bf), "db": sb(960, bf), "dli": sb(192, i32), "nq": sb(88, i32),
     "rr": sb(WN, f32), "ws": sb(6144, f32), "wk": sb(17 * C, f32), "xs": sb(3072, f32), "tr": sb(3072, f32),
-    "pe": sb(NS * C, f32), "po": sb(NS * C, f32), "so": sb(NS * C, f32),
+    "pe": sb(Y0[3], f32), "po": sb(Y0[3], f32), "so": sb(Y0[3], f32),
     "mx": sb(3072, f32), "mn": sb(3072, f32), "m01": sb(512, bf), "mbg": sb(512, bf),
     "eqs": sb(3072, bf), "eqw": sb(3072, bf),
     "es": sb(C, f32), "eo": sb(S * C, f32), "land": sb(S * C, f32),
@@ -33,7 +34,7 @@ SCRATCH = {
     "m16": sb(16, f32), "dm": sb(C, f32), "s0": sb(144, bf), "s1": sb(144, bf), "w0s": sb(144, f16), "w1s": sb(144, f16),
     "jj": sb(256, f32), "i64": sb(128, f32), "bof": sb(128, f32), "nbo": sb(128, f32),
     "bob": sb(128, bf), "boc": sb(128, bf), "idb": sb(128, bf), "nib": sb(128, bf), "nhu": sb(128, bf), "n2k": sb(128, bf),
-    "boh": sb(128, f16), "nbh": sb(128, f16), "nih": sb(128, f16), "cn": sb(4, f16), "neg": sb(CB, bf), "pqt": sb(CB, f32),
+    "boh": sb(128, f16), "nbh": sb(128, f16), "nih": sb(128, f16), "cn": sb(4, f16), "neg": sb(CB, bf), "pqt": sb(CB, f32), "idp": sb(128, bf),
     "l1": sb(24, u16), "l2": sb(12, u16), "l3": sb(24, u16), "l4": sb(12, u16), "cj": sb(12, f32), "kj": sb(12, i32),
     "tj": sb(12, f32), "ntu": sb(60, u16), "ex": sb(1344, f16), "tin": sb(384, f32), "tout": sb(384, f32),
     "aa": sb(S * C, f16), "af": sb(C, f32), "ab1": sb(C, f32), "ab2": sb(C, f32), "sgn": sb(C, bf),
@@ -59,18 +60,19 @@ def issue_order(calls):
     need = [[(d, lag(d, i)) for d in calls[i]["deps"]] for i in range(n)]
     feed = [[(j, lag(i, j)) for j in after[i]] for i in range(n)]
 
-    def below(spans, x):
-        lo, hi = 0, len(spans)
-        while lo < hi:
-            m = (lo + hi) // 2
-            if spans[m][0] < x:
-                lo = m + 1
-            else:
-                hi = m
-        return lo
+    def below(spans, x, sign):
+        if sign > 0:
+            k = len(spans)
+            while k and spans[k - 1][0] >= x:
+                k -= 1
+        else:
+            k, m = 0, len(spans)
+            while k < m and spans[k][0] < x:
+                k += 1
+        return k
 
     def clash(spans, a, b, sign):
-        k = below(spans, b - 1e-6)
+        k = below(spans, b - 1e-6, sign)
         if not k or spans[k - 1][1] <= a + 1e-6:
             return 0
         if sign > 0:
@@ -100,7 +102,7 @@ def issue_order(calls):
                 x += moved
             t[i] = x
             for row, end in [(own, x + hold)] + [(spans.setdefault((k, e), []), x + ns) for k in c["B"]]:
-                row.insert(below(row, x), (x, end))
+                row.insert(below(row, x, sign), (x, end))
         return t
 
     def settle(rank):
@@ -110,12 +112,15 @@ def issue_order(calls):
         return max(t[i] + calls[i]["ns"] for i in range(n)), t
     best, seed = settle(list(range(n))), 1
     for r in range(ROUNDS):
-        rank = []
+        rank, t0 = [], (r * 0.618 % 1) * best[0]
+        t1, size = t0 + WAKE * (10, 20, 40)[r % 3], WAKE * (0.5, 1.5, 3)[r // 3 % 3]
         for i in range(n):
-            seed = (seed * 1103515245 + 12345) % 2 ** 31
-            x = best[1][i] + (seed / 2 ** 30 - 1) * WAKE * (1 + r % 2) / 2
+            x = best[1][i]
+            if t0 < x < t1:
+                seed = (seed * 1103515245 + 12345) % 2 ** 31
+                x += (seed / 2 ** 30 - 1) * size
             rank.append(max([x] + [rank[d] + 1e-3 for d, _ in need[i]]))
-        best = min(best, settle(rank), key=lambda b: b[0])
+        best = min(settle(rank), best, key=lambda b: b[0])
     return sorted(range(n), key=lambda i: (best[1][i], i))
 
 
@@ -216,8 +221,8 @@ def rank_program(g, core, T, topo):
     dma("s", T.dli[:], T.dl[:], 2400, (), ["dli"])
     dma("a", T.nq[:, 60:84], T.qu[:], 2400, (), ["qu"])
     dma("s", T.rb[:], T.r0[:], 6500, (), ["rb"])
-    dma("s", T.wb[:, 0:1536], T.w0[:, 0:1536], 8000, (), ["wb0"])
-    dma("s", T.wb[:, 1536:3072], T.w0[:, 1536:3072], 9400, (), ["wb1"])
+    dma("s", T.wb[:, 0:K1 * C], T.w0[:, 0:K1 * C], 8700, (), ["wb0"])
+    dma("s", T.wb[:, K1 * C:3072], T.w0[:, K1 * C:3072], 9400, (), ["wb1"])
     dma("s", T.db[:, 0:C], T.d0[:, 0:C], 9700, (), ["db0"])
     dma("s", T.db[:, C:960], T.d0[:, C:960], 10500, (), ["db1"])
 
@@ -258,10 +263,12 @@ def rank_program(g, core, T, topo):
         tt(cs(T.vi, b), cs(T.py, b, 256), cs(T.aa, b), A.subtract, ["yT"] + A0, ["vi%d" % b], [Y])
         ts(cs(T.vm, b), cs(T.vi, b), WN - 1, A.bitwise_and, ["vi%d" % b], ["vm%d" % b])
         cp(T.idx[:, LW * b:LW * b + CB], cs(T.vm, b), ["vm%d" % b], ["idx%d" % b])
-    for t_, j, v in ((T.pe, 0, BIG), (T.po, 0, -BIG), (T.po, NS - 1, 0.0)) + (
-            ((T.pe, 5, 0.0), (T.pe, 6, 0.0), (T.po, 5, 0.0), (T.po, 6, 0.0)) if HP else ()):
-        ms(t_[:, j:NS * C:NS], v, ["pc"], 192, "pc")
+    for c0, c1, ns in ((0, Y0[1], 10), (Y0[1], Y0[3], 12)):
+        for t_, j, v in ((T.pe, 0, BIG), (T.po, 0, -BIG), (T.po, ns - 1, 0.0)) + (
+                ((T.pe, 5, 0.0), (T.pe, 6, 0.0), (T.po, 5, 0.0), (T.po, 6, 0.0)) if ns == 12 else ()):
+            ms(t_[:, c0 + j:c1:ns], v, ["pc"], (c1 - c0) // ns, "pc")
     ts(T.jj[:], T.jj[:], 0.0, A.is_equal, [], ["jj"], n=256)
+    ts(T.idp[:], T.nib[:], -1.0, A.mult, ["nib"], ["idp"])
 
     def constants():
         act(T.bof[:], T.gb[:], F.Copy, ["gb"], ["bof"], n=128)
@@ -284,7 +291,7 @@ def rank_program(g, core, T, topo):
         cp(T.ntu[:], T.nq[:, 0:60], ["nt"], ["ntu"])
         ms(T.pqt[:], 0.25, ["pqt"])
         ms(T.neg[:], -1.0, ["neg"])
-        for o, a, k, f in ((T.i64, idf, "jj", 1.0 / 64), (T.nbo, T.bof[:], "bof", -1.0), (T.bob, T.bof[:], "bof", 1.0),
+        for o, a, k, f in ((T.i64, idf, "jj", -1.0 / 64), (T.nbo, T.bof[:], "bof", -1.0), (T.bob, T.bof[:], "bof", 1.0),
                            (T.nhu, T.nib[:], "nib", HUGE), (T.n2k, T.nib[:], "nib", 2048.0), (T.idb, T.nib[:], "nib", 2.5)):
             act(o[:], a, F.Copy, [k], ["mats"], scale=f, n=128, part="mats")
         tt(T.boc[:], T.idb[:], T.bob[:], A.add, ["mats"], ["boc"], n=256)
@@ -305,47 +312,52 @@ def rank_program(g, core, T, topo):
         tt(T.tj[:], T.tj[:], T.cj[:], A.add, ["cj"], ["tj"])
         ts(T.l4[:], T.tj[:], 32.0, A.mult, ["tj", "cH"], ["l4"], s2=col(H16), f2=A.add)
 
-    def taps_in(b, l, h, stop):
+    def taps_in(b, l, h):
         for j in wbank(b):
-            for k in range(8 * h, 8 * h + 8):
+            for k in range(K1 * h, TP if h else K1):
                 mm(T.wp[:, 512 * j + k:512 * (j + 1):TP], l, T.wb[:, k * C + 32 * j:k * C + 32 * (j + 1)],
-                   k % 8 == 0, stop and k % 8 == 7, ["wb%d" % h, "nib"], wkey(j, h), j)
+                   k in (0, K1), k in (K1 - 1, TP - 1), ["wb%d" % h, "nib", "idp"], wkey(j, h), j)
 
     def fetch(s, b):
         win, key = (T.rb, "rb") if s == 0 else (T.rr, "rr")
         for j in wbank(b):
             o = LW * b + 32 * (j % 2)
             act(half(T.xs, j), win[:, 0:WN].indirect(T.idx[:, o:o + 32]), F.Copy, [key, "idx%d" % b], ["x%d" % j],
-                n=512 * GA / CY)
+                n=512 * GA / CY, scale=1.0 if s or b else -1.0)
         if s == 0:
-            taps_in(b, T.nib[:], 0, True)
-            taps_in(b, T.nib[:], 1, True)
+            for h in range(2 if b else 1):
+                taps_in(b, T.nib[:] if b else T.idp[:], h)
         else:
             for j in wbank(b):
                 act(half(T.wp, j), store(j), F.Copy, ["ws%d" % j], wkey(j), [j], scale=-1.0, n=512)
-        if b == 0:
-            act(T.pe[:, NS - 1:NS * C:NS], T.db[:, s * C:(s + 1) * C], F.Copy, ["db%d" % min(s, 1)], ["pd"], n=192)
+        if b < 2:
+            c0, c1 = (0, Y0[1]) if b == 0 else (Y0[1], Y0[3])
+            act(T.pe[:, c0 + NS[b] - 1:c1:NS[b]], T.db[:, s * C + b * CB:s * C + (1 + 2 * b) * CB], F.Copy,
+                ["db%d" % min(s, 1)], ["pd%d" % b], n=CB * (1 + b))
 
     def residual(s, b):
-        c0, c1 = NS * b * CB, NS * (b + 1) * CB
-        n = NS * CB // 2
-        if HP and (s, b) != (0, 0):
+        ns, c0, c1 = NS[b], Y0[b], Y0[b + 1]
+        n = ns * CB // 2
+        if ns == 12:
             for j in wbank(b):
+                o = c0 + n * (j % 2)
                 for k in range(8):
-                    tt((T.pe, T.po)[k % 2][:, n * j + 1 + k // 2:n * (j + 1):NS // 2], pair(T.wp, j, k), pair(T.xs, j, k), A.mult,
+                    tt((T.pe, T.po)[k % 2][:, o + 1 + k // 2:o + n:6], pair(T.wp, j, k), pair(T.xs, j, k), A.mult,
                        wkey(j) + ["x%d" % j], ["p%d" % j], [j], part=s)
-        else:
-            for k in range(TP):
-                tt((T.pe, T.po)[k % 2][:, c0 + 1 + k // 2 + (NS - 10) * (k // 8):c1:NS], blk(T.wp, b, k), blk(T.xs, b, k), A.mult,
-                   wkeys(b, k // 8) + per("x", b), per("p", b), wbank(b), part=s)
+        for k in range(TP if ns == 10 else 0):
+            o = (T.pe, T.po)[k % 2][:, c0 + 1 + k // 2:c1:ns]
+            if s or k < K1:
+                tt(o, blk(T.wp, b, k), blk(T.xs, b, k), A.mult, wkeys(b, k // K1) + per("x", b), per("p", b), wbank(b), part=s)
+            else:
+                tt(o, cs(T.wb, b, k * C), blk(T.xs, b, k), A.mult, ["wb1"] + per("x", b), per("p", b), n=128, part=s)
         for j in wbank(b):
-            o = slice(n * j, n * (j + 1))
-            scan(T.so[:, o], T.pe[:, o], T.po[:, o], A.add, A.add, ["p%d" % j, "pd", "pc"], ["so%d" % b], (), n, part=s)
-        src = T.so[:, c0 + NS - 1:c1:NS]
-        for i in range(1 + HT):
-            ts(T.px[:, 128 * b + i:128 * (b + 1):2] if HT else cs(T.px, b), src, -2.0, A.max, ["so%d" % b], ["e%d" % b], [X],
-               s2=2.0, f2=A.min, part=s)
-        ts(cs(T.es, b), src, -2.0, A.max, ["so%d" % b], ["es%d" % b], s2=2.0, f2=A.min)
+            o = c0 + n * (j % 2)
+            scan(T.so[:, o:o + n], T.pe[:, o:o + n], T.po[:, o:o + n], A.add, A.add, ["p%d" % j, "pd%d" % min(b, 1), "pc"],
+                 ["so%d" % j], (), n)
+            for i in range(2):
+                ts(T.px[:, CB * j + i:CB * (j + 1):2], T.so[:, o + ns - 1:o + n:ns], -2.0, A.max, ["so%d" % j], ["e%d" % j], [X],
+                   s2=2.0, f2=A.min, part=s)
+        ts(cs(T.es, b), T.so[:, c0 + ns - 1:c1:ns], -2.0, A.max, per("so", b), ["es%d" % b], s2=2.0, f2=A.min)
 
     def send(s, b):
         sh = 16 * (1 + s)
@@ -365,12 +377,12 @@ def rank_program(g, core, T, topo):
                 act(store(j), half(T.wp, j), F.Copy, wkey(j), ["ws%d" % j], [j], scale=-1.0, n=512)
         if m == "P":
             for j in wbank(b):
-                mm(half(T.wp, j), idf, store(j), True, False, ["ws%d" % j, "jj"], wkey(j), j, 2048)
-        for j in wbank(b) if HT else ():
+                for k in range(TP):
+                    mm(T.wp[:, 512 * j + k:512 * (j + 1):TP], T.idp[:], T.wb[:, k * C + 32 * j:k * C + 32 * (j + 1)],
+                       k == 0, False, ["wb0", "wb1", "idp"], wkey(j), j)
+        for j in wbank(b):
             for k in range(8):
-                tt(pair(T.tr, j, k), pair(T.xs, j, k), cs(T.px, j), A.mult, ["x%d" % j, "e%d" % b], ["t%d" % j], [X], part=s)
-        for k in range(0 if HT else TP):
-            tt(blk(T.tr, b, k), blk(T.xs, b, k), cs(T.px, b), A.mult, per("x", b) + ["e%d" % b], per("t", b), [X], part=s)
+                tt(pair(T.tr, j, k), pair(T.xs, j, k), cs(T.px, j), A.mult, ["x%d" % j, "e%d" % j], ["t%d" % j], [X], part=s)
         if m == "P":
             for j in wbank(b):
                 mm(half(T.wp, j), T.i64[:], half(T.tr, j), False, True, ["t%d" % j, "mats"], wkey(j), j, 2048)
@@ -402,10 +414,10 @@ def rank_program(g, core, T, topo):
         nm, ext, eq, o, bk = ("mx", T.mx, T.eqs, xV, X) if strong else ("mn", T.mn, T.eqw, yV, Y)
         for k in range(TP):
             tt(eq[:, b * BW + k * CB:b * BW + (k + 1) * CB], blk(T.wp, b, k), blk(ext, b, TP - 1), A.is_equal,
-               wkeys(b, k // 8) + per(nm, b), ["eq%s%d_%d" % (nm, b, k // 4)], wbank(b), part=s)
+               wkeys(b, k // 8) + per(nm, b), ["eq%s%d_%d" % (nm, b, k // 2)], wbank(b), part=s)
         for k in range(TP):
             mm(o, sel(k, T.s1, T.s0), eq[:, b * BW + k * CB:b * BW + (k + 1) * CB], k == 0, k == TP - 1,
-               ["eq%s%d_%d" % (nm, b, k // 4), "s0", "s1"], ["xV" if strong else "yV"], bk)
+               ["eq%s%d_%d" % (nm, b, k // 2), "s0", "s1"], ["xV" if strong else "yV"], bk)
 
     def choose(s, b):
         old, new = "a%d_%d" % (s, b), "a%d_%d" % (s + 1, b)
@@ -426,8 +438,7 @@ def rank_program(g, core, T, topo):
         k0, k1 = wkey(j0), wkey(j1)
         c0, c1 = 512 * j0, 512 * j1
         zz, dd = T.wp[:, c0:c0 + CB], T.wp[:, c0 + CB:c0 + 2 * CB]
-        ee, sl, both = T.wp[:, c1:c1 + CB], T.wp[:, c1 + CB:c1 + LW], T.wp[:, c1:c1 + LW]
-        head(s, dd, k0, j0, b, True)
+        ee, sl, both = T.wp[:, c1 - CB:c1], T.wp[:, c1:c1 + 4], T.wp[:, c1 - CB:c1 + 4]
         mm(zz, T.nhu[:], T.neg[:], True, False, ["mats", "neg"], k0, j0)
         mm(zz, T.nhu[:], T.sx[:], False, False, ["mats", "sx"], k0, j0)
         mm(zz, T.boc[:], T.uw[:], False, True, ["uw", "boc"], k0, j0)
@@ -436,7 +447,7 @@ def rank_program(g, core, T, topo):
         for r in range(16):
             mm(sl, sel(r, T.k1s, T.k0s) if last else sel(r, T.w1s, T.w0s), T.hit[:, r:CB:16], False, r == 15,
                ["hit", "wsel"], k1, j1)
-        tt(zz, T.hit[:], dd, A.mult, ["hit"], k0, [j0])
+        tt(zz, T.hit[:], cs(T.py, b, 256), A.mult, ["hit", "yT"], k0, [j0, Y])
         tt(an, zz, ao, A.add, k0 + [old], [new], [j0])
         if last:
             ts(slb, sl, col(PM), A.add, k1 + ["cPM"], ["idx%d" % b], [j1])
@@ -444,14 +455,14 @@ def rank_program(g, core, T, topo):
             cp(T.wk[:, 0:17 * C].indirect(slb), T.pqt[:], ["idx%d" % b, "pqt"], wk, n=60 + CB * SC / CY)
             return
         for wrap in (False, True):
-            mm(ee, T.boh[:], cs(T.ex, b, (s + 1) * C), True, False, ["ex", "boh"], k1, j1)
-            mm(ee, T.nih[:], an, False, not wrap, [new, "nih"], k1, j1)
+            mm(ee, T.boh[:], cs(T.ex, b, (s + 1) * C), True, False, ["ex", "boh"], k0, j0)
+            mm(ee, T.nih[:], an, False, not wrap, [new, "nih"], k0, j0)
             if wrap:
-                mm(ee, T.n2k[:], T.neg[:], False, False, ["mats", "neg"], k1, j1)
-                mm(ee, T.n2k[:], T.sm[:], False, True, ["sm", "mats"], k1, j1)
+                mm(ee, T.n2k[:], T.neg[:], False, False, ["mats", "neg"], k0, j0)
+                mm(ee, T.n2k[:], T.sm[:], False, True, ["sm", "mats"], k0, j0)
             else:
-                act(T.sm[:], ee, F.Sign, k1, ["sm"], [j1], bias=0.5)
-        cp(T.idx[:, LW * b:LW * (b + 1)], both, k1, ["idx%d" % b], [j1], n=68)
+                act(T.sm[:], ee, F.Sign, k0, ["sm"], [j0], bias=0.5)
+        cp(T.idx[:, LW * b:LW * (b + 1)], both, k0 + k1, ["idx%d" % b], [j0, j1], n=68)
         cp(T.ws[:, 2 * BW * b:2 * BW * (b + 1)].indirect(slb), T.pqt[:], ["idx%d" % b, "pqt"], per("ws", b), n=60 + CB * SC / CY)
 
     def akeys(i, b=None):
@@ -487,7 +498,7 @@ def rank_program(g, core, T, topo):
     def put(s):
         src = T.land[:, s * C:(s + 1) * C]
         if s == S - 1:
-            op("s", landed(s, SY, lambda: SY.dma_start(T.yr[:], src)), 2500, ["arr%d" % s], (), kind="d", hold=60)
+            op("s", landed(s, SY, lambda: SY.dma_start(T.yr[:], src)), 12000, ["arr%d" % s], (), kind="d", hold=60)
         else:
             op("v", landed(s, V, lambda: V.tensor_copy(T.rr[:, 0:WN].indirect(T.ntu[:, 12 * s:12 * s + 12]), src)),
                50 + C * SC, ["ntu", "arr%d" % s], ["rr"])
@@ -502,9 +513,6 @@ def rank_program(g, core, T, topo):
             send(s, b)
             update(s, b)
         reach(s)
-        if s == S - 1:
-            head(S, yT, ["yT"], Y)
-            tt(T.qm[:, 0:C], yT, T.dm[:], A.mult, ["yT", "dmr"], ["qm0"], [Y], n=192)
         for b in range(NB):
             choose(s, b)
             if b == 0:
@@ -516,7 +524,9 @@ def rank_program(g, core, T, topo):
         if s == 0:
             last_constants()
 
-    dma("s", T.yw[:], T.wk[:, 0:3072], 6000, ["wk%d_%d" % (i, h) for i in range(NB) for h in range(2)], ())
+    dma("s", T.yw[:], T.wk[:, 0:3072], 7500, ["wk%d_%d" % (i, h) for i in range(NB) for h in range(2)], ())
+    head(S, T.px[:, 0:C], ["e0", "e1", "e2"], X)
+    tt(T.qm[:, 0:C], T.px[:, 0:C], T.dm[:], A.mult, ["e0", "e1", "e2", "dmr"], ["qm0"], [X], n=192)
     head(S + 1, yT, ["yT"], Y)
     cp(T.tin[:], T.af[:, 0:C].indirect(T.l3[:, 0:24]), akeys(S) + ["l3"], ["tin"], n=60 + 384 * GA / CY)
     op("v", lambda: V.transpose(T.tout[:], T.tin[:]), vns(384), ["tin"], ["tout"])

from concourse.mybir import AluOpType as A, ActivationFunctionType as F

TP, C, WN, S, NB, CB = 16, 192, 4096, 5, 3, 64
BW = TP * CB
BIG = float(2 ** 40)
HUGE = float(2 ** 96)
OFF = 2048.0
NS = (10, 12, 12)
Y0 = (0, 10 * CB, 22 * CB, 34 * CB)
K1 = 12
LW = CB + 4
MODE = ["PVD", "DDD", "DDD", "DDD", "DDD"]
GCH = 2
CY, PC, WAKE, OWN, AF, GA, SC, DADD, DREM = 0.83, 0.6, 310, 270, 40, 1.4, 3.0, 4200, 4000
ROUNDS = 450
SCH, YCH = 256, 2
ORDER = []
f32, bf, f16, i32, u16 = "float32", "bfloat16", "float16", "int32", "uint16"


def sb(n, t):
    return ("sbuf", [128, n], t)


SCRATCH = {
    "wp": ("psum", [128, 3072], f32), "px": ("psum", [128, 512], f32), "py": ("psum", [128, 512], f32),
    "wb": sb(3072, bf), "rb": sb(WN, bf), "db": sb(960, bf), "dli": sb(192, i32), "nq": sb(88, i32),
    "rr": sb(WN, f32), "ws": sb(6144, f32), "wk": sb(17 * C, f32), "xs": sb(3072, f32), "tr": sb(3072, f32),
    "pe": sb(Y0[3], f32), "po": sb(Y0[3], f32), "so": sb(Y0[3], f32),
    "mx": sb(3072, f32), "mn": sb(3072, f32), "m01": sb(512, bf), "mbg": sb(512, bf),
    "eqs": sb(3072, bf), "eqw": sb(3072, bf),
    "es": sb(C, f32), "eo": sb(S * C, f32), "land": sb(S * C, f32),
    "ip": sb(4, i32), "it": sb(8, i32), "col": sb(16, f32), "fj": sb(144, f32), "gb": sb(128, f32), "fn": sb(24, f32),
    "m16": sb(16, f32), "dm": sb(C, f32), "s0": sb(144, bf), "s1": sb(144, bf), "w0s": sb(144, f16), "w1s": sb(144, f16),
    "jj": sb(256, f32), "i64": sb(128, f32), "bof": sb(128, f32), "nbo": sb(128, f32),
    "bob": sb(128, bf), "boc": sb(128, bf), "idb": sb(128, bf), "nib": sb(128, bf), "nhu": sb(128, bf), "n2k": sb(128, bf),
    "boh": sb(128, f16), "nbh": sb(128, f16), "nih": sb(128, f16), "cn": sb(4, f16), "neg": sb(CB, bf), "pqt": sb(CB, f32), "idp": sb(128, bf),
    "l1": sb(24, u16), "l2": sb(12, u16), "l3": sb(24, u16), "l4": sb(12, u16), "cj": sb(12, f32), "kj": sb(12, i32),
    "tj": sb(12, f32), "ntu": sb(60, u16), "ex": sb(1344, f16), "tin": sb(384, f32), "tout": sb(384, f32),
    "aa": sb(S * C, f16), "af": sb(C, f32), "ab1": sb(C, f32), "ab2": sb(C, f32), "sgn": sb(C, bf),
    "us2": sb(CB, bf), "uw": sb(CB, bf), "sx": sb(CB, bf), "sm": sb(CB, bf), "hit": sb(CB, f16),
    "vi": sb(C, i32), "vm": sb(C, i32), "idx": sb(NB * LW, u16),
    "k0s": sb(144, f16), "k1s": sb(144, f16), "ck": sb(12, f16),
    "ydo": sb(C, f32), "qm": sb(2 * C, f32), "qs": sb(2 * C, f32), "yqo": sb(24, f32),
}
SEMAPHORES = (["cv", "ca", "cp", "cg", "snt"] + ["arr%d" % s for s in range(S)] + ["dm%d" % i for i in range(60)])


def issue_order(calls):
    n = len(calls)
    after = [[] for _ in calls]
    for i, c in enumerate(calls):
        for d in c["deps"]:
            after[d].append(i)

    def lag(i, j):
        a, b = calls[i]["e"], calls[j]["e"]
        return calls[i]["ns"] + (WAKE if a != b else 0 if a == "p" else OWN)

    need = [[(d, lag(d, i)) for d in calls[i]["deps"]] for i in range(n)]
    feed = [[(j, lag(i, j)) for j in after[i]] for i in range(n)]

    def below(spans, x, sign):
        if sign > 0:
            k = len(spans)
            while k and spans[k - 1][0] >= x:
                k -= 1
        else:
            k, m = 0, len(spans)
            while k < m and spans[k][0] < x:
                k += 1
        return k

    def clash(spans, a, b, sign):
        k = below(spans, b - 1e-6, sign)
        if not k or spans[k - 1][1] <= a + 1e-6:
            return 0
        if sign > 0:
            return spans[k - 1][1] - a
        while k > 1 and spans[k - 2][1] > a + 1e-6:
            k -= 1
        return spans[k - 1][0] - b

    def place(order, sign):
        t, spans = [0.0] * n, {}
        for i in order:
            c = calls[i]
            e, ns, hold = c["e"], c["ns"], c["hold"]
            if sign > 0:
                x = max([t[d] + w for d, w in need[i]] + [0.0])
            else:
                x = min([t[j] - w for j, w in feed[i]] + [-ns])
            moved = c["kind"] != "l"
            if not moved and sign > 0:
                x = i * hold
            own = spans.setdefault(e, [])
            banks = [spans[k, f] for k in c["B"] for f in "vap" if f != e and (k, f) in spans]
            while moved:
                moved = clash(own, x, x + hold, sign)
                for other in banks:
                    moved = moved or clash(other, x - WAKE, x + ns + WAKE, sign)
                x += moved
            t[i] = x
            for row, end in [(own, x + hold)] + [(spans.setdefault((k, e), []), x + ns) for k in c["B"]]:
                row.insert(below(row, x, sign), (x, end))
        return t

    def settle(rank):
        t = place(sorted(range(n), key=lambda i: (rank[i], i)), 1)
        t = place(sorted(range(n), key=lambda i: (-t[i] - calls[i]["ns"], -i)), -1)
        t = place(sorted(range(n), key=lambda i: (t[i], i)), 1)
        return max(t[i] + calls[i]["ns"] for i in range(n)), t
    best, seed = settle(list(range(n))), 1
    for r in range(ROUNDS):
        rank, t0 = [], (r * 0.618 % 1) * best[0]
        t1, size = t0 + WAKE * (10, 20, 40)[r % 3], WAKE * (0.5, 1.5, 3)[r // 3 % 3]
        for i in range(n):
            x = best[1][i]
            if t0 < x < t1:
                seed = (seed * 1103515245 + 12345) % 2 ** 31
                x += (seed / 2 ** 30 - 1) * size
            rank.append(max([x] + [rank[d] + 1e-3 for d, _ in need[i]]))
        best = min(settle(rank), best, key=lambda b: b[0])
    return sorted(range(n), key=lambda i: (best[1][i], i))


def rank_program(g, core, T, topo):
    rank = T.rank_of(core)
    if rank is None:
        return
    N = len(T.cores)
    V, ACT, PE, SY = g.vector, g.scalar, g.tensor, g.sync
    calls, wrote, read, before = [], {}, {}, {}

    def op(e, call, ns, R=(), W=(), B=(), kind="c", part=None, hold=None):
        i, deps = len(calls), set()
        for k in R:
            deps.update(wrote.get(k, (None, []))[1])
        for k in W:
            if part is None or wrote.get(k, (None,))[0] != part:
                before[k] = wrote.get(k, (None, []))[1] + read.get(k, [])
                wrote[k], read[k] = (part, []), []
            deps.update(before[k])
            wrote[k][1].append(i)
        for k in R:
            if k not in W:
                read.setdefault(k, []).append(i)
        calls.append(dict(e=e, call=call, ns=ns, hold=ns if hold is None else hold, deps=sorted(deps), B=B, kind=kind))

    def vns(n):
        return max(64, n) * CY

    def tt(o, a, b, f, R, W, B=(), n=64, part=None):
        op("v", lambda: V.tensor_tensor(o, a, b, f), vns(n), R, W, B, part=part)

    def ts(o, a, s1, f1, R, W, B=(), s2=None, f2=None, n=64, part=None):
        if f2 is None:
            op("v", lambda: V.tensor_scalar(o, a, s1, None, f1), vns(n), R, W, B, part=part)
        else:
            op("v", lambda: V.tensor_scalar(o, a, s1, s2, f1, f2), vns(n), R, W, B, part=part)

    def cp(o, a, R, W, B=(), n=64):
        op("v", lambda: V.tensor_copy(o, a), vns(n), R, W, B)

    def ms(o, c, W, n=64, part=None):
        op("v", lambda: V.memset(o, c), vns(n), (), W, part=part)

    def scan(o, a, b, f0, f1, R, W, B, n, part=None):
        op("v", lambda: V.tensor_tensor_scan(o, a, b, 0.0, f0, f1), vns(n), R, W, B, part=part)

    def act(o, a, f, R, W, B=(), bias=0.0, scale=1.0, n=64, part=None):
        op("a", lambda: ACT.activation(o, a, f, bias=bias, scale=scale), AF + n * CY, R, W, B, part=part)

    def mm(o, l, r, st, sp, R, W, bk, n=64):
        op("p", lambda: PE.matmul(o, l, r, st, sp), n * PC, R, list(W) + ["bank%d" % bk], [bk])

    def dma(e, o, a, ns, R, W, **kw):
        q = {"a": ACT, "s": SY, "g": g}[e]
        op(e, lambda: q.dma_start(o, a, **kw), ns, R, W, kind="d" if R else "l", hold=800 if e == "g" else 30)

    def col(i):
        return T.col[:, i:i + 1]

    def wbank(b):
        return (2 * b, 2 * b + 1)

    def wkey(j, h=None):
        return ["wp%d_%d" % (j, i) for i in ((0, 1) if h is None else (h,))]

    def wkeys(b, h=None):
        return wkey(2 * b, h) + wkey(2 * b + 1, h)

    def per(name, b):
        return ["%s%d" % (name, j) for j in wbank(b)]

    def blk(t, b, k=None):
        return t[:, b * BW:(b + 1) * BW] if k is None else t[:, b * BW + k:(b + 1) * BW:TP]

    def half(t, j):
        return t[:, 512 * j:512 * (j + 1)]

    def pair(t, j, k):
        return t[:, 512 * j + k:512 * (j + 1):8]

    def store(j):
        return half(T.ws, j + 2 * (j // 2))

    def cs(t, b, off=0):
        return t[:, off + b * CB:off + (b + 1) * CB]

    def sel(k, even, odd):
        return even[:, 16 - k:144 - k] if k % 2 == 0 else odd[:, 15 - k:143 - k]

    X, Y = 6, 7
    xD, xV, xZ = T.px[:, 192:384], T.px[:, 384:448], T.px[:, 448:512]
    yE, yS, yL, yV, yR, yT = (T.py[:, 0:64], T.py[:, 64:68], T.py[:, 0:68], T.py[:, 128:192], T.py[:, 192:256],
                              T.py[:, 256:448])
    idf = T.jj[:, 0:128]

    dma("a", T.nq[:, 0:60], T.nt[:], 2200, (), ["nt"])
    dma("s", T.dli[:], T.dl[:], 2400, (), ["dli"])
    dma("a", T.nq[:, 60:84], T.qu[:], 2400, (), ["qu"])
    dma("s", T.rb[:], T.r0[:], 6500, (), ["rb"])
    dma("s", T.wb[:, 0:K1 * C], T.w0[:, 0:K1 * C], 8700, (), ["wb0"])
    dma("s", T.wb[:, K1 * C:3072], T.w0[:, K1 * C:3072], 9400, (), ["wb1"])
    dma("s", T.db[:, 0:C], T.d0[:, 0:C], 9700, (), ["db0"])
    dma("s", T.db[:, C:960], T.d0[:, C:960], 10500, (), ["db1"])

    def io(o, pat, cm, W, n, small=True):
        if small:
            op("g", lambda: g.iota(o, pat, 0, cm, allow_small_or_imprecise_dtypes=True), 130 + 2 * n * CY, (), W)
        else:
            op("g", lambda: g.iota(o, pat, 0, cm), 130 + 2 * n * CY, (), W)
    io(T.ip[:, 0:1], [[0, 1]], 1, ["ip"], 1, False)
    io(T.fn[:], [[1, 12], [0, 2]], 0, ["fn"], 24)
    io(T.fj[:], [[1, 144]], 0, ["fj"], 144)
    io(T.gb[:], [[16, 8], [0, 16]], 0, ["gb"], 128)
    io(T.jj[:], [[0, 2], [1, 128]], -1, ["jj"], 256)
    io(T.dm[:], [[0, 12], [1, 16]], 0, ["dmr"], 192)

    PM, PG, G15, G16, P31, M12, M16, H16, BS, BWK, WSL, WK = range(12)
    ts(T.it[:, 0:1], T.ip[:, 0:1], 15, A.bitwise_and, ["ip"], ["it0"])
    ts(T.it[:, 1:2], T.ip[:, 0:1], 31, A.bitwise_and, ["ip"], ["it1"])
    ts(T.it[:, 2:3], T.ip[:, 0:1], 112, A.bitwise_and, ["ip"], ["it2"])
    cp(col(PM), T.it[:, 0:1], ["it0"], ["cPM"])
    cp(col(PG), T.it[:, 2:3], ["it2"], ["cPG"])
    cp(col(P31), T.it[:, 1:2], ["it1"], ["cP31"])
    ts(col(M12), T.it[:, 0:1], 12.0, A.mult, ["it0"], ["cM12"])
    ts(T.m16[:], T.fj[:, 0:16], col(PM), A.is_equal, ["fj", "cPM"], ["m16"])
    ts(T.boh[:], T.gb[:], col(PG), A.is_equal, ["gb", "cPG"], ["boh"], n=128)
    ts(T.l1[:], T.fn[:], col(M12), A.add, ["fn", "cM12"], ["l1"])
    ts(T.l2[:], T.fj[:, 0:12], 32.0, A.mult, ["fj", "cP31"], ["l2"], s2=col(P31), f2=A.add)
    ts(T.nib[:], T.jj[:, 0:128], 0.0, A.is_equal, ["jj"], ["nib"], s2=-1.0, f2=A.mult, n=128)
    A0 = ["a0_0", "a0_1", "a0_2"]
    cp(T.tin[:], T.dli[:, 0:192].indirect(T.l1[:, 0:24]), ["dli", "l1"], ["tin"], n=60 + 384 * GA / CY)
    op("v", lambda: V.transpose(T.tout[:], T.tin[:]), vns(384), ["tin"], ["tout"])
    ts(T.aa[:, 0:192], T.tout[:, 0:384].indirect(T.l2[:, 0:12]), -OFF, A.add, ["tout", "l2"], A0, n=60 + 192 * GA / CY)
    for r in range(16):
        ts(T.ex[:, r:1344:16], T.nq[:, 0:84], -OFF, A.add, ["nt", "qu", "m16"], ["ex"], s2=T.m16[:, r:r + 1], f2=A.mult,
           n=84, part="ex")
    mm(yT, T.boh[:], T.ex[:, 0:192], True, True, ["ex", "boh"], ["yT"], Y, 192)
    for b in range(NB):
        tt(cs(T.vi, b), cs(T.py, b, 256), cs(T.aa, b), A.subtract, ["yT"] + A0, ["vi%d" % b], [Y])
        ts(cs(T.vm, b), cs(T.vi, b), WN - 1, A.bitwise_and, ["vi%d" % b], ["vm%d" % b])
        cp(T.idx[:, LW * b:LW * b + CB], cs(T.vm, b), ["vm%d" % b], ["idx%d" % b])
    for c0, c1, ns in ((0, Y0[1], 10), (Y0[1], Y0[3], 12)):
        for t_, j, v in ((T.pe, 0, BIG), (T.po, 0, -BIG), (T.po, ns - 1, 0.0)) + (
                ((T.pe, 5, 0.0), (T.pe, 6, 0.0), (T.po, 5, 0.0), (T.po, 6, 0.0)) if ns == 12 else ()):
            ms(t_[:, c0 + j:c1:ns], v, ["pc"], (c1 - c0) // ns, "pc")
    ts(T.jj[:], T.jj[:], 0.0, A.is_equal, [], ["jj"], n=256)
    ts(T.idp[:], T.nib[:], -1.0, A.mult, ["nib"], ["idp"])

    def constants():
        act(T.bof[:], T.gb[:], F.Copy, ["gb"], ["bof"], n=128)
        ts(T.bof[:], T.bof[:], col(PG), A.is_equal, ["cPG"], ["bof"], n=128)
        ts(col(G15), col(PG), 15.0, A.add, ["cPG"], ["cG15"])
        ts(col(G16), col(PG), 16.0, A.add, ["cPG"], ["cG16"])
        ts(col(WSL), col(PM), -float(BW), A.add, ["cPM"], ["cWS"])
        ts(col(M16), col(PM), 16.0, A.mult, ["cPM"], ["cM16"], s2=float(BW), f2=A.add)
        ts(col(BS), col(PM), -0.71, A.mult, ["cPM"], ["cBS"], s2=-94.0, f2=A.add)
        ts(col(BWK), col(PM), -0.55, A.mult, ["cPM"], ["cBW"], s2=-78.8, f2=A.add)
        ts(col(WK), col(PM), -16.0, A.add, ["cPM"], ["cWK"], s2=float(C), f2=A.mult)
        ts(T.s0[:], T.fj[:], col(G15), A.is_equal, ["fj", "cG15"], ["s0"], n=144)
        ts(T.s1[:], T.fj[:], col(G16), A.is_equal, ["fj", "cG16"], ["s1"], n=144)
        for o, a, c_, k in ((T.w0s, T.s0, WSL, "cWS"), (T.w1s, T.s1, WSL, "cWS"), (T.k0s, T.s0, WK, "cWK"), (T.k1s, T.s1, WK, "cWK")):
            ts(o[:], a[:], col(c_), A.mult, ["s0", "s1", k], ["wsel"], n=72, part="wsel")
        ts(T.nih[:], T.nib[:], 1.0, A.mult, ["nib"], ["nih"])
        ts(T.nbh[:], T.boh[:], -1.0, A.mult, ["boh"], ["nbh"])
        ts(T.cn[:], T.fj[:, 0:4], -256.0, A.mult, ["fj", "cM16"], ["cn"], s2=col(M16), f2=A.subtract)
        ts(T.ck[:], T.fj[:, 0:12], -16.0, A.mult, ["fj"], ["ck"], s2=-16.0 * C, f2=A.add)
        cp(T.ntu[:], T.nq[:, 0:60], ["nt"], ["ntu"])
        ms(T.pqt[:], 0.25, ["pqt"])
        ms(T.neg[:], -1.0, ["neg"])
        for o, a, k, f in ((T.i64, idf, "jj", -1.0 / 64), (T.nbo, T.bof[:], "bof", -1.0), (T.bob, T.bof[:], "bof", 1.0),
                           (T.nhu, T.nib[:], "nib", HUGE), (T.n2k, T.nib[:], "nib", 2048.0), (T.idb, T.nib[:], "nib", 2.5)):
            act(o[:], a, F.Copy, [k], ["mats"], scale=f, n=128, part="mats")
        tt(T.boc[:], T.idb[:], T.bob[:], A.add, ["mats"], ["boc"], n=256)
        for h in range(4):
            act(T.m01[:, 128 * h:128 * (h + 1)], T.fj[:, 0:128], F.Identity, ["fj"], ["m01"], scale=0.0, bias=1.0, n=128, part="m")
            act(T.mbg[:, 128 * h:128 * (h + 1)], T.fj[:, 0:128], F.Copy, ["fj"], ["mbg"], scale=0.0, n=128, part="m")
        act(T.m01[:, 0:512:16], T.fj[:, 0:32], F.Copy, ["fj"], ["m01"], scale=0.0)
        act(T.mbg[:, 0:512:16], T.fj[:, 0:32], F.Exp, ["fj"], ["mbg"], scale=0.0, bias=8.0, n=1600)

    def last_constants():
        ts(T.cj[:], T.fj[:, 0:12], 16.0, A.mult, ["fj", "cPM"], ["cj"], s2=col(PM), f2=A.add)
        ts(T.l3[:], T.fn[:], 16.0, A.mult, ["fn", "cPM"], ["l3"], s2=col(PM), f2=A.add)
        tt(col(H16), col(P31), col(PM), A.subtract, ["cP31", "cPM"], ["cH"])
        ts(T.dm[:], T.dm[:], col(PM), A.is_equal, ["cPM"], ["dmr"], n=192)
        ts(T.tj[:], T.cj[:], -5.5, A.add, ["cj"], ["tj"], s2=1.0 / 12, f2=A.mult)
        cp(T.kj[:], T.tj[:], ["tj"], ["kj"])
        ts(T.tj[:], T.kj[:], -383.0 / 32, A.mult, ["kj"], ["tj"])
        tt(T.tj[:], T.tj[:], T.cj[:], A.add, ["cj"], ["tj"])
        ts(T.l4[:], T.tj[:], 32.0, A.mult, ["tj", "cH"], ["l4"], s2=col(H16), f2=A.add)

    def taps_in(b, l, h):
        for j in wbank(b):
            for k in range(K1 * h, TP if h else K1):
                mm(T.wp[:, 512 * j + k:512 * (j + 1):TP], l, T.wb[:, k * C + 32 * j:k * C + 32 * (j + 1)],
                   k in (0, K1), k in (K1 - 1, TP - 1), ["wb%d" % h, "nib", "idp"], wkey(j, h), j)

    def fetch(s, b):
        win, key = (T.rb, "rb") if s == 0 else (T.rr, "rr")
        for j in wbank(b):
            o = LW * b + 32 * (j % 2)
            act(half(T.xs, j), win[:, 0:WN].indirect(T.idx[:, o:o + 32]), F.Copy, [key, "idx%d" % b], ["x%d" % j],
                n=512 * GA / CY, scale=1.0 if s or b else -1.0)
        if s == 0:
            for h in range(2 if b else 1):
                taps_in(b, T.nib[:] if b else T.idp[:], h)
        else:
            for j in wbank(b):
                act(half(T.wp, j), store(j), F.Copy, ["ws%d" % j], wkey(j), [j], scale=-1.0, n=512)
        if b < 2:
            c0, c1 = (0, Y0[1]) if b == 0 else (Y0[1], Y0[3])
            act(T.pe[:, c0 + NS[b] - 1:c1:NS[b]], T.db[:, s * C + b * CB:s * C + (1 + 2 * b) * CB], F.Copy,
                ["db%d" % min(s, 1)], ["pd%d" % b], n=CB * (1 + b))

    def residual(s, b):
        ns, c0, c1 = NS[b], Y0[b], Y0[b + 1]
        n = ns * CB // 2
        if ns == 12:
            for j in wbank(b):
                o = c0 + n * (j % 2)
                for k in range(8):
                    tt((T.pe, T.po)[k % 2][:, o + 1 + k // 2:o + n:6], pair(T.wp, j, k), pair(T.xs, j, k), A.mult,
                       wkey(j) + ["x%d" % j], ["p%d" % j], [j], part=s)
        for k in range(TP if ns == 10 else 0):
            o = (T.pe, T.po)[k % 2][:, c0 + 1 + k // 2:c1:ns]
            if s or k < K1:
                tt(o, blk(T.wp, b, k), blk(T.xs, b, k), A.mult, wkeys(b, k // K1) + per("x", b), per("p", b), wbank(b), part=s)
            else:
                tt(o, cs(T.wb, b, k * C), blk(T.xs, b, k), A.mult, ["wb1"] + per("x", b), per("p", b), n=128, part=s)
        for j in wbank(b):
            o = c0 + n * (j % 2)
            scan(T.so[:, o:o + n], T.pe[:, o:o + n], T.po[:, o:o + n], A.add, A.add, ["p%d" % j, "pd%d" % min(b, 1), "pc"],
                 ["so%d" % j], (), n)
            for i in range(2):
                ts(T.px[:, CB * j + i:CB * (j + 1):2], T.so[:, o + ns - 1:o + n:ns], -2.0, A.max, ["so%d" % j], ["e%d" % j], [X],
                   s2=2.0, f2=A.min, part=s)
        ts(cs(T.es, b), T.so[:, c0 + ns - 1:c1:ns], -2.0, A.max, per("so", b), ["es%d" % b], s2=2.0, f2=A.min)

    def send(s, b):
        sh = 16 * (1 + s)
        mm(yR, T.jj[:, 128 - sh:256 - sh], cs(T.es, b), True, True, ["es%d" % b, "jj"], ["yR"], Y, 256)
        act(cs(T.eo, b, s * C), yR, F.Copy, ["yR"], ["eo%d_%d" % (s, b)], [Y])
        dst = T.cores[(rank + 1 + b) % N]
        eng = topo.engines(core, dst)[-8:]
        rid, pid, _ = topo.addr(dst)
        op("g", lambda: g.remote_dma(cs(T.land, b, s * C), cs(T.eo, b, s * C), T.sem["arr%d" % s], T.sem.snt, pid, rid,
                                     sum(1 << e for e in eng)),
           DREM, ["eo%d_%d" % (s, b)], ["arr%d" % s], kind="r", part="arr", hold=600)

    def update(s, b):
        m, last = MODE[s][b], s == S - 1
        if m == "D" and s == 0:
            for j in wbank(b):
                act(store(j), half(T.wp, j), F.Copy, wkey(j), ["ws%d" % j], [j], scale=-1.0, n=512)
        if m == "P":
            for j in wbank(b):
                for k in range(TP):
                    mm(T.wp[:, 512 * j + k:512 * (j + 1):TP], T.idp[:], T.wb[:, k * C + 32 * j:k * C + 32 * (j + 1)],
                       k == 0, False, ["wb0", "wb1", "idp"], wkey(j), j)
        for j in wbank(b):
            for k in range(8):
                tt(pair(T.tr, j, k), pair(T.xs, j, k), cs(T.px, j), A.mult, ["x%d" % j, "e%d" % j], ["t%d" % j], [X], part=s)
        if m == "P":
            for j in wbank(b):
                mm(half(T.wp, j), T.i64[:], half(T.tr, j), False, True, ["t%d" % j, "mats"], wkey(j), j, 2048)
                act(store(j), half(T.wp, j), F.Copy, wkey(j), ["ws%d" % j], [j], n=512)
                act(half(T.wp, j), half(T.wp, j), F.Abs, [], wkey(j), [j], n=512)
            return
        for j in wbank(b):
            act(half(T.tr, j), half(T.tr, j), F.Copy, [], ["t%d" % j], scale=1.0 / 64, n=512)
        for j in wbank(b):
            if m == "D":
                dma("g", store(j), half(T.tr, j), DADD, ["t%d" % j], ["ws%d" % j], accum_op=A.add)
            else:
                for h in range(2):
                    o = slice(256 * h, 256 * (h + 1))
                    tt(store(j)[:, o], half(T.tr, j)[:, o], half(T.wp, j)[:, o], A.subtract, ["t%d" % j] + wkey(j),
                       ["ws%d" % j], [j], n=256, part=s)
            act(half(T.wp, j), store(j), F.Abs, ["ws%d" % j], wkey(j), [j], n=512)
        for k in range(TP if last else 0):
            act(cs(T.wk, b, k * C), T.ws[:, 2 * BW * b + k:2 * BW * b + BW:TP], F.Copy, per("ws", b),
                ["wk%d_%d" % (b, k // 8)], part="out")

    def extreme(s, j, strong):
        nm, ext, msk, f = ("mx", T.mx, T.m01, (A.mult, A.max)) if strong else ("mn", T.mn, T.mbg, (A.max, A.min))
        for o in range(512 * j, 512 * (j + 1), SCH):
            scan(ext[:, o:o + SCH], msk[:, 0:SCH], T.wp[:, o:o + SCH], f[0], f[1], wkey(j) + ["m01", "mbg"],
                 ["%s%d" % (nm, j)], [j], SCH, part=s)

    def votes(s, b, strong):
        nm, ext, eq, o, bk = ("mx", T.mx, T.eqs, xV, X) if strong else ("mn", T.mn, T.eqw, yV, Y)
        for k in range(TP):
            tt(eq[:, b * BW + k * CB:b * BW + (k + 1) * CB], blk(T.wp, b, k), blk(ext, b, TP - 1), A.is_equal,
               wkeys(b, k // 8) + per(nm, b), ["eq%s%d_%d" % (nm, b, k // 2)], wbank(b), part=s)
        for k in range(TP):
            mm(o, sel(k, T.s1, T.s0), eq[:, b * BW + k * CB:b * BW + (k + 1) * CB], k == 0, k == TP - 1,
               ["eq%s%d_%d" % (nm, b, k // 2), "s0", "s1"], ["xV" if strong else "yV"], bk)

    def choose(s, b):
        old, new = "a%d_%d" % (s, b), "a%d_%d" % (s + 1, b)
        last = s == S - 1
        ao, an = cs(T.aa, b, s * C), cs(T.af, b) if last else cs(T.aa, b, (s + 1) * C)
        slb = T.idx[:, LW * b + CB:LW * (b + 1)]
        for j, strong in ((2 * b, True), (2 * b + 1, True), (2 * b, False)):
            extreme(s, j, strong)
        votes(s, b, True)
        act(xV, xV, F.Exp, ["cBS"], ["xV"], [X], bias=col(BS), scale=11.36)
        tt(T.us2[:], xV, cs(T.sgn, b), A.mult, ["xV", "sgn"], ["us2"], [X])
        mm(xV, T.bob[:], T.us2[:], True, True, ["us2", "mats"], ["xV"], X)
        act(T.sx[:], xV, F.Sign, ["xV"], ["sx"], [X])
        extreme(s, 2 * b + 1, False)
        votes(s, b, False)
        act(T.uw[:], yV, F.Exp, ["yV", "cBW"], ["uw"], [Y], bias=col(BWK), scale=8.8)
        j0, j1 = wbank(b)
        k0, k1 = wkey(j0), wkey(j1)
        c0, c1 = 512 * j0, 512 * j1
        zz, dd = T.wp[:, c0:c0 + CB], T.wp[:, c0 + CB:c0 + 2 * CB]
        ee, sl, both = T.wp[:, c1 - CB:c1], T.wp[:, c1:c1 + 4], T.wp[:, c1 - CB:c1 + 4]
        mm(zz, T.nhu[:], T.neg[:], True, False, ["mats", "neg"], k0, j0)
        mm(zz, T.nhu[:], T.sx[:], False, False, ["mats", "sx"], k0, j0)
        mm(zz, T.boc[:], T.uw[:], False, True, ["uw", "boc"], k0, j0)
        ts(T.hit[:], zz, 0.0, A.is_lt, k0, ["hit"], [j0])
        mm(sl, T.nih[:], T.ck[:, 4 * b:4 * b + 4] if last else T.cn[:], True, False, ["nih", "ck", "cn"], k1, j1)
        for r in range(16):
            mm(sl, sel(r, T.k1s, T.k0s) if last else sel(r, T.w1s, T.w0s), T.hit[:, r:CB:16], False, r == 15,
               ["hit", "wsel"], k1, j1)
        tt(zz, T.hit[:], cs(T.py, b, 256), A.mult, ["hit", "yT"], k0, [j0, Y])
        tt(an, zz, ao, A.add, k0 + [old], [new], [j0])
        if last:
            ts(slb, sl, col(PM), A.add, k1 + ["cPM"], ["idx%d" % b], [j1])
            wk = ["wk%d_%d" % (i, h) for i in range(NB) for h in range(2)]
            cp(T.wk[:, 0:17 * C].indirect(slb), T.pqt[:], ["idx%d" % b, "pqt"], wk, n=60 + CB * SC / CY)
            return
        for wrap in (False, True):
            mm(ee, T.boh[:], cs(T.ex, b, (s + 1) * C), True, False, ["ex", "boh"], k0, j0)
            mm(ee, T.nih[:], an, False, not wrap, [new, "nih"], k0, j0)
            if wrap:
                mm(ee, T.n2k[:], T.neg[:], False, False, ["mats", "neg"], k0, j0)
                mm(ee, T.n2k[:], T.sm[:], False, True, ["sm", "mats"], k0, j0)
            else:
                act(T.sm[:], ee, F.Sign, k0, ["sm"], [j0], bias=0.5)
        cp(T.idx[:, LW * b:LW * (b + 1)], both, k0 + k1, ["idx%d" % b], [j0, j1], n=68)
        cp(T.ws[:, 2 * BW * b:2 * BW * (b + 1)].indirect(slb), T.pqt[:], ["idx%d" % b, "pqt"], per("ws", b), n=60 + CB * SC / CY)

    def akeys(i, b=None):
        return ["a%d_%d" % (i, j) for j in (range(NB) if b is None else (b,))]

    def head(s, o, keys, bk, b=None, gap=False):
        c0, n = (0, C) if b is None else (b * CB, CB)

        def delays(t):
            return T.aa[:, t * C + c0:t * C + c0 + n] if t < S else T.af[:, c0:c0 + n]
        q0 = (S + s % 2) * C + c0
        terms = [(T.boh[:], T.ex[:, q0:q0 + n], ["ex"], n)]
        for t in range(s % 2, s, 2):
            terms += [(T.boh[:], delays(t), akeys(t, b), n),
                      (T.nbh[:], delays(t + 1), akeys(t + 1, b), n) if t + 1 < S else (T.nbo[:], delays(S), akeys(S, b), 4 * n)]
        if gap:
            terms.append((T.nih[:], delays(s), akeys(s, b), n))
        for i, (l, r, rk, m) in enumerate(terms):
            mm(o, l, r, i == 0, i == len(terms) - 1, rk + ["boh", "nbh", "mats", "nih"], keys, bk, m)

    def reach(s):
        head(s, yT, ["yT"], Y, gap=True)
        act(T.ab1[:], yT, F.Abs, ["yT"], ["ab1"], [Y], n=192)
        act(T.ab2[:], T.ab1[:], F.Abs, ["ab1"], ["ab2"], bias=-2048.0, n=192)
        act(T.sgn[:], T.ab2[:], F.Sign, ["ab2"], ["sgn"], bias=-1023.5, n=192)

    def landed(s, q, call):
        def run():
            q.wait_ge(T.sem["arr%d" % s], 8 * NB)
            return call()
        return run

    def put(s):
        src = T.land[:, s * C:(s + 1) * C]
        if s == S - 1:
            op("s", landed(s, SY, lambda: SY.dma_start(T.yr[:], src)), 12000, ["arr%d" % s], (), kind="d", hold=60)
        else:
            op("v", landed(s, V, lambda: V.tensor_copy(T.rr[:, 0:WN].indirect(T.ntu[:, 12 * s:12 * s + 12]), src)),
               50 + C * SC, ["ntu", "arr%d" % s], ["rr"])

    for b in range(NB):
        fetch(0, b)
    for s in range(S):
        for b in range(NB):
            residual(s, b)
            if s == 0 and b == 0:
                constants()
            send(s, b)
            update(s, b)
        reach(s)
        for b in range(NB):
            choose(s, b)
            if b == 0:
                for j in range(8 if s == 0 else 0):
                    act(half(T.rr, j), half(T.rb, j), F.Copy, ["rb"], ["rr"], n=512, part="wide")
                put(s)
            if s < S - 1:
                fetch(s + 1, b)
        if s == 0:
            last_constants()

    dma("s", T.yw[:], T.wk[:, 0:3072], 7500, ["wk%d_%d" % (i, h) for i in range(NB) for h in range(2)], ())
    head(S, T.px[:, 0:C], ["e0", "e1", "e2"], X)
    tt(T.qm[:, 0:C], T.px[:, 0:C], T.dm[:], A.mult, ["e0", "e1", "e2", "dmr"], ["qm0"], [X], n=192)
    head(S + 1, yT, ["yT"], Y)
    cp(T.tin[:], T.af[:, 0:C].indirect(T.l3[:, 0:24]), akeys(S) + ["l3"], ["tin"], n=60 + 384 * GA / CY)
    op("v", lambda: V.transpose(T.tout[:], T.tin[:]), vns(384), ["tin"], ["tout"])
    ts(T.ydo[:], T.tout[:, 0:384].indirect(T.l4[:, 0:12]), OFF, A.add, ["tout", "l4"], ["ydo"], n=60 + 192 * GA / CY)
    dma("a", T.yd[:], T.ydo[:], 2500, ["ydo"], ())
    tt(T.qm[:, C:2 * C], yT, T.dm[:], A.mult, ["yT", "dmr"], ["qm1"], [Y], n=192)
    scan(T.qs[:], T.m01[:, 0:2 * C], T.qm[:], A.mult, A.add, ["qm0", "qm1", "m01"], ["qs"], (), 384)
    ts(T.yqo[:], T.qs[:, 15:2 * C:16], OFF, A.add, ["qs"], ["yqo"])
    dma("a", T.yq[:], T.yqo[:], 2500, ["yqo"], ())

    Q = {"v": V, "a": ACT, "p": PE, "g": g, "s": SY}
    cnt, seen, tok, bank, ndma = {e: 0 for e in "vapg"}, {e: {} for e in Q}, {}, {}, 0
    if not ORDER:
        ORDER.extend(issue_order(calls))
    for i in ORDER:
        c = calls[i]
        e, need = c["e"], {}
        for d in c["deps"] + [bank[b] for b in c["B"] if b in bank and calls[bank[b]]["e"] != e]:
            if d in tok and not (e == "p" and calls[d]["e"] == "p"):
                need[tok[d][0]] = max(need.get(tok[d][0], 0), tok[d][1])
        for name, n in need.items():
            if seen[e].get(name, 0) < n:
                Q[e].wait_ge(T.sem[name], n)
                seen[e][name] = n
        ins = c["call"]()
        if c["kind"] in "dl":
            tok[i] = ("dm%d" % ndma, 16)
            ndma += 1
            ins.then_inc(T.sem[tok[i][0]], 16)
        elif c["kind"] == "c":
            cnt[e] += 1
            tok[i] = ("c" + e, cnt[e])
            ins.then_inc(T.sem["c" + e], 1)
        for b in c["B"]:
            bank[b] = i
    g.wait_ge(T.sem.snt, 8 * NB * S)
    for e in "vapg":
        g.wait_ge(T.sem["c" + e], cnt[e])
    for i in range(ndma):
        g.wait_ge(T.sem["dm%d" % i], 16)
